import numpy as np
import ml_dtypes


def mxq(x, axis, fmt="e4m3"):
    dtype, down = {"e4m3": (ml_dtypes.float8_e4m3fn, 7), "e5m2": (ml_dtypes.float8_e5m2, 14)}[fmt]
    v = np.moveaxis(np.asarray(x, np.float32).astype(ml_dtypes.bfloat16).astype(np.float64), axis, -1)
    blocks = v.reshape(v.shape[:-1] + (-1, 32))
    amax = np.abs(blocks).max(-1, keepdims=True)
    byte = np.maximum(np.where(amax > 0, np.frexp(amax)[1] - 1 + 127, 0) - down, 1)
    scale = np.exp2(byte - 127.0)
    codes = (blocks / scale).astype(np.float32).astype(dtype).astype(np.float64)
    return np.moveaxis((codes * scale).reshape(v.shape), -1, axis)


WIDE = False


def mx_kscale(k):
    if not WIDE:
        return np.ones(k)
    levels = np.array([10, -10, 5, -5, 0])
    if k % 512:
        return np.exp2(np.random.permutation(np.resize(levels, k // 32))).repeat(32)
    a = np.empty((k // 512, 16))
    for p in range(k // 512):
        a[p, :8] = np.random.permutation(np.resize(levels, 8))
        for g in range(8):
            far = levels[np.abs(levels - a[p, g]) >= 10]
            a[p, g + 8] = far[np.random.randint(len(far))]
    return np.exp2(a.ravel()).repeat(32)


def f64(x):
    return np.asarray(x).astype(np.float64)


def striped(idx):
    return np.tile(idx.reshape(-1, 16).T, (8, 1)).astype(np.uint16)


def unstriped(offs):
    return offs[:16].T.reshape(-1).astype(np.int64)


def pack_weight(w):
    k, n = w.shape
    w = f64(np.asarray(w, np.float32).astype(ml_dtypes.bfloat16)).reshape(k // 32, 32, n)
    amax = np.abs(w).max(1)
    byte = np.clip(np.where(amax > 0, np.frexp(amax)[1] - 1 + 127 - 7, 1), 1, 254)
    scaled = (w * np.exp2(127.0 - byte)[:, None, :]).reshape(k, n).astype(np.float32)
    words = np.ascontiguousarray(scaled.reshape(k // 512, 128, 4, n).transpose(0, 1, 3, 2)).astype(ml_dtypes.float8_e4m3fn).view(np.uint8)
    return words, np.ascontiguousarray(byte.astype(np.uint8).reshape(k // 512, 16, n))


def unpack_weight(words, scales):
    g, p, n, _ = words.shape
    vals = np.ascontiguousarray(words).view(ml_dtypes.float8_e4m3fn).astype(np.float64) * np.repeat(np.exp2(scales.astype(np.float64) - 127.0), 8, axis=1)[..., None]
    return vals.transpose(0, 1, 3, 2).reshape(g * 512, n)


def relu(v):
    return np.maximum(v, 0.0)


K, T, E, C, N = 1536, 1024, 24, 128, 128
TOP = 3


def by_expert(wq, xq):
    return np.concatenate([wq[e].T @ xq[:, e * C:(e + 1) * C] for e in range(E)], axis=1)


def setup_inputs():
    n = np.random.standard_normal
    s = mx_kscale(K)[:, None]
    deal = np.repeat(np.arange(E), C).reshape(TOP, T)[:, np.random.permutation(T)]
    deal = np.take_along_axis(deal, np.argsort(np.random.rand(TOP, T), axis=0), axis=0)
    for _ in range(8):
        s_, t_ = np.random.permutation(T).reshape(2, -1); r = np.random.randint(TOP, size=T // 2); x, y = deal[r, s_].copy(), deal[r, t_].copy()
        ok = ~((deal[:, s_] == y).any(0) | (deal[:, t_] == x).any(0)); deal[r[ok], s_[ok]] = y[ok]; deal[r[ok], t_[ok]] = x[ok]
    order = np.lexsort((np.random.rand(TOP * T), deal.reshape(-1)))
    slot_token = order % T; pos = np.empty(TOP * T, np.int64); pos[order] = np.arange(TOP * T); pos = pos.reshape(TOP, T)
    g = np.random.uniform(0.5, 1.5, (TOP, T)); g = g / g.sum(0)
    packed = [pack_weight(m) for m in n((E, K, N)) / np.sqrt(K) / s[None]]
    w_slot = np.empty(E * C)
    for r in range(TOP): w_slot[pos[r]] = g[r]
    return {
        "xT": (n((K, T)) * s).astype(np.float32),
        "w_words": np.stack([m[0] for m in packed]),
        "w_scales": np.stack([m[1] for m in packed]),
        "b": (0.3 * n((N, E))).astype(np.float32),
        "gate": np.tile(w_slot, (K, 1)).astype(np.float32),
        "offs": striped(slot_token),
        "pos1": striped(pos[0]),
        "pos2": striped(pos[1]),
        "pos3": striped(pos[2]),
    }


def reference(xT, w_words, w_scales, b, gate, offs, pos1, pos2, pos3):
    idx = unstriped(offs)
    w = np.stack([unpack_weight(w_words[e], w_scales[e]) for e in range(E)])
    xq = mxq(f64(gate) * f64(xT)[:, idx], 0, "e4m3")
    y = by_expert(w, xq)
    y = relu(y + np.repeat(f64(b), C, axis=1))
    return y[:, unstriped(pos1)] + y[:, unstriped(pos2)] + y[:, unstriped(pos3)]

@@ -1,0 +1,165 @@
+from contextlib import ExitStack
+
+import concourse.mybir as mybir
+from concourse.masks import make_identity
+
+K, T, E, C, N = 1536, 1024, 24, 128, 128
+S = E * C
+P = 128
+PASSES = K // 512
+WINDOW = T + 32
+CHUNKS = (8, 8, 4, 2, 2)
+FLOPS = 2 * K * S * N
+BYTES = 4 * K * T + E * K * N + E * K * N // 32 + 4 * N * E + 4 * S + 2 * P * (S + 3 * T) // 16 + 4 * N * T
+
+F32 = mybir.dt.float32
+BF16 = mybir.dt.bfloat16
+I32 = mybir.dt.int32
+U32 = mybir.dt.uint32
+U16 = mybir.dt.uint16
+U8 = mybir.dt.uint8
+FP8X4 = mybir.dt.float8_e4m3fn_x4
+ACT = mybir.ActivationFunctionType
+ADD = mybir.AluOpType.add
+
+
+def tile_moe_pre_lin_relu_kernel(tc, xT, w_words, w_scales, b, gate, offs, pos1, pos2, pos3, out):
+    nc = tc.nc
+    with ExitStack() as ctx:
+        keep = ctx.enter_context(tc.tile_pool(name="keep", bufs=1))
+        ring = ctx.enter_context(tc.tile_pool(name="ring", bufs=1))
+        psum = ctx.enter_context(tc.psum_pool(name="psum", bufs=1))
+
+        offs_t = keep.tile([P, S // 16], U16, name="offs_t")
+        nc.sync.dma_start(offs_t[:], offs)
+
+        gate_rows = keep.tile([P, C], F32, name="gate_rows")
+        nc.gpsimd.memset(gate_rows[:], 0.0)
+        ident = keep.tile([P, P], F32, name="ident")
+        make_identity(nc, ident[:])
+
+        planes = {}
+        for a in range(PASSES):
+            for r in range(4):
+                plane = keep.tile([P, WINDOW], F32, name="plane%d_%d" % (a, r))
+                nc.gpsimd.memset(plane[:, T:WINDOW], 0.0)
+                nc.sync.dma_start(plane[:, 0:T], xT[512 * a + r : 512 * (a + 1) : 4, :])
+                planes[a, r] = plane
+            if a == 0:
+                nc.sync.dma_start(gate_rows[0:E, :], gate[0:1, :].rearrange("o (e c) -> (o e) c", c=C))
+
+        w_scale = keep.tile([P, E * PASSES * N], U8, name="w_scale", align_bytes=64)
+        nc.gpsimd.memset(w_scale[:].bitcast(I32), 0)
+
+        gate_ps = psum.tile([P, 512], F32, name="turned", bufs=3)
+        nc.tensor.transpose(gate_ps[:, 0:P], gate_rows[:], ident[:])
+        gate_col = keep.tile([P, E], F32, name="gate_col")
+        nc.scalar.copy(gate_col[:], gate_ps[:, 0:E])
+
+        w_src = w_words.rearrange("e a p n r -> p (e a) (n r)").bitcast(I32)
+        sc_src = w_scales.rearrange("e a q n -> q (e a) n").bitcast(I32)
+        sc_dst = w_scale[:].bitcast(I32).rearrange("p (g n) -> p g n", n=N // 4)
+        w_tiles = []
+        first = 0
+        for ci, ne in enumerate(CHUNKS):
+            wt = keep.tile([P, ne * PASSES * N], U32, name="w%d" % ci, align_bytes=64)
+            nc.sync.dma_start(
+                wt[:].bitcast(I32).rearrange("p (g n) -> p g n", n=N),
+                w_src[:, first * PASSES : (first + ne) * PASSES, :],
+            )
+            w_tiles.append(wt)
+            if ci == 0:
+                for q in range(4):
+                    nc.sync.dma_start(sc_dst[32 * q : 32 * q + 4, :, :], sc_src[4 * q : 4 * q + 4, :, :])
+                bias = keep.tile([P, E], F32, name="bias")
+                nc.sync.dma_start(bias[:], b)
+            first = first + ne
+        pos_t = []
+        for i, pos in enumerate((pos1, pos2, pos3)):
+            pt = keep.tile([P, T // 16], U16, name="pos%d" % i)
+            nc.sync.dma_start(pt[:], pos)
+            pos_t.append(pt)
+
+        y = keep.tile([P, S], F32, name="y")
+
+        pieces = []
+        first = 0
+        for ci, ne in enumerate(CHUNKS):
+            for a in range(PASSES):
+                pieces.append((ci, first, ne, a))
+            first = first + ne
+
+        grouped = {}
+        codes = {}
+        scales = {}
+
+        def gather_and_gate(ci, e0, ne, a):
+            n = ne * C
+            got = []
+            for r in range(4):
+                g = ring.tile([P, n], F32, name="gathered", bufs=8)
+                nc.vector.tensor_copy(g[:], planes[a, r][:].indirect(offs_t[:, e0 * 8 : (e0 + ne) * 8]))
+                got.append(g)
+            q_in = ring.tile([P, 4 * n], BF16, name="grouped", bufs=3, align_bytes=64)
+            for j0 in range(0, ne, 2):
+                back = psum.tile([P, 512], F32, name="back", bufs=2)
+                for jj in range(2):
+                    j = j0 + jj
+                    turned = psum.tile([P, 512], F32, name="turned", bufs=3)
+                    for r in range(4):
+                        nc.tensor.transpose(turned[:, r * P : (r + 1) * P], got[r][:, j * C : (j + 1) * C], ident[:])
+                    gated = ring.tile([P, 512], BF16, name="gated", bufs=4)
+                    nc.scalar.activation(
+                        gated[:].rearrange("s (u p e) -> s u p e", u=2, e=2),
+                        turned[:].rearrange("s (u e p) -> s u p e", u=2, e=2),
+                        ACT.Copy,
+                        scale=gate_col[:, e0 + j : e0 + j + 1],
+                    )
+                    words = gated[:].bitcast(F32)
+                    for u in range(2):
+                        nc.tensor.transpose(back[:, (2 * jj + u) * P : (2 * jj + u + 1) * P], words[:, u * P : (u + 1) * P], ident[:])
+                nc.scalar.copy(
+                    q_in[:].bitcast(F32)[:, j0 * 256 : (j0 + 2) * 256].rearrange("p (j s u) -> p j s u", j=2, u=2),
+                    back[:].rearrange("p (j u s) -> p j s u", j=2, u=2),
+                )
+            grouped[ci, a] = q_in
+
+        def quantise(ci, e0, ne, a):
+            n = ne * C
+            cd = keep.tile([P, n], U32, name="codes%d_%d" % (ci, a), align_bytes=64)
+            sc = keep.tile([P, n], U8, name="scales%d_%d" % (ci, a), align_bytes=64)
+            nc.vector.quantize_mx(cd[:].bitcast(FP8X4), sc[:], grouped[ci, a][:])
+            codes[ci, a] = cd
+            scales[ci, a] = sc
+            if a == PASSES - 1:
+                for j in range(ne):
+                    e = e0 + j
+                    acc = psum.tile([P, C], F32, name="acc", bufs=3)
+                    for aa in range(PASSES):
+                        nc.tensor.matmul_mx(
+                            acc[:],
+                            lhsT=w_tiles[ci][:, (j * PASSES + aa) * N : (j * PASSES + aa + 1) * N].bitcast(FP8X4),
+                            lhsT_scale=w_scale[:, (e * PASSES + aa) * N : (e * PASSES + aa + 1) * N],
+                            rhs=codes[ci, aa][:, j * C : (j + 1) * C].bitcast(FP8X4),
+                            rhs_scale=scales[ci, aa][:, j * C : (j + 1) * C],
+                            start=(aa == 0),
+                            stop=(aa == PASSES - 1),
+                        )
+                    nc.scalar.activation(y[:, e * C : (e + 1) * C], acc[:], ACT.Relu, bias=bias[:, e : e + 1])
+
+        for i, piece in enumerate(pieces):
+            gather_and_gate(*piece)
+            if i > 0:
+                quantise(*pieces[i - 1])
+        quantise(*pieces[-1])
+
+        half = T // 2
+        for h in range(2):
+            cols = slice(h * half // 16, (h + 1) * half // 16)
+            s1 = ring.tile([P, half], F32, name="sum1", bufs=2)
+            nc.vector.tensor_copy(s1[:], y[:].indirect(pos_t[0][:, cols]))
+            s2 = ring.tile([P, half], F32, name="sum2", bufs=2)
+            nc.vector.tensor_tensor(s2[:], y[:].indirect(pos_t[1][:, cols]), s1[:], ADD)
+            s3 = ring.tile([P, half], F32, name="sum3", bufs=2)
+            nc.vector.tensor_tensor(s3[:], y[:].indirect(pos_t[2][:, cols]), s2[:], ADD)
+            nc.sync.dma_start(out[:, h * half : (h + 1) * half], s3[:])

@@ -1,7 +1,6 @@
 from contextlib import ExitStack
 
 import concourse.mybir as mybir
-from concourse.masks import make_identity
 
 K, T, E, C, N = 1536, 1024, 24, 128, 128
 S = E * C
@@ -9,6 +8,7 @@ P = 128
 PASSES = K // 512
 WINDOW = T + 32
 CHUNKS = (8, 8, 4, 2, 2)
+HEAD = 256
 FLOPS = 2 * K * S * N
 BYTES = 4 * K * T + E * K * N + E * K * N // 32 + 4 * N * E + 4 * S + 2 * P * (S + 3 * T) // 16 + 4 * N * T
 
@@ -21,6 +21,7 @@ U8 = mybir.dt.uint8
 FP8X4 = mybir.dt.float8_e4m3fn_x4
 ACT = mybir.ActivationFunctionType
 ADD = mybir.AluOpType.add
+MULT = mybir.AluOpType.mult
 
 
 def tile_moe_pre_lin_relu_kernel(tc, xT, w_words, w_scales, b, gate, offs, pos1, pos2, pos3, out):
@@ -33,10 +34,15 @@ def tile_moe_pre_lin_relu_kernel(tc, xT, w_words, w_scales, b, gate, offs, pos1,
         offs_t = keep.tile([P, S // 16], U16, name="offs_t")
         nc.sync.dma_start(offs_t[:], offs)
 
-        gate_rows = keep.tile([P, C], F32, name="gate_rows")
-        nc.gpsimd.memset(gate_rows[:], 0.0)
-        ident = keep.tile([P, P], F32, name="ident")
-        make_identity(nc, ident[:])
+        starts = [sum(CHUNKS[:i]) for i in range(len(CHUNKS))]
+        gates = []
+
+        def load_gate(ci):
+            gt = keep.tile([P, CHUNKS[ci] * C], F32, name="gate%d" % ci)
+            cuts = (0, HEAD, CHUNKS[ci] * C) if ci == 0 else (0, CHUNKS[ci] * C)
+            for lo, hi in zip(cuts[:-1], cuts[1:]):
+                nc.sync.dma_start(gt[:, lo:hi], gate[0:P, starts[ci] * C + lo : starts[ci] * C + hi])
+            gates.append(gt)
 
         planes = {}
         for a in range(PASSES):
@@ -45,35 +51,29 @@ def tile_moe_pre_lin_relu_kernel(tc, xT, w_words, w_scales, b, gate, offs, pos1,
                 nc.gpsimd.memset(plane[:, T:WINDOW], 0.0)
                 nc.sync.dma_start(plane[:, 0:T], xT[512 * a + r : 512 * (a + 1) : 4, :])
                 planes[a, r] = plane
-            if a == 0:
-                nc.sync.dma_start(gate_rows[0:E, :], gate[0:1, :].rearrange("o (e c) -> (o e) c", c=C))
+                if a == 0 and r == 0:
+                    load_gate(0)
+        for ci in range(1, len(CHUNKS)):
+            load_gate(ci)
 
         w_scale = keep.tile([P, E * PASSES * N], U8, name="w_scale", align_bytes=64)
         nc.gpsimd.memset(w_scale[:].bitcast(I32), 0)
 
-        gate_ps = psum.tile([P, 512], F32, name="turned", bufs=3)
-        nc.tensor.transpose(gate_ps[:, 0:P], gate_rows[:], ident[:])
-        gate_col = keep.tile([P, E], F32, name="gate_col")
-        nc.scalar.copy(gate_col[:], gate_ps[:, 0:E])
-
         w_src = w_words.rearrange("e a p n r -> p (e a) (n r)").bitcast(I32)
         sc_src = w_scales.rearrange("e a q n -> q (e a) n").bitcast(I32)
         sc_dst = w_scale[:].bitcast(I32).rearrange("p (g n) -> p g n", n=N // 4)
+        for q in range(4):
+            nc.sync.dma_start(sc_dst[32 * q : 32 * q + 4, :, :], sc_src[4 * q : 4 * q + 4, :, :])
+        bias = keep.tile([P, E], F32, name="bias")
+        nc.sync.dma_start(bias[:], b)
         w_tiles = []
-        first = 0
         for ci, ne in enumerate(CHUNKS):
             wt = keep.tile([P, ne * PASSES * N], U32, name="w%d" % ci, align_bytes=64)
             nc.sync.dma_start(
                 wt[:].bitcast(I32).rearrange("p (g n) -> p g n", n=N),
-                w_src[:, first * PASSES : (first + ne) * PASSES, :],
+                w_src[:, starts[ci] * PASSES : (starts[ci] + ne) * PASSES, :],
             )
             w_tiles.append(wt)
-            if ci == 0:
-                for q in range(4):
-                    nc.sync.dma_start(sc_dst[32 * q : 32 * q + 4, :, :], sc_src[4 * q : 4 * q + 4, :, :])
-                bias = keep.tile([P, E], F32, name="bias")
-                nc.sync.dma_start(bias[:], b)
-            first = first + ne
         pos_t = []
         for i, pos in enumerate((pos1, pos2, pos3)):
             pt = keep.tile([P, T // 16], U16, name="pos%d" % i)
@@ -82,70 +82,59 @@ def tile_moe_pre_lin_relu_kernel(tc, xT, w_words, w_scales, b, gate, offs, pos1,
 
         y = keep.tile([P, S], F32, name="y")
 
-        pieces = []
-        first = 0
-        for ci, ne in enumerate(CHUNKS):
-            for a in range(PASSES):
-                pieces.append((ci, first, ne, a))
-            first = first + ne
-
+        pieces = [(ci, starts[ci], ne, a) for ci, ne in enumerate(CHUNKS) for a in range(PASSES)]
         grouped = {}
         codes = {}
         scales = {}
 
         def gather_and_gate(ci, e0, ne, a):
             n = ne * C
-            got = []
+            g = ring.tile([P, 4 * n], F32, name="gathered", bufs=3)
             for r in range(4):
-                g = ring.tile([P, n], F32, name="gathered", bufs=8)
-                nc.vector.tensor_copy(g[:], planes[a, r][:].indirect(offs_t[:, e0 * 8 : (e0 + ne) * 8]))
-                got.append(g)
-            q_in = ring.tile([P, 4 * n], BF16, name="grouped", bufs=3, align_bytes=64)
-            for j0 in range(0, ne, 2):
-                back = psum.tile([P, 512], F32, name="back", bufs=2)
-                for jj in range(2):
-                    j = j0 + jj
-                    turned = psum.tile([P, 512], F32, name="turned", bufs=3)
-                    for r in range(4):
-                        nc.tensor.transpose(turned[:, r * P : (r + 1) * P], got[r][:, j * C : (j + 1) * C], ident[:])
-                    gated = ring.tile([P, 512], BF16, name="gated", bufs=4)
-                    nc.scalar.activation(
-                        gated[:].rearrange("s (u p e) -> s u p e", u=2, e=2),
-                        turned[:].rearrange("s (u e p) -> s u p e", u=2, e=2),
-                        ACT.Copy,
-                        scale=gate_col[:, e0 + j : e0 + j + 1],
+                cuts = (0, HEAD, n) if (ci, a, r) == (0, 0, 0) else (0, n)
+                for lo, hi in zip(cuts[:-1], cuts[1:]):
+                    nc.vector.tensor_tensor(
+                        g[:, r * n + lo : r * n + hi],
+                        planes[a, r][:].indirect(offs_t[:, (e0 * C + lo) // 16 : (e0 * C + hi) // 16]),
+                        gates[ci][:, lo:hi],
+                        MULT,
                     )
-                    words = gated[:].bitcast(F32)
-                    for u in range(2):
-                        nc.tensor.transpose(back[:, (2 * jj + u) * P : (2 * jj + u + 1) * P], words[:, u * P : (u + 1) * P], ident[:])
-                nc.scalar.copy(
-                    q_in[:].bitcast(F32)[:, j0 * 256 : (j0 + 2) * 256].rearrange("p (j s u) -> p j s u", j=2, u=2),
-                    back[:].rearrange("p (j u s) -> p j s u", j=2, u=2),
-                )
-            grouped[ci, a] = q_in
+            src = g[:].rearrange("p (r s) -> p s r", r=4)
+            if (ci, a) == (len(CHUNKS) - 1, PASSES - 1):
+                parts = []
+                for j, copy in enumerate((nc.scalar.copy, nc.vector.tensor_copy)):
+                    q_in = keep.tile([P, 4 * C], BF16, name="last%d" % j, align_bytes=64)
+                    copy(q_in[:].rearrange("p (s r) -> p s r", r=4), src[:, j * C : (j + 1) * C, :])
+                    parts.append((q_in, j, 1))
+                grouped[ci, a] = parts[::-1]
+            else:
+                q_in = ring.tile([P, 4 * n], BF16, name="grouped", bufs=3, align_bytes=64)
+                nc.scalar.copy(q_in[:].rearrange("p (s r) -> p s r", r=4), src)
+                grouped[ci, a] = [(q_in, 0, ne)]
 
         def quantise(ci, e0, ne, a):
-            n = ne * C
-            cd = keep.tile([P, n], U32, name="codes%d_%d" % (ci, a), align_bytes=64)
-            sc = keep.tile([P, n], U8, name="scales%d_%d" % (ci, a), align_bytes=64)
-            nc.vector.quantize_mx(cd[:].bitcast(FP8X4), sc[:], grouped[ci, a][:])
-            codes[ci, a] = cd
-            scales[ci, a] = sc
-            if a == PASSES - 1:
-                for j in range(ne):
-                    e = e0 + j
-                    acc = psum.tile([P, C], F32, name="acc", bufs=3)
-                    for aa in range(PASSES):
-                        nc.tensor.matmul_mx(
-                            acc[:],
-                            lhsT=w_tiles[ci][:, (j * PASSES + aa) * N : (j * PASSES + aa + 1) * N].bitcast(FP8X4),
-                            lhsT_scale=w_scale[:, (e * PASSES + aa) * N : (e * PASSES + aa + 1) * N],
-                            rhs=codes[ci, aa][:, j * C : (j + 1) * C].bitcast(FP8X4),
-                            rhs_scale=scales[ci, aa][:, j * C : (j + 1) * C],
-                            start=(aa == 0),
-                            stop=(aa == PASSES - 1),
-                        )
-                    nc.scalar.activation(y[:, e * C : (e + 1) * C], acc[:], ACT.Relu, bias=bias[:, e : e + 1])
+            for q_in, j0, nj in grouped[ci, a]:
+                cd = ring.tile([P, nj * C], U32, name="codes", bufs=6, align_bytes=64)
+                sc = ring.tile([P, nj * C], U8, name="scales", bufs=6, align_bytes=64)
+                nc.vector.quantize_mx(cd[:].bitcast(FP8X4), sc[:], q_in[:])
+                for j in range(nj):
+                    codes[e0 + j0 + j, a] = cd[:, j * C : (j + 1) * C]
+                    scales[e0 + j0 + j, a] = sc[:, j * C : (j + 1) * C]
+                if a == PASSES - 1:
+                    for j in range(j0, j0 + nj):
+                        e = e0 + j
+                        acc = psum.tile([P, C], F32, name="acc", bufs=8)
+                        for aa in range(PASSES):
+                            nc.tensor.matmul_mx(
+                                acc[:],
+                                lhsT=w_tiles[ci][:, (j * PASSES + aa) * N : (j * PASSES + aa + 1) * N].bitcast(FP8X4),
+                                lhsT_scale=w_scale[:, (e * PASSES + aa) * N : (e * PASSES + aa + 1) * N],
+                                rhs=codes[e, aa].bitcast(FP8X4),
+                                rhs_scale=scales[e, aa],
+                                start=(aa == 0),
+                                stop=(aa == PASSES - 1),
+                            )
+                        nc.scalar.activation(y[:, e * C : (e + 1) * C], acc[:], ACT.Relu, bias=bias[:, e : e + 1])
 
         for i, piece in enumerate(pieces):
             gather_and_gate(*piece)
@@ -153,13 +142,11 @@ def tile_moe_pre_lin_relu_kernel(tc, xT, w_words, w_scales, b, gate, offs, pos1,
                 quantise(*pieces[i - 1])
         quantise(*pieces[-1])
 
-        half = T // 2
-        for h in range(2):
-            cols = slice(h * half // 16, (h + 1) * half // 16)
-            s1 = ring.tile([P, half], F32, name="sum1", bufs=2)
-            nc.vector.tensor_copy(s1[:], y[:].indirect(pos_t[0][:, cols]))
-            s2 = ring.tile([P, half], F32, name="sum2", bufs=2)
-            nc.vector.tensor_tensor(s2[:], y[:].indirect(pos_t[1][:, cols]), s1[:], ADD)
-            s3 = ring.tile([P, half], F32, name="sum3", bufs=2)
-            nc.vector.tensor_tensor(s3[:], y[:].indirect(pos_t[2][:, cols]), s2[:], ADD)
-            nc.sync.dma_start(out[:, h * half : (h + 1) * half], s3[:])
+        s1 = ring.tile([P, T], F32, name="sum1")
+        nc.vector.tensor_copy(s1[:], y[:].indirect(pos_t[0][:]))
+        s2 = ring.tile([P, T], F32, name="sum2")
+        nc.vector.tensor_tensor(s2[:], y[:].indirect(pos_t[1][:]), s1[:], ADD)
+        s3 = ring.tile([P, T], F32, name="sum3")
+        for lo, hi in ((0, 512), (512, 896), (896, T)):
+            nc.vector.tensor_tensor(s3[:, lo:hi], y[:].indirect(pos_t[2][:, lo // 16 : hi // 16]), s2[:, lo:hi], ADD)
+            nc.sync.dma_start(out[:, lo:hi], s3[:, lo:hi])

@@ -7,8 +7,8 @@ S = E * C
 P = 128
 PASSES = K // 512
 WINDOW = T + 32
-CHUNKS = (8, 8, 4, 2, 2)
-HEAD = 256
+GROUP = 8
+HEAD = 384
 FLOPS = 2 * K * S * N
 BYTES = 4 * K * T + E * K * N + E * K * N // 32 + 4 * N * E + 4 * S + 2 * P * (S + 3 * T) // 16 + 4 * N * T
 
@@ -26,6 +26,7 @@ MULT = mybir.AluOpType.mult
 
 def tile_moe_pre_lin_relu_kernel(tc, xT, w_words, w_scales, b, gate, offs, pos1, pos2, pos3, out):
     nc = tc.nc
+    groups = E // GROUP
     with ExitStack() as ctx:
         keep = ctx.enter_context(tc.tile_pool(name="keep", bufs=1))
         ring = ctx.enter_context(tc.tile_pool(name="ring", bufs=1))
@@ -34,30 +35,21 @@ def tile_moe_pre_lin_relu_kernel(tc, xT, w_words, w_scales, b, gate, offs, pos1,
         offs_t = keep.tile([P, S // 16], U16, name="offs_t")
         nc.sync.dma_start(offs_t[:], offs)
 
-        starts = [sum(CHUNKS[:i]) for i in range(len(CHUNKS))]
-        gates = []
-
-        def load_gate(ci):
-            gt = keep.tile([P, CHUNKS[ci] * C], F32, name="gate%d" % ci)
-            cuts = (0, HEAD, CHUNKS[ci] * C) if ci == 0 else (0, CHUNKS[ci] * C)
-            for lo, hi in zip(cuts[:-1], cuts[1:]):
-                nc.sync.dma_start(gt[:, lo:hi], gate[0:P, starts[ci] * C + lo : starts[ci] * C + hi])
-            gates.append(gt)
-
+        gate_t = keep.tile([P, S], F32, name="gate_t")
         planes = {}
         for a in range(PASSES):
             for r in range(4):
                 plane = keep.tile([P, WINDOW], F32, name="plane%d_%d" % (a, r))
-                nc.gpsimd.memset(plane[:, T:WINDOW], 0.0)
+                nc.vector.memset(plane[:, T:WINDOW], 0.0)
                 nc.sync.dma_start(plane[:, 0:T], xT[512 * a + r : 512 * (a + 1) : 4, :])
                 planes[a, r] = plane
                 if a == 0 and r == 0:
-                    load_gate(0)
-        for ci in range(1, len(CHUNKS)):
-            load_gate(ci)
+                    nc.sync.dma_start(gate_t[:, 0:HEAD], gate[0:P, 0:HEAD])
+                    nc.sync.dma_start(gate_t[:, HEAD : GROUP * C], gate[0:P, HEAD : GROUP * C])
+        nc.sync.dma_start(gate_t[:, GROUP * C : S], gate[0:P, GROUP * C : S])
 
         w_scale = keep.tile([P, E * PASSES * N], U8, name="w_scale", align_bytes=64)
-        nc.gpsimd.memset(w_scale[:].bitcast(I32), 0)
+        nc.vector.memset(w_scale[:].bitcast(I32), 0)
 
         w_src = w_words.rearrange("e a p n r -> p (e a) (n r)").bitcast(I32)
         sc_src = w_scales.rearrange("e a q n -> q (e a) n").bitcast(I32)
@@ -67,11 +59,11 @@ def tile_moe_pre_lin_relu_kernel(tc, xT, w_words, w_scales, b, gate, offs, pos1,
         bias = keep.tile([P, E], F32, name="bias")
         nc.sync.dma_start(bias[:], b)
         w_tiles = []
-        for ci, ne in enumerate(CHUNKS):
-            wt = keep.tile([P, ne * PASSES * N], U32, name="w%d" % ci, align_bytes=64)
+        for gi in range(groups):
+            wt = keep.tile([P, GROUP * PASSES * N], U32, name="w%d" % gi, align_bytes=64)
             nc.sync.dma_start(
                 wt[:].bitcast(I32).rearrange("p (g n) -> p g n", n=N),
-                w_src[:, starts[ci] * PASSES : (starts[ci] + ne) * PASSES, :],
+                w_src[:, gi * GROUP * PASSES : (gi + 1) * GROUP * PASSES, :],
             )
             w_tiles.append(wt)
         pos_t = []
@@ -82,52 +74,62 @@ def tile_moe_pre_lin_relu_kernel(tc, xT, w_words, w_scales, b, gate, offs, pos1,
 
         y = keep.tile([P, S], F32, name="y")
 
-        pieces = [(ci, starts[ci], ne, a) for ci, ne in enumerate(CHUNKS) for a in range(PASSES)]
+        pieces = [(gi * GROUP, GROUP, a) for gi in range(groups - 1) for a in range(PASSES)]
+        pieces.extend([(16, 8, 0), (16, 4, 1), (16, 4, 2), (20, 4, 1), (20, 2, 2), (22, 2, 2)])
+        last = len(pieces) - 1
         grouped = {}
         codes = {}
         scales = {}
 
-        def gather_and_gate(ci, e0, ne, a):
+        def gather_and_gate(i):
+            e0, ne, a = pieces[i]
             n = ne * C
-            g = ring.tile([P, 4 * n], F32, name="gathered", bufs=3)
+            if i == last:
+                g = ring.tile([P, 4 * n], F32, name="held", align_bytes=64)
+            else:
+                g = ring.tile([P, 4 * n], F32, name="gathered", bufs=3)
             for r in range(4):
-                cuts = (0, HEAD, n) if (ci, a, r) == (0, 0, 0) else (0, n)
+                cuts = (0, HEAD, n) if (i, r) == (0, 0) else (0, n)
                 for lo, hi in zip(cuts[:-1], cuts[1:]):
                     nc.vector.tensor_tensor(
                         g[:, r * n + lo : r * n + hi],
                         planes[a, r][:].indirect(offs_t[:, (e0 * C + lo) // 16 : (e0 * C + hi) // 16]),
-                        gates[ci][:, lo:hi],
+                        gate_t[:, e0 * C + lo : e0 * C + hi],
                         MULT,
                     )
-            src = g[:].rearrange("p (r s) -> p s r", r=4)
-            if (ci, a) == (len(CHUNKS) - 1, PASSES - 1):
+            src = g[:].rearrange("p (r c i) -> p c r i", r=4, i=4)
+            if i == len(pieces) - 1:
                 parts = []
                 for j, copy in enumerate((nc.scalar.copy, nc.vector.tensor_copy)):
                     q_in = keep.tile([P, 4 * C], BF16, name="last%d" % j, align_bytes=64)
-                    copy(q_in[:].rearrange("p (s r) -> p s r", r=4), src[:, j * C : (j + 1) * C, :])
-                    parts.append((q_in, j, 1))
-                grouped[ci, a] = parts[::-1]
+                    copy(q_in[:].rearrange("p (c i r) -> p c r i", r=4, i=4), src[:, j * C // 4 : (j + 1) * C // 4, :, :])
+                    parts.append((q_in, e0 + j, 1))
+                grouped[i] = parts[::-1]
             else:
-                q_in = ring.tile([P, 4 * n], BF16, name="grouped", bufs=3, align_bytes=64)
-                nc.scalar.copy(q_in[:].rearrange("p (s r) -> p s r", r=4), src)
-                grouped[ci, a] = [(q_in, 0, ne)]
+                if i == last - 2:
+                    q_in = ring.tile([P, 4 * n], BF16, name="held", align_bytes=64)
+                else:
+                    q_in = ring.tile([P, 4 * n], BF16, name="grouped", bufs=3, align_bytes=64)
+                nc.scalar.copy(q_in[:].rearrange("p (c i r) -> p c r i", r=4, i=4), src)
+                grouped[i] = [(q_in, e0, ne)]
 
-        def quantise(ci, e0, ne, a):
-            for q_in, j0, nj in grouped[ci, a]:
-                cd = ring.tile([P, nj * C], U32, name="codes", bufs=6, align_bytes=64)
-                sc = ring.tile([P, nj * C], U8, name="scales", bufs=6, align_bytes=64)
+        def quantise(i):
+            a = pieces[i][2]
+            for q_in, e0, ne in grouped[i]:
+                cd = ring.tile([P, ne * C], U32, name="codes", bufs=5, align_bytes=64)
+                sc = ring.tile([P, ne * C], U8, name="scales", bufs=5, align_bytes=64)
                 nc.vector.quantize_mx(cd[:].bitcast(FP8X4), sc[:], q_in[:])
-                for j in range(nj):
-                    codes[e0 + j0 + j, a] = cd[:, j * C : (j + 1) * C]
-                    scales[e0 + j0 + j, a] = sc[:, j * C : (j + 1) * C]
+                for j in range(ne):
+                    codes[e0 + j, a] = cd[:, j * C : (j + 1) * C]
+                    scales[e0 + j, a] = sc[:, j * C : (j + 1) * C]
                 if a == PASSES - 1:
-                    for j in range(j0, j0 + nj):
-                        e = e0 + j
+                    for e in range(e0, e0 + ne):
                         acc = psum.tile([P, C], F32, name="acc", bufs=8)
                         for aa in range(PASSES):
+                            col = (e % GROUP * PASSES + aa) * N
                             nc.tensor.matmul_mx(
                                 acc[:],
-                                lhsT=w_tiles[ci][:, (j * PASSES + aa) * N : (j * PASSES + aa + 1) * N].bitcast(FP8X4),
+                                lhsT=w_tiles[e // GROUP][:, col : col + N].bitcast(FP8X4),
                                 lhsT_scale=w_scale[:, (e * PASSES + aa) * N : (e * PASSES + aa + 1) * N],
                                 rhs=codes[e, aa].bitcast(FP8X4),
                                 rhs_scale=scales[e, aa],
@@ -136,17 +138,19 @@ def tile_moe_pre_lin_relu_kernel(tc, xT, w_words, w_scales, b, gate, offs, pos1,
                             )
                         nc.scalar.activation(y[:, e * C : (e + 1) * C], acc[:], ACT.Relu, bias=bias[:, e : e + 1])
 
-        for i, piece in enumerate(pieces):
-            gather_and_gate(*piece)
+        for i in range(len(pieces)):
+            gather_and_gate(i)
             if i > 0:
-                quantise(*pieces[i - 1])
-        quantise(*pieces[-1])
+                quantise(i - 1)
+        quantise(len(pieces) - 1)
 
-        s1 = ring.tile([P, T], F32, name="sum1")
-        nc.vector.tensor_copy(s1[:], y[:].indirect(pos_t[0][:]))
-        s2 = ring.tile([P, T], F32, name="sum2")
-        nc.vector.tensor_tensor(s2[:], y[:].indirect(pos_t[1][:]), s1[:], ADD)
-        s3 = ring.tile([P, T], F32, name="sum3")
+        sums = ring.tile([P, 3 * T], F32, name="gathered", bufs=3)
+        for lo, hi in ((0, 512), (512, T)):
+            nc.vector.tensor_copy(sums[:, lo:hi], y[:].indirect(pos_t[0][:, lo // 16 : hi // 16]))
+        for lo, hi in ((0, 512), (512, T)):
+            nc.vector.tensor_tensor(sums[:, T + lo : T + hi], y[:].indirect(pos_t[1][:, lo // 16 : hi // 16]), sums[:, lo:hi], ADD)
         for lo, hi in ((0, 512), (512, 896), (896, T)):
-            nc.vector.tensor_tensor(s3[:, lo:hi], y[:].indirect(pos_t[2][:, lo // 16 : hi // 16]), s2[:, lo:hi], ADD)
-            nc.sync.dma_start(out[:, lo:hi], s3[:, lo:hi])
+            nc.vector.tensor_tensor(
+                sums[:, 2 * T + lo : 2 * T + hi], y[:].indirect(pos_t[2][:, lo // 16 : hi // 16]), sums[:, T + lo : T + hi], ADD
+            )
+            nc.sync.dma_start(out[:, lo:hi], sums[:, 2 * T + lo : 2 * T + hi])

@@ -5,12 +5,18 @@ import concourse.mybir as mybir
 K, T, E, C, N = 1536, 1024, 24, 128, 128
 S = E * C
 P = 128
-PASSES = K // 512
-WINDOW = T + 32
+PACK = 4
+K_PASS = P * PACK
+PASSES = K // K_PASS
+PER_COLUMN = 16
 GROUP = 8
-HEAD = 384
+WINDOW = T + 32
+HEAD_CUTS = (0, 128, 384, GROUP * C)
+TOKEN_HALVES = ((0, T // 2), (T // 2, T))
+STORE_CUTS = ((0, T // 2), (T // 2, T - 128), (T - 128, T))
+
 FLOPS = 2 * K * S * N
-BYTES = 4 * K * T + E * K * N + E * K * N // 32 + 4 * N * E + 4 * S + 2 * P * (S + 3 * T) // 16 + 4 * N * T
+BYTES = 4 * K * T + E * K * N + E * K * N // 32 + 4 * N * E + 4 * S + 2 * P * (S + 3 * T) // PER_COLUMN + 4 * N * T
 
 F32 = mybir.dt.float32
 BF16 = mybir.dt.bfloat16
@@ -19,138 +25,143 @@ U32 = mybir.dt.uint32
 U16 = mybir.dt.uint16
 U8 = mybir.dt.uint8
 FP8X4 = mybir.dt.float8_e4m3fn_x4
-ACT = mybir.ActivationFunctionType
+RELU = mybir.ActivationFunctionType.Relu
 ADD = mybir.AluOpType.add
 MULT = mybir.AluOpType.mult
 
 
+def piece_order():
+    tail = E - GROUP
+    half = GROUP // 2
+    pieces = [(e0, GROUP, a) for e0 in range(0, tail, GROUP) for a in range(PASSES)]
+    pieces.append((tail, GROUP, 0))
+    pieces.extend((tail, half, a) for a in range(1, PASSES))
+    pieces.extend((tail + half, half, a) for a in range(1, PASSES - 1))
+    pieces.extend([(E - 4, 2, PASSES - 1), (E - 2, 1, PASSES - 1), (E - 1, 1, PASSES - 1)])
+    return pieces
+
+
+def entries(list_tile, lo, hi):
+    return list_tile[:, lo // PER_COLUMN : hi // PER_COLUMN]
+
+
 def tile_moe_pre_lin_relu_kernel(tc, xT, w_words, w_scales, b, gate, offs, pos1, pos2, pos3, out):
     nc = tc.nc
-    groups = E // GROUP
     with ExitStack() as ctx:
         keep = ctx.enter_context(tc.tile_pool(name="keep", bufs=1))
         ring = ctx.enter_context(tc.tile_pool(name="ring", bufs=1))
         psum = ctx.enter_context(tc.psum_pool(name="psum", bufs=1))
 
-        offs_t = keep.tile([P, S // 16], U16, name="offs_t")
+        offs_t = keep.tile([P, S // PER_COLUMN], U16, name="offs_t")
         nc.sync.dma_start(offs_t[:], offs)
 
         gate_t = keep.tile([P, S], F32, name="gate_t")
         planes = {}
         for a in range(PASSES):
-            for r in range(4):
+            for r in range(PACK):
                 plane = keep.tile([P, WINDOW], F32, name="plane%d_%d" % (a, r))
                 nc.vector.memset(plane[:, T:WINDOW], 0.0)
-                nc.sync.dma_start(plane[:, 0:T], xT[512 * a + r : 512 * (a + 1) : 4, :])
+                nc.sync.dma_start(plane[:, 0:T], xT[K_PASS * a + r : K_PASS * (a + 1) : PACK, :])
                 planes[a, r] = plane
                 if a == 0 and r == 0:
-                    nc.sync.dma_start(gate_t[:, 0:HEAD], gate[0:P, 0:HEAD])
-                    nc.sync.dma_start(gate_t[:, HEAD : GROUP * C], gate[0:P, HEAD : GROUP * C])
+                    for lo, hi in zip(HEAD_CUTS[:-1], HEAD_CUTS[1:]):
+                        nc.sync.dma_start(gate_t[:, lo:hi], gate[0:P, lo:hi])
         nc.sync.dma_start(gate_t[:, GROUP * C : S], gate[0:P, GROUP * C : S])
 
         w_scale = keep.tile([P, E * PASSES * N], U8, name="w_scale", align_bytes=64)
         nc.vector.memset(w_scale[:].bitcast(I32), 0)
-
-        w_src = w_words.rearrange("e a p n r -> p (e a) (n r)").bitcast(I32)
-        sc_src = w_scales.rearrange("e a q n -> q (e a) n").bitcast(I32)
-        sc_dst = w_scale[:].bitcast(I32).rearrange("p (g n) -> p g n", n=N // 4)
-        for q in range(4):
-            nc.sync.dma_start(sc_dst[32 * q : 32 * q + 4, :, :], sc_src[4 * q : 4 * q + 4, :, :])
+        words_src = w_words.rearrange("e a p n r -> p (e a) (n r)").bitcast(I32)
+        scale_src = w_scales.rearrange("e a q n -> q (e a) n").bitcast(I32)
+        scale_dst = w_scale[:].bitcast(I32).rearrange("p (g n) -> p g n", n=N // 4)
+        for quadrant in range(4):
+            nc.sync.dma_start(scale_dst[32 * quadrant : 32 * quadrant + 4, :, :], scale_src[4 * quadrant : 4 * quadrant + 4, :, :])
         bias = keep.tile([P, E], F32, name="bias")
         nc.sync.dma_start(bias[:], b)
         w_tiles = []
-        for gi in range(groups):
+        for gi in range(E // GROUP):
             wt = keep.tile([P, GROUP * PASSES * N], U32, name="w%d" % gi, align_bytes=64)
             nc.sync.dma_start(
                 wt[:].bitcast(I32).rearrange("p (g n) -> p g n", n=N),
-                w_src[:, gi * GROUP * PASSES : (gi + 1) * GROUP * PASSES, :],
+                words_src[:, gi * GROUP * PASSES : (gi + 1) * GROUP * PASSES, :],
             )
             w_tiles.append(wt)
         pos_t = []
-        for i, pos in enumerate((pos1, pos2, pos3)):
-            pt = keep.tile([P, T // 16], U16, name="pos%d" % i)
+        for choice, pos in enumerate((pos1, pos2, pos3)):
+            pt = keep.tile([P, T // PER_COLUMN], U16, name="pos%d" % choice)
             nc.sync.dma_start(pt[:], pos)
             pos_t.append(pt)
 
         y = keep.tile([P, S], F32, name="y")
 
-        pieces = [(gi * GROUP, GROUP, a) for gi in range(groups - 1) for a in range(PASSES)]
-        pieces.extend([(16, 8, 0), (16, 4, 1), (16, 4, 2), (20, 4, 1), (20, 2, 2), (22, 2, 2)])
+        pieces = piece_order()
         last = len(pieces) - 1
-        grouped = {}
+        rounded = {}
         codes = {}
         scales = {}
 
-        def gather_and_gate(i):
-            e0, ne, a = pieces[i]
-            n = ne * C
-            if i == last:
-                g = ring.tile([P, 4 * n], F32, name="held", align_bytes=64)
+        def gather_and_round(i):
+            e0, experts, a = pieces[i]
+            width = experts * C
+            if i == last - 1:
+                gathered = ring.tile([P, PACK * width], F32, name="held", align_bytes=64)
             else:
-                g = ring.tile([P, 4 * n], F32, name="gathered", bufs=3)
-            for r in range(4):
-                cuts = (0, HEAD, n) if (i, r) == (0, 0) else (0, n)
+                gathered = ring.tile([P, PACK * width], F32, name="gathered", bufs=3)
+            for r in range(PACK):
+                cuts = HEAD_CUTS if (i, r) == (0, 0) else (0, width)
                 for lo, hi in zip(cuts[:-1], cuts[1:]):
                     nc.vector.tensor_tensor(
-                        g[:, r * n + lo : r * n + hi],
-                        planes[a, r][:].indirect(offs_t[:, (e0 * C + lo) // 16 : (e0 * C + hi) // 16]),
+                        gathered[:, r * width + lo : r * width + hi],
+                        planes[a, r][:].indirect(entries(offs_t, e0 * C + lo, e0 * C + hi)),
                         gate_t[:, e0 * C + lo : e0 * C + hi],
                         MULT,
                     )
-            src = g[:].rearrange("p (r c i) -> p c r i", r=4, i=4)
-            if i == len(pieces) - 1:
-                parts = []
-                for j, copy in enumerate((nc.scalar.copy, nc.vector.tensor_copy)):
-                    q_in = keep.tile([P, 4 * C], BF16, name="last%d" % j, align_bytes=64)
-                    copy(q_in[:].rearrange("p (c i r) -> p c r i", r=4, i=4), src[:, j * C // 4 : (j + 1) * C // 4, :, :])
-                    parts.append((q_in, e0 + j, 1))
-                grouped[i] = parts[::-1]
+            if i == last - 3:
+                rounded[i] = ring.tile([P, PACK * width], BF16, name="held", align_bytes=64)
             else:
-                if i == last - 2:
-                    q_in = ring.tile([P, 4 * n], BF16, name="held", align_bytes=64)
-                else:
-                    q_in = ring.tile([P, 4 * n], BF16, name="grouped", bufs=3, align_bytes=64)
-                nc.scalar.copy(q_in[:].rearrange("p (c i r) -> p c r i", r=4, i=4), src)
-                grouped[i] = [(q_in, e0, ne)]
+                rounded[i] = ring.tile([P, PACK * width], BF16, name="rounded", bufs=3, align_bytes=64)
+            copy = nc.vector.tensor_copy if i == last else nc.scalar.copy
+            copy(
+                rounded[i][:].rearrange("p (c i r) -> p c r i", r=PACK, i=4),
+                gathered[:].rearrange("p (r c i) -> p c r i", r=PACK, i=4),
+            )
 
-        def quantise(i):
-            a = pieces[i][2]
-            for q_in, e0, ne in grouped[i]:
-                cd = ring.tile([P, ne * C], U32, name="codes", bufs=5, align_bytes=64)
-                sc = ring.tile([P, ne * C], U8, name="scales", bufs=5, align_bytes=64)
-                nc.vector.quantize_mx(cd[:].bitcast(FP8X4), sc[:], q_in[:])
-                for j in range(ne):
-                    codes[e0 + j, a] = cd[:, j * C : (j + 1) * C]
-                    scales[e0 + j, a] = sc[:, j * C : (j + 1) * C]
-                if a == PASSES - 1:
-                    for e in range(e0, e0 + ne):
-                        acc = psum.tile([P, C], F32, name="acc", bufs=8)
-                        for aa in range(PASSES):
-                            col = (e % GROUP * PASSES + aa) * N
-                            nc.tensor.matmul_mx(
-                                acc[:],
-                                lhsT=w_tiles[e // GROUP][:, col : col + N].bitcast(FP8X4),
-                                lhsT_scale=w_scale[:, (e * PASSES + aa) * N : (e * PASSES + aa + 1) * N],
-                                rhs=codes[e, aa].bitcast(FP8X4),
-                                rhs_scale=scales[e, aa],
-                                start=(aa == 0),
-                                stop=(aa == PASSES - 1),
-                            )
-                        nc.scalar.activation(y[:, e * C : (e + 1) * C], acc[:], ACT.Relu, bias=bias[:, e : e + 1])
+        def quantise_and_multiply(i):
+            e0, experts, a = pieces[i]
+            piece_codes = ring.tile([P, experts * C], U32, name="codes", bufs=5, align_bytes=64)
+            piece_scales = ring.tile([P, experts * C], U8, name="scales", bufs=5, align_bytes=64)
+            nc.vector.quantize_mx(piece_codes[:].bitcast(FP8X4), piece_scales[:], rounded[i][:])
+            for j in range(experts):
+                codes[e0 + j, a] = piece_codes[:, j * C : (j + 1) * C]
+                scales[e0 + j, a] = piece_scales[:, j * C : (j + 1) * C]
+            if a == PASSES - 1:
+                for e in range(e0, e0 + experts):
+                    acc = psum.tile([P, C], F32, name="acc", bufs=8)
+                    for k_pass in range(PASSES):
+                        col = (e % GROUP * PASSES + k_pass) * N
+                        nc.tensor.matmul_mx(
+                            acc[:],
+                            lhsT=w_tiles[e // GROUP][:, col : col + N].bitcast(FP8X4),
+                            lhsT_scale=w_scale[:, (e * PASSES + k_pass) * N : (e * PASSES + k_pass + 1) * N],
+                            rhs=codes[e, k_pass].bitcast(FP8X4),
+                            rhs_scale=scales[e, k_pass],
+                            start=(k_pass == 0),
+                            stop=(k_pass == PASSES - 1),
+                        )
+                    nc.scalar.activation(y[:, e * C : (e + 1) * C], acc[:], RELU, bias=bias[:, e : e + 1])
 
         for i in range(len(pieces)):
-            gather_and_gate(i)
+            gather_and_round(i)
             if i > 0:
-                quantise(i - 1)
-        quantise(len(pieces) - 1)
+                quantise_and_multiply(i - 1)
+        quantise_and_multiply(last)
 
         sums = ring.tile([P, 3 * T], F32, name="gathered", bufs=3)
-        for lo, hi in ((0, 512), (512, T)):
-            nc.vector.tensor_copy(sums[:, lo:hi], y[:].indirect(pos_t[0][:, lo // 16 : hi // 16]))
-        for lo, hi in ((0, 512), (512, T)):
-            nc.vector.tensor_tensor(sums[:, T + lo : T + hi], y[:].indirect(pos_t[1][:, lo // 16 : hi // 16]), sums[:, lo:hi], ADD)
-        for lo, hi in ((0, 512), (512, 896), (896, T)):
+        for lo, hi in TOKEN_HALVES:
+            nc.vector.tensor_copy(sums[:, lo:hi], y[:].indirect(entries(pos_t[0], lo, hi)))
+        for lo, hi in TOKEN_HALVES:
+            nc.vector.tensor_tensor(sums[:, T + lo : T + hi], y[:].indirect(entries(pos_t[1], lo, hi)), sums[:, lo:hi], ADD)
+        for lo, hi in STORE_CUTS:
             nc.vector.tensor_tensor(
-                sums[:, 2 * T + lo : 2 * T + hi], y[:].indirect(pos_t[2][:, lo // 16 : hi // 16]), sums[:, T + lo : T + hi], ADD
+                sums[:, 2 * T + lo : 2 * T + hi], y[:].indirect(entries(pos_t[2], lo, hi)), sums[:, T + lo : T + hi], ADD
             )
             nc.sync.dma_start(out[:, lo:hi], sums[:, 2 * T + lo : 2 * T + hi])

@@ -9,9 +9,11 @@ PACK = 4
 K_PASS = P * PACK
 PASSES = K // K_PASS
 PER_COLUMN = 16
-GROUP = 8
-WINDOW = T + 32
-HEAD_CUTS = (0, 128, 384, GROUP * C)
+CHUNK = 8
+WIDE = S + 8
+TAPER = ((0, 12), (12, 6), (18, 3), (21, 2), (23, 1))
+NARROW = TAPER[0][1] * C + 8
+HEAD_CUTS = (0, 256, 768, 1792, S)
 TOKEN_HALVES = ((0, T // 2), (T // 2, T))
 STORE_CUTS = ((0, T // 2), (T // 2, T - 128), (T - 128, T))
 
@@ -30,19 +32,17 @@ ADD = mybir.AluOpType.add
 MULT = mybir.AluOpType.mult
 
 
-def piece_order():
-    tail = E - GROUP
-    half = GROUP // 2
-    pieces = [(e0, GROUP, a) for e0 in range(0, tail, GROUP) for a in range(PASSES)]
-    pieces.append((tail, GROUP, 0))
-    pieces.extend((tail, half, a) for a in range(1, PASSES))
-    pieces.extend((tail + half, half, a) for a in range(1, PASSES - 1))
-    pieces.extend([(E - 4, 2, PASSES - 1), (E - 2, 1, PASSES - 1), (E - 1, 1, PASSES - 1)])
-    return pieces
-
-
 def entries(list_tile, lo, hi):
     return list_tile[:, lo // PER_COLUMN : hi // PER_COLUMN]
+
+
+def powers_of_two(experts):
+    runs, first = [], 0
+    while first < experts:
+        count = max(c for c in (CHUNK, 4, 2, 1) if c <= experts - first)
+        runs.append((first, count))
+        first = first + count
+    return runs
 
 
 def tile_moe_pre_lin_relu_kernel(tc, xT, w_words, w_scales, b, gate, offs, pos1, pos2, pos3, out):
@@ -50,23 +50,46 @@ def tile_moe_pre_lin_relu_kernel(tc, xT, w_words, w_scales, b, gate, offs, pos1,
     with ExitStack() as ctx:
         keep = ctx.enter_context(tc.tile_pool(name="keep", bufs=1))
         ring = ctx.enter_context(tc.tile_pool(name="ring", bufs=1))
+        stage = ctx.enter_context(tc.tile_pool(name="stage", bufs=1))
         psum = ctx.enter_context(tc.psum_pool(name="psum", bufs=1))
+
+        def placed(name, columns, dtype, offset):
+            return stage.tile([P, columns], dtype, name=name, offset=offset, align_bytes=64)
+
+        full = 4 * PACK * S
+        g0_at = 0
+        ga_at = 4 * E * PASSES * N
+        y_at = ga_at + 4 * PACK * 12 * C
+        g1_at = y_at + 4 * S
+        gb_at = g1_at
+        ra_at = gb_at + 4 * PACK * 6 * C
+        rb_at = ra_at + 2 * PACK * 12 * C
+        codes_at = rb_at + 2 * PACK * 6 * C
+        sums_at = ga_at
+        rc_at = sums_at + 4 * 3 * T
+        rd_at = rc_at + 2 * PACK * 3 * C
+        re_at = rd_at + 2 * PACK * 2 * C
+        late_codes_at = re_at + 2 * PACK * C
+        gathered_at = (ga_at, gb_at, ra_at, rb_at, rc_at)
+        rounded_at = (ra_at, rb_at, rc_at, rd_at, re_at)
 
         offs_t = keep.tile([P, S // PER_COLUMN], U16, name="offs_t")
         nc.sync.dma_start(offs_t[:], offs)
 
         gate_t = keep.tile([P, S], F32, name="gate_t")
-        planes = {}
-        for a in range(PASSES):
-            for r in range(PACK):
-                plane = keep.tile([P, WINDOW], F32, name="plane%d_%d" % (a, r))
-                nc.vector.memset(plane[:, T:WINDOW], 0.0)
-                nc.sync.dma_start(plane[:, 0:T], xT[K_PASS * a + r : K_PASS * (a + 1) : PACK, :])
-                planes[a, r] = plane
-                if a == 0 and r == 0:
-                    for lo, hi in zip(HEAD_CUTS[:-1], HEAD_CUTS[1:]):
-                        nc.sync.dma_start(gate_t[:, lo:hi], gate[0:P, lo:hi])
-        nc.sync.dma_start(gate_t[:, GROUP * C : S], gate[0:P, GROUP * C : S])
+        wide = [keep.tile([P, WIDE], F32, name="wide%d" % i) for i in range(3)]
+
+        def load_plane(window, a, r):
+            nc.sync.dma_start(window[:, 0:T], xT[K_PASS * a + r : K_PASS * (a + 1) : PACK, :])
+
+        load_plane(wide[0], 0, 0)
+        for lo, hi in zip(HEAD_CUTS[:-1], HEAD_CUTS[1:]):
+            nc.sync.dma_start(gate_t[:, lo:hi], gate[0:P, lo:hi])
+        load_plane(wide[1], 0, 1)
+        load_plane(wide[2], 0, 2)
+        narrow = [keep.tile([P, NARROW], F32, name="narrow%d" % i) for i in range(2)]
+        for i in range(2):
+            load_plane(narrow[i], PASSES - 1, 1 + i)
 
         w_scale = keep.tile([P, E * PASSES * N], U8, name="w_scale", align_bytes=64)
         nc.vector.memset(w_scale[:].bitcast(I32), 0)
@@ -77,85 +100,110 @@ def tile_moe_pre_lin_relu_kernel(tc, xT, w_words, w_scales, b, gate, offs, pos1,
             nc.sync.dma_start(scale_dst[32 * quadrant : 32 * quadrant + 4, :, :], scale_src[4 * quadrant : 4 * quadrant + 4, :, :])
         bias = keep.tile([P, E], F32, name="bias")
         nc.sync.dma_start(bias[:], b)
-        w_tiles = []
-        for gi in range(E // GROUP):
-            wt = keep.tile([P, GROUP * PASSES * N], U32, name="w%d" % gi, align_bytes=64)
-            nc.sync.dma_start(
-                wt[:].bitcast(I32).rearrange("p (g n) -> p g n", n=N),
-                words_src[:, gi * GROUP * PASSES : (gi + 1) * GROUP * PASSES, :],
-            )
-            w_tiles.append(wt)
         pos_t = []
         for choice, pos in enumerate((pos1, pos2, pos3)):
             pt = keep.tile([P, T // PER_COLUMN], U16, name="pos%d" % choice)
             nc.sync.dma_start(pt[:], pos)
             pos_t.append(pt)
 
-        y = keep.tile([P, S], F32, name="y")
-
-        pieces = piece_order()
-        last = len(pieces) - 1
-        rounded = {}
         codes = {}
         scales = {}
 
-        def gather_and_round(i):
-            e0, experts, a = pieces[i]
+        def gather(gathered, window, r, e0, experts, cuts):
             width = experts * C
-            if i == last - 1:
-                gathered = ring.tile([P, PACK * width], F32, name="held", align_bytes=64)
-            else:
-                gathered = ring.tile([P, PACK * width], F32, name="gathered", bufs=3)
-            for r in range(PACK):
-                cuts = HEAD_CUTS if (i, r) == (0, 0) else (0, width)
-                for lo, hi in zip(cuts[:-1], cuts[1:]):
-                    nc.vector.tensor_tensor(
-                        gathered[:, r * width + lo : r * width + hi],
-                        planes[a, r][:].indirect(entries(offs_t, e0 * C + lo, e0 * C + hi)),
-                        gate_t[:, e0 * C + lo : e0 * C + hi],
-                        MULT,
-                    )
-            if i == last - 3:
-                rounded[i] = ring.tile([P, PACK * width], BF16, name="held", align_bytes=64)
-            else:
-                rounded[i] = ring.tile([P, PACK * width], BF16, name="rounded", bufs=3, align_bytes=64)
-            copy = nc.vector.tensor_copy if i == last else nc.scalar.copy
+            for lo, hi in zip(cuts[:-1], cuts[1:]):
+                nc.vector.tensor_tensor(
+                    gathered[:, r * width + lo : r * width + hi],
+                    window[:].indirect(entries(offs_t, e0 * C + lo, e0 * C + hi)),
+                    gate_t[:, e0 * C + lo : e0 * C + hi],
+                    MULT,
+                )
+
+        def round_and_interleave(copy, rounded, gathered, first, count):
             copy(
-                rounded[i][:].rearrange("p (c i r) -> p c r i", r=PACK, i=4),
-                gathered[:].rearrange("p (r c i) -> p c r i", r=PACK, i=4),
+                rounded.rearrange("p (c i r) -> p c r i", r=PACK, i=4),
+                gathered[:].rearrange("p (r c i) -> p c r i", r=PACK, i=4)[:, first * C // 4 : (first + count) * C // 4],
             )
 
-        def quantise_and_multiply(i):
-            e0, experts, a = pieces[i]
-            piece_codes = ring.tile([P, experts * C], U32, name="codes", bufs=5, align_bytes=64)
-            piece_scales = ring.tile([P, experts * C], U8, name="scales", bufs=5, align_bytes=64)
-            nc.vector.quantize_mx(piece_codes[:].bitcast(FP8X4), piece_scales[:], rounded[i][:])
-            for j in range(experts):
-                codes[e0 + j, a] = piece_codes[:, j * C : (j + 1) * C]
-                scales[e0 + j, a] = piece_scales[:, j * C : (j + 1) * C]
-            if a == PASSES - 1:
-                for e in range(e0, e0 + experts):
-                    acc = psum.tile([P, C], F32, name="acc", bufs=8)
-                    for k_pass in range(PASSES):
-                        col = (e % GROUP * PASSES + k_pass) * N
-                        nc.tensor.matmul_mx(
-                            acc[:],
-                            lhsT=w_tiles[e // GROUP][:, col : col + N].bitcast(FP8X4),
-                            lhsT_scale=w_scale[:, (e * PASSES + k_pass) * N : (e * PASSES + k_pass + 1) * N],
-                            rhs=codes[e, k_pass].bitcast(FP8X4),
-                            rhs_scale=scales[e, k_pass],
-                            start=(k_pass == 0),
-                            stop=(k_pass == PASSES - 1),
-                        )
-                    nc.scalar.activation(y[:, e * C : (e + 1) * C], acc[:], RELU, bias=bias[:, e : e + 1])
+        def quantise(words, scale_bytes, rounded, e0, count, a):
+            nc.vector.quantize_mx(words[:].bitcast(FP8X4), scale_bytes[:], rounded)
+            for j in range(count):
+                codes[e0 + j, a] = words[:, j * C : (j + 1) * C]
+                scales[e0 + j, a] = scale_bytes[:, j * C : (j + 1) * C]
 
-        for i in range(len(pieces)):
-            gather_and_round(i)
+        for a in range(PASSES - 1):
+            gathered = placed("gathered%d" % a, PACK * S, F32, (g0_at, g1_at)[a])
+            for r in range(PACK):
+                n = PACK * a + r
+                cuts = HEAD_CUTS if n == 0 else ((0, CHUNK * C, S) if n == 2 * PACK - 1 else (0, S))
+                gather(gathered, wide[n % 3], r, 0, E, cuts)
+                if n + 3 < 2 * PACK:
+                    load_plane(wide[n % 3], (n + 3) // PACK, (n + 3) % PACK)
+                elif n + 1 < 2 * PACK:
+                    load_plane(wide[n % 3], PASSES - 1, (0, 3)[n + 3 - 2 * PACK])
+            for e0 in range(0, E, CHUNK):
+                rounded = ring.tile([P, PACK * CHUNK * C], BF16, name="rounded", bufs=2, align_bytes=64)
+                round_and_interleave(nc.scalar.copy, rounded[:], gathered, e0, CHUNK)
+                words = keep.tile([P, CHUNK * C], U32, name="words%d_%d" % (a, e0), align_bytes=64)
+                scale_bytes = keep.tile([P, CHUNK * C], U8, name="bytes%d_%d" % (a, e0), align_bytes=64)
+                quantise(words, scale_bytes, rounded[:], e0, CHUNK, a)
+            if a == 0:
+                w_tiles = []
+                for gi in range(E // CHUNK):
+                    wt = placed("w%d" % gi, CHUNK * PASSES * N, U32, 4 * gi * CHUNK * PASSES * N)
+                    nc.sync.dma_start(
+                        wt[:].bitcast(I32).rearrange("p (g n) -> p g n", n=N),
+                        words_src[:, gi * CHUNK * PASSES : (gi + 1) * CHUNK * PASSES, :],
+                    )
+                    w_tiles.append(wt)
+
+        y = placed("y", S, F32, y_at)
+
+        def multiply(e0, experts):
+            for e in range(e0, e0 + experts):
+                acc = psum.tile([P, C], F32, name="acc", bufs=8)
+                for k_pass in range(PASSES):
+                    col = (e % CHUNK * PASSES + k_pass) * N
+                    nc.tensor.matmul_mx(
+                        acc[:],
+                        lhsT=w_tiles[e // CHUNK][:, col : col + N].bitcast(FP8X4),
+                        lhsT_scale=w_scale[:, (e * PASSES + k_pass) * N : (e * PASSES + k_pass + 1) * N],
+                        rhs=codes[e, k_pass].bitcast(FP8X4),
+                        rhs_scale=scales[e, k_pass],
+                        start=(k_pass == 0),
+                        stop=(k_pass == PASSES - 1),
+                    )
+                nc.scalar.activation(y[:, e * C : (e + 1) * C], acc[:], RELU, bias=bias[:, e : e + 1])
+
+        last_windows = (wide[2], narrow[0], narrow[1], wide[0])
+        last = len(TAPER) - 1
+        for i, (e0, experts) in enumerate(TAPER):
+            gathered = placed("piece%d" % i, PACK * experts * C, F32, gathered_at[i])
+            for r in range(PACK):
+                cuts = (0, CHUNK * C, experts * C) if (experts > CHUNK and r == PACK - 1) else (0, experts * C)
+                gather(gathered, last_windows[r], r, e0, experts, cuts)
+            runs = powers_of_two(experts)
+            tiles = []
+            if i == 0:
+                for first, count in runs:
+                    rounded = placed("rounded0_%d" % first, PACK * count * C, BF16, rounded_at[i] + 2 * PACK * first * C)
+                    round_and_interleave(nc.scalar.copy, rounded[:], gathered, first, count)
+                    tiles.append(rounded[:])
+            else:
+                rounded = placed("rounded%d" % i, PACK * experts * C, BF16, rounded_at[i])
+                round_and_interleave(nc.vector.tensor_copy if i == last else nc.scalar.copy, rounded[:], gathered, 0, experts)
+                tiles = [rounded[:, PACK * first * C : PACK * (first + count) * C] for first, count in runs]
+            for (first, count), piece in zip(runs, tiles):
+                e = e0 + first
+                at = codes_at + 5 * C * e if i < 2 else late_codes_at + 5 * C * (e - TAPER[2][0])
+                words = placed("words2_%d" % e, count * C, U32, at)
+                scale_bytes = placed("bytes2_%d" % e, count * C, U8, at + 4 * count * C)
+                quantise(words, scale_bytes, piece, e, count, PASSES - 1)
             if i > 0:
-                quantise_and_multiply(i - 1)
-        quantise_and_multiply(last)
+                multiply(*TAPER[i - 1])
+        multiply(*TAPER[last])
 
-        sums = ring.tile([P, 3 * T], F32, name="gathered", bufs=3)
+        sums = placed("sums", 3 * T, F32, sums_at)
         for lo, hi in TOKEN_HALVES:
             nc.vector.tensor_copy(sums[:, lo:hi], y[:].indirect(entries(pos_t[0], lo, hi)))
         for lo, hi in TOKEN_HALVES:

@@ -11,9 +11,9 @@ PASSES = K // K_PASS
 PER_COLUMN = 16
 CHUNK = 8
 WIDE = S + 8
-TAPER = ((0, 12), (12, 6), (18, 3), (21, 2), (23, 1))
+TAPER = ((0, 8), (8, 6), (14, 4), (18, 3), (21, 2), (23, 1))
 NARROW = TAPER[0][1] * C + 8
-HEAD_CUTS = (0, 256, 768, 1792, S)
+HEAD_CUTS = (0, 128, 512, 1280, S)
 TOKEN_HALVES = ((0, T // 2), (T // 2, T))
 STORE_CUTS = ((0, T // 2), (T // 2, T - 128), (T - 128, T))
 
@@ -36,13 +36,9 @@ def entries(list_tile, lo, hi):
     return list_tile[:, lo // PER_COLUMN : hi // PER_COLUMN]
 
 
-def powers_of_two(experts):
-    runs, first = [], 0
-    while first < experts:
-        count = max(c for c in (CHUNK, 4, 2, 1) if c <= experts - first)
-        runs.append((first, count))
-        first = first + count
-    return runs
+def two_runs(experts):
+    count = max(c for c in (4, 2, 1) if c < experts)
+    return ((0, count), (count, experts - count))
 
 
 def tile_moe_pre_lin_relu_kernel(tc, xT, w_words, w_scales, b, gate, offs, pos1, pos2, pos3, out):
@@ -56,22 +52,17 @@ def tile_moe_pre_lin_relu_kernel(tc, xT, w_words, w_scales, b, gate, offs, pos1,
         def placed(name, columns, dtype, offset):
             return stage.tile([P, columns], dtype, name=name, offset=offset, align_bytes=64)
 
-        full = 4 * PACK * S
         g0_at = 0
         ga_at = 4 * E * PASSES * N
-        y_at = ga_at + 4 * PACK * 12 * C
+        y_at = ga_at + 4 * PACK * TAPER[0][1] * C
         g1_at = y_at + 4 * S
-        gb_at = g1_at
-        ra_at = gb_at + 4 * PACK * 6 * C
-        rb_at = ra_at + 2 * PACK * 12 * C
-        codes_at = rb_at + 2 * PACK * 6 * C
+        codes_at = g1_at + 4 * PACK * TAPER[1][1] * C
+        rounded_at = [codes_at + 5 * S]
+        for piece in range(3):
+            rounded_at.append(rounded_at[-1] + 2 * PACK * TAPER[piece][1] * C)
         sums_at = ga_at
-        rc_at = sums_at + 4 * 3 * T
-        rd_at = rc_at + 2 * PACK * 3 * C
-        re_at = rd_at + 2 * PACK * 2 * C
-        late_codes_at = re_at + 2 * PACK * C
-        gathered_at = (ga_at, gb_at, ra_at, rb_at, rc_at)
-        rounded_at = (ra_at, rb_at, rc_at, rd_at, re_at)
+        rounded_at.append(sums_at + 4 * 3 * T)
+        rounded_at.append(rounded_at[-1] + 2 * PACK * TAPER[4][1] * C)
 
         offs_t = keep.tile([P, S // PER_COLUMN], U16, name="offs_t")
         nc.sync.dma_start(offs_t[:], offs)
@@ -87,9 +78,10 @@ def tile_moe_pre_lin_relu_kernel(tc, xT, w_words, w_scales, b, gate, offs, pos1,
             nc.sync.dma_start(gate_t[:, lo:hi], gate[0:P, lo:hi])
         load_plane(wide[1], 0, 1)
         load_plane(wide[2], 0, 2)
-        narrow = [keep.tile([P, NARROW], F32, name="narrow%d" % i) for i in range(2)]
-        for i in range(2):
-            load_plane(narrow[i], PASSES - 1, 1 + i)
+        narrow = [keep.tile([P, NARROW], F32, name="narrow%d" % i) for i in range(PACK - 1)]
+        for r in range(PACK - 1):
+            load_plane(narrow[r], PASSES - 1, r)
+        narrow.append(wide[2])
 
         w_scale = keep.tile([P, E * PASSES * N], U8, name="w_scale", align_bytes=64)
         nc.vector.memset(w_scale[:].bitcast(I32), 0)
@@ -139,10 +131,10 @@ def tile_moe_pre_lin_relu_kernel(tc, xT, w_words, w_scales, b, gate, offs, pos1,
                 gather(gathered, wide[n % 3], r, 0, E, cuts)
                 if n + 3 < 2 * PACK:
                     load_plane(wide[n % 3], (n + 3) // PACK, (n + 3) % PACK)
-                elif n + 1 < 2 * PACK:
-                    load_plane(wide[n % 3], PASSES - 1, (0, 3)[n + 3 - 2 * PACK])
+                elif n + 3 == 2 * PACK:
+                    load_plane(wide[n % 3], PASSES - 1, PACK - 1)
             for e0 in range(0, E, CHUNK):
-                rounded = ring.tile([P, PACK * CHUNK * C], BF16, name="rounded", bufs=2, align_bytes=64)
+                rounded = ring.tile([P, PACK * CHUNK * C], BF16, name="rounded", bufs=3, align_bytes=64)
                 round_and_interleave(nc.scalar.copy, rounded[:], gathered, e0, CHUNK)
                 words = keep.tile([P, CHUNK * C], U32, name="words%d_%d" % (a, e0), align_bytes=64)
                 scale_bytes = keep.tile([P, CHUNK * C], U8, name="bytes%d_%d" % (a, e0), align_bytes=64)
@@ -175,27 +167,23 @@ def tile_moe_pre_lin_relu_kernel(tc, xT, w_words, w_scales, b, gate, offs, pos1,
                     )
                 nc.scalar.activation(y[:, e * C : (e + 1) * C], acc[:], RELU, bias=bias[:, e : e + 1])
 
-        last_windows = (wide[2], narrow[0], narrow[1], wide[0])
         last = len(TAPER) - 1
+        rounded_tiles = []
         for i, (e0, experts) in enumerate(TAPER):
-            gathered = placed("piece%d" % i, PACK * experts * C, F32, gathered_at[i])
-            for r in range(PACK):
-                cuts = (0, CHUNK * C, experts * C) if (experts > CHUNK and r == PACK - 1) else (0, experts * C)
-                gather(gathered, last_windows[r], r, e0, experts, cuts)
-            runs = powers_of_two(experts)
-            tiles = []
-            if i == 0:
-                for first, count in runs:
-                    rounded = placed("rounded0_%d" % first, PACK * count * C, BF16, rounded_at[i] + 2 * PACK * first * C)
-                    round_and_interleave(nc.scalar.copy, rounded[:], gathered, first, count)
-                    tiles.append(rounded[:])
+            if i < 2:
+                gathered = placed("piece%d" % i, PACK * experts * C, F32, (ga_at, g1_at)[i])
             else:
-                rounded = placed("rounded%d" % i, PACK * experts * C, BF16, rounded_at[i])
-                round_and_interleave(nc.vector.tensor_copy if i == last else nc.scalar.copy, rounded[:], gathered, 0, experts)
-                tiles = [rounded[:, PACK * first * C : PACK * (first + count) * C] for first, count in runs]
+                gathered = rounded_tiles[i - 2][:].bitcast(F32)[:, 0 : PACK * experts * C]
+            for r in range(PACK):
+                gather(gathered, narrow[r], r, e0, experts, (0, experts * C))
+            runs = two_runs(experts) if i < last - 1 else ((0, experts),)
+            rounded = placed("rounded%d" % i, PACK * experts * C, BF16, rounded_at[i])
+            rounded_tiles.append(rounded)
+            round_and_interleave(nc.vector.tensor_copy if i == last else nc.scalar.copy, rounded[:], gathered, 0, experts)
+            tiles = [rounded[:, PACK * first * C : PACK * (first + count) * C] for first, count in runs]
             for (first, count), piece in zip(runs, tiles):
                 e = e0 + first
-                at = codes_at + 5 * C * e if i < 2 else late_codes_at + 5 * C * (e - TAPER[2][0])
+                at = codes_at + 5 * C * e
                 words = placed("words2_%d" % e, count * C, U32, at)
                 scale_bytes = placed("bytes2_%d" % e, count * C, U8, at + 4 * count * C)
                 quantise(words, scale_bytes, piece, e, count, PASSES - 1)

@@ -13,9 +13,9 @@ CHUNK = 8
 WIDE = S + 8
 TAPER = ((0, 8), (8, 6), (14, 4), (18, 3), (21, 2), (23, 1))
 NARROW = TAPER[0][1] * C + 8
-HEAD_CUTS = (0, 128, 512, 1280, S)
-TOKEN_HALVES = ((0, T // 2), (T // 2, T))
-STORE_CUTS = ((0, T // 2), (T // 2, T - 128), (T - 128, T))
+HEAD_CUTS = (0, 128, 384, 896, 1920, S)
+TOKEN_HALVES = ((0, 640), (640, T))
+STORE_CUTS = ((0, 640), (640, T - 128), (T - 128, T))
 
 FLOPS = 2 * K * S * N
 BYTES = 4 * K * T + E * K * N + E * K * N // 32 + 4 * N * E + 4 * S + 2 * P * (S + 3 * T) // PER_COLUMN + 4 * N * T
@@ -65,7 +65,6 @@ def tile_moe_pre_lin_relu_kernel(tc, xT, w_words, w_scales, b, gate, offs, pos1,
         rounded_at.append(rounded_at[-1] + 2 * PACK * TAPER[4][1] * C)
 
         offs_t = keep.tile([P, S // PER_COLUMN], U16, name="offs_t")
-        nc.sync.dma_start(offs_t[:], offs)
 
         gate_t = keep.tile([P, S], F32, name="gate_t")
         wide = [keep.tile([P, WIDE], F32, name="wide%d" % i) for i in range(3)]
@@ -74,6 +73,7 @@ def tile_moe_pre_lin_relu_kernel(tc, xT, w_words, w_scales, b, gate, offs, pos1,
             nc.sync.dma_start(window[:, 0:T], xT[K_PASS * a + r : K_PASS * (a + 1) : PACK, :])
 
         load_plane(wide[0], 0, 0)
+        nc.sync.dma_start(offs_t[:], offs)
         for lo, hi in zip(HEAD_CUTS[:-1], HEAD_CUTS[1:]):
             nc.sync.dma_start(gate_t[:, lo:hi], gate[0:P, lo:hi])
         load_plane(wide[1], 0, 1)
@@ -169,6 +169,13 @@ def tile_moe_pre_lin_relu_kernel(tc, xT, w_words, w_scales, b, gate, offs, pos1,
 
         last = len(TAPER) - 1
         rounded_tiles = []
+
+        def quantise_run(i, first, count):
+            e = TAPER[i][0] + first
+            words = placed("words2_%d" % e, count * C, U32, codes_at + 5 * C * e)
+            scale_bytes = placed("bytes2_%d" % e, count * C, U8, codes_at + 5 * C * e + 4 * count * C)
+            quantise(words, scale_bytes, rounded_tiles[i][:, PACK * first * C : PACK * (first + count) * C], e, count, PASSES - 1)
+
         for i, (e0, experts) in enumerate(TAPER):
             if i < 2:
                 gathered = placed("piece%d" % i, PACK * experts * C, F32, (ga_at, g1_at)[i])
@@ -176,19 +183,21 @@ def tile_moe_pre_lin_relu_kernel(tc, xT, w_words, w_scales, b, gate, offs, pos1,
                 gathered = rounded_tiles[i - 2][:].bitcast(F32)[:, 0 : PACK * experts * C]
             for r in range(PACK):
                 gather(gathered, narrow[r], r, e0, experts, (0, experts * C))
-            runs = two_runs(experts) if i < last - 1 else ((0, experts),)
             rounded = placed("rounded%d" % i, PACK * experts * C, BF16, rounded_at[i])
             rounded_tiles.append(rounded)
-            round_and_interleave(nc.vector.tensor_copy if i == last else nc.scalar.copy, rounded[:], gathered, 0, experts)
-            tiles = [rounded[:, PACK * first * C : PACK * (first + count) * C] for first, count in runs]
-            for (first, count), piece in zip(runs, tiles):
-                e = e0 + first
-                at = codes_at + 5 * C * e
-                words = placed("words2_%d" % e, count * C, U32, at)
-                scale_bytes = placed("bytes2_%d" % e, count * C, U8, at + 4 * count * C)
-                quantise(words, scale_bytes, piece, e, count, PASSES - 1)
-            if i > 0:
+            if i < last:
+                round_and_interleave(nc.scalar.copy, rounded[:], gathered, 0, experts)
+            if i < last - 1:
+                for first, count in two_runs(experts):
+                    quantise_run(i, first, count)
+            if 0 < i < last:
                 multiply(*TAPER[i - 1])
+        before, behind = two_runs(TAPER[last - 1][1])
+        quantise_run(last - 1, *before)
+        round_and_interleave(nc.vector.tensor_copy, rounded[:], gathered, 0, experts)
+        quantise_run(last - 1, *behind)
+        quantise_run(last, 0, experts)
+        multiply(*TAPER[last - 1])
         multiply(*TAPER[last])
 
         sums = placed("sums", 3 * T, F32, sums_at)

@@ -8,14 +8,19 @@ P = 128
 PACK = 4
 K_PASS = P * PACK
 PASSES = K // K_PASS
+LAST_PASS = PASSES - 1
 PER_COLUMN = 16
+LINE = 4
 CHUNK = 8
+BANKS = 8
+PIECES = ((0, 12), (12, 6), (18, 3), (21, 2), (23, 1))
 WIDE = S + 8
-TAPER = ((0, 8), (8, 6), (14, 4), (18, 3), (21, 2), (23, 1))
-NARROW = TAPER[0][1] * C + 8
+NARROW = PIECES[0][1] * C + 8
+WIDE_WINDOWS = 3
+ROUNDED_BUFFERS = 3
 HEAD_CUTS = (0, 128, 384, 896, 1920, S)
-TOKEN_HALVES = ((0, 640), (640, T))
-STORE_CUTS = ((0, 640), (640, T - 128), (T - 128, T))
+TOKEN_PARTS = ((0, 640), (640, T))
+STORE_PARTS = ((0, 640), (640, T - 128), (T - 128, T))
 
 FLOPS = 2 * K * S * N
 BYTES = 4 * K * T + E * K * N + E * K * N // 32 + 4 * N * E + 4 * S + 2 * P * (S + 3 * T) // PER_COLUMN + 4 * N * T
@@ -37,8 +42,16 @@ def entries(list_tile, lo, hi):
 
 
 def two_runs(experts):
-    count = max(c for c in (4, 2, 1) if c < experts)
+    count = max(c for c in (8, 4, 2, 1) if c < experts)
     return ((0, count), (count, experts - count))
+
+
+def gathered_bytes(experts):
+    return 4 * PACK * experts * C
+
+
+def rounded_bytes(experts):
+    return 2 * PACK * experts * C
 
 
 def tile_moe_pre_lin_relu_kernel(tc, xT, w_words, w_scales, b, gate, offs, pos1, pos2, pos3, out):
@@ -52,22 +65,27 @@ def tile_moe_pre_lin_relu_kernel(tc, xT, w_words, w_scales, b, gate, offs, pos1,
         def placed(name, columns, dtype, offset):
             return stage.tile([P, columns], dtype, name=name, offset=offset, align_bytes=64)
 
-        g0_at = 0
-        ga_at = 4 * E * PASSES * N
-        y_at = ga_at + 4 * PACK * TAPER[0][1] * C
-        g1_at = y_at + 4 * S
-        codes_at = g1_at + 4 * PACK * TAPER[1][1] * C
+        pass0_at = 0
+        weights_at = pass0_at
+        piece0_at = weights_at + 4 * E * PASSES * N
+        y_at = piece0_at + gathered_bytes(PIECES[0][1])
+        pass1_at = y_at + 4 * WIDE + 32
+        piece1_at = pass1_at
+        codes_at = piece1_at + gathered_bytes(PIECES[1][1])
         rounded_at = [codes_at + 5 * S]
-        for piece in range(3):
-            rounded_at.append(rounded_at[-1] + 2 * PACK * TAPER[piece][1] * C)
-        sums_at = ga_at
+        for first_expert, experts in PIECES[: len(PIECES) - 3]:
+            rounded_at.append(rounded_at[-1] + rounded_bytes(experts))
+        sums_at = piece0_at
         rounded_at.append(sums_at + 4 * 3 * T)
-        rounded_at.append(rounded_at[-1] + 2 * PACK * TAPER[4][1] * C)
+        rounded_at.append(rounded_at[-1] + rounded_bytes(PIECES[-2][1]))
 
         offs_t = keep.tile([P, S // PER_COLUMN], U16, name="offs_t")
-
         gate_t = keep.tile([P, S], F32, name="gate_t")
-        wide = [keep.tile([P, WIDE], F32, name="wide%d" % i) for i in range(3)]
+        wide = [
+            keep.tile([P, WIDE], F32, name="wide0"),
+            placed("wide1", WIDE, F32, y_at),
+            keep.tile([P, WIDE], F32, name="wide2"),
+        ]
 
         def load_plane(window, a, r):
             nc.sync.dma_start(window[:, 0:T], xT[K_PASS * a + r : K_PASS * (a + 1) : PACK, :])
@@ -78,10 +96,10 @@ def tile_moe_pre_lin_relu_kernel(tc, xT, w_words, w_scales, b, gate, offs, pos1,
             nc.sync.dma_start(gate_t[:, lo:hi], gate[0:P, lo:hi])
         load_plane(wide[1], 0, 1)
         load_plane(wide[2], 0, 2)
-        narrow = [keep.tile([P, NARROW], F32, name="narrow%d" % i) for i in range(PACK - 1)]
+        last_windows = [keep.tile([P, NARROW], F32, name="narrow%d" % r) for r in range(PACK - 1)]
         for r in range(PACK - 1):
-            load_plane(narrow[r], PASSES - 1, r)
-        narrow.append(wide[2])
+            load_plane(last_windows[r], LAST_PASS, r)
+        last_windows.append(wide[2])
 
         w_scale = keep.tile([P, E * PASSES * N], U8, name="w_scale", align_bytes=64)
         nc.vector.memset(w_scale[:].bitcast(I32), 0)
@@ -94,9 +112,9 @@ def tile_moe_pre_lin_relu_kernel(tc, xT, w_words, w_scales, b, gate, offs, pos1,
         nc.sync.dma_start(bias[:], b)
         pos_t = []
         for choice, pos in enumerate((pos1, pos2, pos3)):
-            pt = keep.tile([P, T // PER_COLUMN], U16, name="pos%d" % choice)
-            nc.sync.dma_start(pt[:], pos)
-            pos_t.append(pt)
+            list_tile = keep.tile([P, T // PER_COLUMN], U16, name="pos%d" % choice)
+            nc.sync.dma_start(list_tile[:], pos)
+            pos_t.append(list_tile)
 
         codes = {}
         scales = {}
@@ -113,8 +131,8 @@ def tile_moe_pre_lin_relu_kernel(tc, xT, w_words, w_scales, b, gate, offs, pos1,
 
         def round_and_interleave(copy, rounded, gathered, first, count):
             copy(
-                rounded.rearrange("p (c i r) -> p c r i", r=PACK, i=4),
-                gathered[:].rearrange("p (r c i) -> p c r i", r=PACK, i=4)[:, first * C // 4 : (first + count) * C // 4],
+                rounded.rearrange("p (c i r) -> p c r i", r=PACK, i=LINE),
+                gathered[:].rearrange("p (r c i) -> p c r i", r=PACK, i=LINE)[:, first * C // LINE : (first + count) * C // LINE],
             )
 
         def quantise(words, scale_bytes, rounded, e0, count, a):
@@ -123,89 +141,99 @@ def tile_moe_pre_lin_relu_kernel(tc, xT, w_words, w_scales, b, gate, offs, pos1,
                 codes[e0 + j, a] = words[:, j * C : (j + 1) * C]
                 scales[e0 + j, a] = scale_bytes[:, j * C : (j + 1) * C]
 
-        for a in range(PASSES - 1):
-            gathered = placed("gathered%d" % a, PACK * S, F32, (g0_at, g1_at)[a])
+        whole_planes = LAST_PASS * PACK
+        w_tiles = []
+        for a in range(LAST_PASS):
+            gathered = placed("gathered%d" % a, PACK * S, F32, (pass0_at, pass1_at)[a])
             for r in range(PACK):
-                n = PACK * a + r
-                cuts = HEAD_CUTS if n == 0 else ((0, CHUNK * C, S) if n == 2 * PACK - 1 else (0, S))
-                gather(gathered, wide[n % 3], r, 0, E, cuts)
-                if n + 3 < 2 * PACK:
-                    load_plane(wide[n % 3], (n + 3) // PACK, (n + 3) % PACK)
-                elif n + 3 == 2 * PACK:
-                    load_plane(wide[n % 3], PASSES - 1, PACK - 1)
+                plane = PACK * a + r
+                window = wide[plane % WIDE_WINDOWS]
+                if plane == 0:
+                    cuts = HEAD_CUTS
+                elif plane == whole_planes - 1:
+                    cuts = (0, CHUNK * C, S)
+                else:
+                    cuts = (0, S)
+                gather(gathered, window, r, 0, E, cuts)
+                successor = plane + WIDE_WINDOWS
+                if successor < whole_planes:
+                    load_plane(window, successor // PACK, successor % PACK)
+                elif successor == whole_planes:
+                    load_plane(window, LAST_PASS, PACK - 1)
             for e0 in range(0, E, CHUNK):
-                rounded = ring.tile([P, PACK * CHUNK * C], BF16, name="rounded", bufs=3, align_bytes=64)
+                rounded = ring.tile([P, PACK * CHUNK * C], BF16, name="rounded", bufs=ROUNDED_BUFFERS, align_bytes=64)
                 round_and_interleave(nc.scalar.copy, rounded[:], gathered, e0, CHUNK)
                 words = keep.tile([P, CHUNK * C], U32, name="words%d_%d" % (a, e0), align_bytes=64)
                 scale_bytes = keep.tile([P, CHUNK * C], U8, name="bytes%d_%d" % (a, e0), align_bytes=64)
                 quantise(words, scale_bytes, rounded[:], e0, CHUNK, a)
             if a == 0:
-                w_tiles = []
-                for gi in range(E // CHUNK):
-                    wt = placed("w%d" % gi, CHUNK * PASSES * N, U32, 4 * gi * CHUNK * PASSES * N)
+                for group in range(E // CHUNK):
+                    columns = CHUNK * PASSES * N
+                    w_tile = placed("w%d" % group, columns, U32, weights_at + 4 * group * columns)
                     nc.sync.dma_start(
-                        wt[:].bitcast(I32).rearrange("p (g n) -> p g n", n=N),
-                        words_src[:, gi * CHUNK * PASSES : (gi + 1) * CHUNK * PASSES, :],
+                        w_tile[:].bitcast(I32).rearrange("p (g n) -> p g n", n=N),
+                        words_src[:, group * CHUNK * PASSES : (group + 1) * CHUNK * PASSES, :],
                     )
-                    w_tiles.append(wt)
+                    w_tiles.append(w_tile)
 
         y = placed("y", S, F32, y_at)
 
         def multiply(e0, experts):
             for e in range(e0, e0 + experts):
-                acc = psum.tile([P, C], F32, name="acc", bufs=8)
-                for k_pass in range(PASSES):
-                    col = (e % CHUNK * PASSES + k_pass) * N
+                acc = psum.tile([P, C], F32, name="acc", bufs=BANKS)
+                for a in range(PASSES):
+                    column = (e % CHUNK * PASSES + a) * N
                     nc.tensor.matmul_mx(
                         acc[:],
-                        lhsT=w_tiles[e // CHUNK][:, col : col + N].bitcast(FP8X4),
-                        lhsT_scale=w_scale[:, (e * PASSES + k_pass) * N : (e * PASSES + k_pass + 1) * N],
-                        rhs=codes[e, k_pass].bitcast(FP8X4),
-                        rhs_scale=scales[e, k_pass],
-                        start=(k_pass == 0),
-                        stop=(k_pass == PASSES - 1),
+                        lhsT=w_tiles[e // CHUNK][:, column : column + N].bitcast(FP8X4),
+                        lhsT_scale=w_scale[:, (e * PASSES + a) * N : (e * PASSES + a + 1) * N],
+                        rhs=codes[e, a].bitcast(FP8X4),
+                        rhs_scale=scales[e, a],
+                        start=(a == 0),
+                        stop=(a == LAST_PASS),
                     )
                 nc.scalar.activation(y[:, e * C : (e + 1) * C], acc[:], RELU, bias=bias[:, e : e + 1])
 
-        last = len(TAPER) - 1
+        last = len(PIECES) - 1
         rounded_tiles = []
 
-        def quantise_run(i, first, count):
-            e = TAPER[i][0] + first
+        def quantise_run(piece, first, count):
+            e = PIECES[piece][0] + first
             words = placed("words2_%d" % e, count * C, U32, codes_at + 5 * C * e)
             scale_bytes = placed("bytes2_%d" % e, count * C, U8, codes_at + 5 * C * e + 4 * count * C)
-            quantise(words, scale_bytes, rounded_tiles[i][:, PACK * first * C : PACK * (first + count) * C], e, count, PASSES - 1)
+            run = rounded_tiles[piece][:, PACK * first * C : PACK * (first + count) * C]
+            quantise(words, scale_bytes, run, e, count, LAST_PASS)
 
-        for i, (e0, experts) in enumerate(TAPER):
-            if i < 2:
-                gathered = placed("piece%d" % i, PACK * experts * C, F32, (ga_at, g1_at)[i])
+        for piece, (e0, experts) in enumerate(PIECES):
+            if piece < 2:
+                gathered = placed("piece%d" % piece, PACK * experts * C, F32, (piece0_at, piece1_at)[piece])
             else:
-                gathered = rounded_tiles[i - 2][:].bitcast(F32)[:, 0 : PACK * experts * C]
+                gathered = rounded_tiles[piece - 2][:].bitcast(F32)[:, 0 : PACK * experts * C]
             for r in range(PACK):
-                gather(gathered, narrow[r], r, e0, experts, (0, experts * C))
-            rounded = placed("rounded%d" % i, PACK * experts * C, BF16, rounded_at[i])
+                gather(gathered, last_windows[r], r, e0, experts, (0, experts * C))
+            rounded = placed("rounded%d" % piece, PACK * experts * C, BF16, rounded_at[piece])
             rounded_tiles.append(rounded)
-            if i < last:
+            if piece < last:
                 round_and_interleave(nc.scalar.copy, rounded[:], gathered, 0, experts)
-            if i < last - 1:
+            if piece < last - 1:
                 for first, count in two_runs(experts):
-                    quantise_run(i, first, count)
-            if 0 < i < last:
-                multiply(*TAPER[i - 1])
-        before, behind = two_runs(TAPER[last - 1][1])
+                    quantise_run(piece, first, count)
+            if 0 < piece < last:
+                multiply(*PIECES[piece - 1])
+        before, behind = two_runs(PIECES[last - 1][1])
         quantise_run(last - 1, *before)
-        round_and_interleave(nc.vector.tensor_copy, rounded[:], gathered, 0, experts)
+        round_and_interleave(nc.vector.tensor_copy, rounded[:], gathered, 0, PIECES[last][1])
         quantise_run(last - 1, *behind)
-        quantise_run(last, 0, experts)
-        multiply(*TAPER[last - 1])
-        multiply(*TAPER[last])
+        quantise_run(last, 0, PIECES[last][1])
+        multiply(*PIECES[last - 1])
+        multiply(*PIECES[last])
 
         sums = placed("sums", 3 * T, F32, sums_at)
-        for lo, hi in TOKEN_HALVES:
+        for lo, hi in TOKEN_PARTS:
             nc.vector.tensor_copy(sums[:, lo:hi], y[:].indirect(entries(pos_t[0], lo, hi)))
-        for lo, hi in TOKEN_HALVES:
+        for lo, hi in TOKEN_PARTS:
             nc.vector.tensor_tensor(sums[:, T + lo : T + hi], y[:].indirect(entries(pos_t[1], lo, hi)), sums[:, lo:hi], ADD)
-        for lo, hi in STORE_CUTS:
+        for lo, hi in STORE_PARTS:
             nc.vector.tensor_tensor(
                 sums[:, 2 * T + lo : 2 * T + hi], y[:].indirect(entries(pos_t[2], lo, hi)), sums[:, T + lo : T + hi], ADD
             )

@@ -13,14 +13,12 @@ PER_COLUMN = 16
 LINE = 4
 CHUNK = 8
 BANKS = 8
-PIECES = ((0, 12), (12, 6), (18, 3), (21, 2), (23, 1))
+PIECES = ((0, 14), (14, 6), (20, 3), (23, 1))
 WIDE = S + 8
 NARROW = PIECES[0][1] * C + 8
 WIDE_WINDOWS = 3
 ROUNDED_BUFFERS = 3
 HEAD_CUTS = (0, 128, 384, 896, 1920, S)
-TOKEN_PARTS = ((0, 640), (640, T))
-STORE_PARTS = ((0, 640), (640, T - 128), (T - 128, T))
 
 FLOPS = 2 * K * S * N
 BYTES = 4 * K * T + E * K * N + E * K * N // 32 + 4 * N * E + 4 * S + 2 * P * (S + 3 * T) // PER_COLUMN + 4 * N * T
@@ -41,9 +39,9 @@ def entries(list_tile, lo, hi):
     return list_tile[:, lo // PER_COLUMN : hi // PER_COLUMN]
 
 
-def two_runs(experts):
-    count = max(c for c in (8, 4, 2, 1) if c < experts)
-    return ((0, count), (count, experts - count))
+def runs(experts):
+    counts = [c for c in (8, 4, 2, 1) if experts & c]
+    return [(sum(counts[:j]), c) for j, c in enumerate(counts)]
 
 
 def gathered_bytes(experts):
@@ -77,7 +75,6 @@ def tile_moe_pre_lin_relu_kernel(tc, xT, w_words, w_scales, b, gate, offs, pos1,
             rounded_at.append(rounded_at[-1] + rounded_bytes(experts))
         sums_at = piece0_at
         rounded_at.append(sums_at + 4 * 3 * T)
-        rounded_at.append(rounded_at[-1] + rounded_bytes(PIECES[-2][1]))
 
         offs_t = keep.tile([P, S // PER_COLUMN], U16, name="offs_t")
         gate_t = keep.tile([P, S], F32, name="gate_t")
@@ -96,10 +93,10 @@ def tile_moe_pre_lin_relu_kernel(tc, xT, w_words, w_scales, b, gate, offs, pos1,
             nc.sync.dma_start(gate_t[:, lo:hi], gate[0:P, lo:hi])
         load_plane(wide[1], 0, 1)
         load_plane(wide[2], 0, 2)
-        last_windows = [keep.tile([P, NARROW], F32, name="narrow%d" % r) for r in range(PACK - 1)]
-        for r in range(PACK - 1):
+        last_windows = [keep.tile([P, NARROW], F32, name="narrow%d" % r) for r in range(PACK - 2)]
+        for r in range(PACK - 2):
             load_plane(last_windows[r], LAST_PASS, r)
-        last_windows.append(wide[2])
+        last_windows.extend([wide[2], wide[0]])
 
         w_scale = keep.tile([P, E * PASSES * N], U8, name="w_scale", align_bytes=64)
         nc.vector.memset(w_scale[:].bitcast(I32), 0)
@@ -148,24 +145,21 @@ def tile_moe_pre_lin_relu_kernel(tc, xT, w_words, w_scales, b, gate, offs, pos1,
             for r in range(PACK):
                 plane = PACK * a + r
                 window = wide[plane % WIDE_WINDOWS]
-                if plane == 0:
-                    cuts = HEAD_CUTS
-                elif plane == whole_planes - 1:
-                    cuts = (0, CHUNK * C, S)
-                else:
-                    cuts = (0, S)
-                gather(gathered, window, r, 0, E, cuts)
+                gather(gathered, window, r, 0, E, HEAD_CUTS if plane == 0 else (0, S))
                 successor = plane + WIDE_WINDOWS
                 if successor < whole_planes:
                     load_plane(window, successor // PACK, successor % PACK)
-                elif successor == whole_planes:
-                    load_plane(window, LAST_PASS, PACK - 1)
+                elif successor < whole_planes + 2:
+                    load_plane(window, LAST_PASS, successor - whole_planes + 2)
             for e0 in range(0, E, CHUNK):
                 rounded = ring.tile([P, PACK * CHUNK * C], BF16, name="rounded", bufs=ROUNDED_BUFFERS, align_bytes=64)
                 round_and_interleave(nc.scalar.copy, rounded[:], gathered, e0, CHUNK)
                 words = keep.tile([P, CHUNK * C], U32, name="words%d_%d" % (a, e0), align_bytes=64)
                 scale_bytes = keep.tile([P, CHUNK * C], U8, name="bytes%d_%d" % (a, e0), align_bytes=64)
-                quantise(words, scale_bytes, rounded[:], e0, CHUNK, a)
+                if a == LAST_PASS - 1 and e0 + CHUNK == E:
+                    deferred = (words, scale_bytes, rounded[:], e0, CHUNK, a)
+                else:
+                    quantise(words, scale_bytes, rounded[:], e0, CHUNK, a)
             if a == 0:
                 for group in range(E // CHUNK):
                     columns = CHUNK * PASSES * N
@@ -208,33 +202,54 @@ def tile_moe_pre_lin_relu_kernel(tc, xT, w_words, w_scales, b, gate, offs, pos1,
             if piece < 2:
                 gathered = placed("piece%d" % piece, PACK * experts * C, F32, (piece0_at, piece1_at)[piece])
             else:
-                gathered = rounded_tiles[piece - 2][:].bitcast(F32)[:, 0 : PACK * experts * C]
+                skip = PACK * CHUNK * C // 2 if piece == 2 else 0
+                gathered = rounded_tiles[piece - 2][:].bitcast(F32)[:, skip : skip + PACK * experts * C]
             for r in range(PACK):
-                gather(gathered, last_windows[r], r, e0, experts, (0, experts * C))
-            rounded = placed("rounded%d" % piece, PACK * experts * C, BF16, rounded_at[piece])
-            rounded_tiles.append(rounded)
+                early = piece == 0 and r == PACK - 1
+                gather(gathered, last_windows[r], r, e0, experts, (0, CHUNK * C, experts * C) if early else (0, experts * C))
+            if piece == 1:
+                quantise(*deferred)
             if piece < last:
+                rounded = placed("rounded%d" % piece, PACK * experts * C, BF16, rounded_at[piece])
+            else:
+                rounded = rounded_tiles[piece - 3][:, PACK * CHUNK * C : PACK * (CHUNK + experts) * C]
+            rounded_tiles.append(rounded)
+            if piece == 0:
+                round_and_interleave(nc.scalar.copy, rounded[:, 0 : PACK * CHUNK * C], gathered, 0, CHUNK)
+                round_and_interleave(nc.scalar.copy, rounded[:, PACK * CHUNK * C : PACK * experts * C], gathered, CHUNK, experts - CHUNK)
+            elif piece < last:
                 round_and_interleave(nc.scalar.copy, rounded[:], gathered, 0, experts)
             if piece < last - 1:
-                for first, count in two_runs(experts):
+                for first, count in runs(experts):
                     quantise_run(piece, first, count)
             if 0 < piece < last:
                 multiply(*PIECES[piece - 1])
-        before, behind = two_runs(PIECES[last - 1][1])
+        before, behind = runs(PIECES[last - 1][1])
         quantise_run(last - 1, *before)
-        round_and_interleave(nc.vector.tensor_copy, rounded[:], gathered, 0, PIECES[last][1])
+        round_and_interleave(nc.vector.tensor_copy, rounded, gathered, 0, PIECES[last][1])
         quantise_run(last - 1, *behind)
         quantise_run(last, 0, PIECES[last][1])
         multiply(*PIECES[last - 1])
         multiply(*PIECES[last])
 
         sums = placed("sums", 3 * T, F32, sums_at)
-        for lo, hi in TOKEN_PARTS:
-            nc.vector.tensor_copy(sums[:, lo:hi], y[:].indirect(entries(pos_t[0], lo, hi)))
-        for lo, hi in TOKEN_PARTS:
-            nc.vector.tensor_tensor(sums[:, T + lo : T + hi], y[:].indirect(entries(pos_t[1], lo, hi)), sums[:, lo:hi], ADD)
-        for lo, hi in STORE_PARTS:
-            nc.vector.tensor_tensor(
-                sums[:, 2 * T + lo : 2 * T + hi], y[:].indirect(entries(pos_t[2], lo, hi)), sums[:, T + lo : T + hi], ADD
-            )
-            nc.sync.dma_start(out[:, lo:hi], sums[:, 2 * T + lo : 2 * T + hi])
+
+        def combine(choice, lo, hi):
+            fetched = y[:].indirect(entries(pos_t[choice], lo, hi))
+            total = sums[:, choice * T + lo : choice * T + hi]
+            if choice == 0:
+                nc.vector.tensor_copy(total, fetched)
+            else:
+                nc.vector.tensor_tensor(total, fetched, sums[:, (choice - 1) * T + lo : (choice - 1) * T + hi], ADD)
+            if choice == 2:
+                nc.sync.dma_start(out[:, lo:hi], total)
+
+        a, b2 = 640, T - 128
+        combine(0, 0, a)
+        combine(0, a, T)
+        combine(1, 0, a)
+        combine(1, a, b2)
+        combine(2, 0, a)
+        combine(1, b2, T)
+        combine(2, a, b2)
+        combine(2, b2, T)

@@ -9,15 +9,19 @@ PACK = 4
 K_PASS = P * PACK
 PASSES = K // K_PASS
 LAST_PASS = PASSES - 1
+PLANES = PASSES * PACK
 PER_COLUMN = 16
 LINE = 4
 CHUNK = 8
-BANKS = 8
-PIECES = ((0, 14), (14, 6), (20, 3), (23, 1))
+CHUNKS = E // CHUNK
+WIDTH = CHUNK * C
+BANK_GROUPS = ((0, 4), (4, 4), (8, 4), (12, 4), (16, 4), (20, 2), (22, 1), (23, 1))
+ON_VECTOR = (20, 21)
 WIDE = S + 8
-NARROW = PIECES[0][1] * C + 8
-WIDE_WINDOWS = 3
-ROUNDED_BUFFERS = 3
+FIRST = 14
+PIECES = ((0, FIRST), (FIRST, E - FIRST))
+WINDOWS = PACK
+REGION = 4 * WIDE + 32
 HEAD_CUTS = (0, 128, 384, 896, 1920, S)
 
 FLOPS = 2 * K * S * N
@@ -33,70 +37,50 @@ FP8X4 = mybir.dt.float8_e4m3fn_x4
 RELU = mybir.ActivationFunctionType.Relu
 ADD = mybir.AluOpType.add
 MULT = mybir.AluOpType.mult
+MAX = mybir.AluOpType.max
 
 
 def entries(list_tile, lo, hi):
     return list_tile[:, lo // PER_COLUMN : hi // PER_COLUMN]
 
 
-def runs(experts):
-    counts = [c for c in (8, 4, 2, 1) if experts & c]
-    return [(sum(counts[:j]), c) for j, c in enumerate(counts)]
-
-
-def gathered_bytes(experts):
-    return 4 * PACK * experts * C
-
-
-def rounded_bytes(experts):
-    return 2 * PACK * experts * C
-
-
 def tile_moe_pre_lin_relu_kernel(tc, xT, w_words, w_scales, b, gate, offs, pos1, pos2, pos3, out):
     nc = tc.nc
     with ExitStack() as ctx:
         keep = ctx.enter_context(tc.tile_pool(name="keep", bufs=1))
-        ring = ctx.enter_context(tc.tile_pool(name="ring", bufs=1))
         stage = ctx.enter_context(tc.tile_pool(name="stage", bufs=1))
         psum = ctx.enter_context(tc.psum_pool(name="psum", bufs=1))
 
         def placed(name, columns, dtype, offset):
             return stage.tile([P, columns], dtype, name=name, offset=offset, align_bytes=64)
 
-        pass0_at = 0
-        weights_at = pass0_at
-        piece0_at = weights_at + 4 * E * PASSES * N
-        y_at = piece0_at + gathered_bytes(PIECES[0][1])
-        pass1_at = y_at + 4 * WIDE + 32
-        piece1_at = pass1_at
-        codes_at = piece1_at + gathered_bytes(PIECES[1][1])
-        rounded_at = [codes_at + 5 * S]
-        for first_expert, experts in PIECES[: len(PIECES) - 3]:
-            rounded_at.append(rounded_at[-1] + rounded_bytes(experts))
-        sums_at = piece0_at
-        rounded_at.append(sums_at + 4 * 3 * T)
+        early_weights_at = WINDOWS * REGION
+        even_at = early_weights_at + 2 * 4 * CHUNK * PASSES * N
+        odd_at = even_at + 4 * PACK * S
+        rounded_at = (odd_at + 4 * PACK * S, odd_at + 6 * PACK * S, odd_at)
+        y_at = odd_at + 2 * PACK * S
+        weights_at = (early_weights_at, early_weights_at + 4 * CHUNK * PASSES * N, y_at + 4 * S)
+        pieces_at = (even_at, even_at + 4 * PACK * FIRST * C)
+        sums_at = pieces_at[1]
 
         offs_t = keep.tile([P, S // PER_COLUMN], U16, name="offs_t")
         gate_t = keep.tile([P, S], F32, name="gate_t")
-        wide = [
-            keep.tile([P, WIDE], F32, name="wide0"),
-            placed("wide1", WIDE, F32, y_at),
-            keep.tile([P, WIDE], F32, name="wide2"),
-        ]
 
-        def load_plane(window, a, r):
+        windows = {}
+        whole_planes = LAST_PASS * PACK
+
+        def load_plane(plane):
+            window = placed("window%d" % plane, WIDE, F32, plane % WINDOWS * REGION)
+            a, r = divmod(plane, PACK)
             nc.sync.dma_start(window[:, 0:T], xT[K_PASS * a + r : K_PASS * (a + 1) : PACK, :])
+            windows[plane] = window
 
-        load_plane(wide[0], 0, 0)
+        load_plane(0)
         nc.sync.dma_start(offs_t[:], offs)
         for lo, hi in zip(HEAD_CUTS[:-1], HEAD_CUTS[1:]):
             nc.sync.dma_start(gate_t[:, lo:hi], gate[0:P, lo:hi])
-        load_plane(wide[1], 0, 1)
-        load_plane(wide[2], 0, 2)
-        last_windows = [keep.tile([P, NARROW], F32, name="narrow%d" % r) for r in range(PACK - 2)]
-        for r in range(PACK - 2):
-            load_plane(last_windows[r], LAST_PASS, r)
-        last_windows.extend([wide[2], wide[0]])
+        for plane in range(1, WINDOWS):
+            load_plane(plane)
 
         w_scale = keep.tile([P, E * PASSES * N], U8, name="w_scale", align_bytes=64)
         nc.vector.memset(w_scale[:].bitcast(I32), 0)
@@ -113,124 +97,107 @@ def tile_moe_pre_lin_relu_kernel(tc, xT, w_words, w_scales, b, gate, offs, pos1,
             nc.sync.dma_start(list_tile[:], pos)
             pos_t.append(list_tile)
 
-        codes = {}
-        scales = {}
-
-        def gather(gathered, window, r, e0, experts, cuts):
+        def gather(gathered, plane, e0, experts, cuts):
             width = experts * C
+            r = plane % PACK
             for lo, hi in zip(cuts[:-1], cuts[1:]):
                 nc.vector.tensor_tensor(
                     gathered[:, r * width + lo : r * width + hi],
-                    window[:].indirect(entries(offs_t, e0 * C + lo, e0 * C + hi)),
+                    windows[plane][:].indirect(entries(offs_t, e0 * C + lo, e0 * C + hi)),
                     gate_t[:, e0 * C + lo : e0 * C + hi],
                     MULT,
                 )
 
-        def round_and_interleave(copy, rounded, gathered, first, count):
-            copy(
-                rounded.rearrange("p (c i r) -> p c r i", r=PACK, i=LINE),
-                gathered[:].rearrange("p (r c i) -> p c r i", r=PACK, i=LINE)[:, first * C // LINE : (first + count) * C // LINE],
-            )
+        rounded = {}
 
-        def quantise(words, scale_bytes, rounded, e0, count, a):
-            nc.vector.quantize_mx(words[:].bitcast(FP8X4), scale_bytes[:], rounded)
-            for j in range(count):
-                codes[e0 + j, a] = words[:, j * C : (j + 1) * C]
-                scales[e0 + j, a] = scale_bytes[:, j * C : (j + 1) * C]
-
-        whole_planes = LAST_PASS * PACK
-        w_tiles = []
-        for a in range(LAST_PASS):
-            gathered = placed("gathered%d" % a, PACK * S, F32, (pass0_at, pass1_at)[a])
-            for r in range(PACK):
-                plane = PACK * a + r
-                window = wide[plane % WIDE_WINDOWS]
-                gather(gathered, window, r, 0, E, HEAD_CUTS if plane == 0 else (0, S))
-                successor = plane + WIDE_WINDOWS
-                if successor < whole_planes:
-                    load_plane(window, successor // PACK, successor % PACK)
-                elif successor < whole_planes + 2:
-                    load_plane(window, LAST_PASS, successor - whole_planes + 2)
-            for e0 in range(0, E, CHUNK):
-                rounded = ring.tile([P, PACK * CHUNK * C], BF16, name="rounded", bufs=ROUNDED_BUFFERS, align_bytes=64)
-                round_and_interleave(nc.scalar.copy, rounded[:], gathered, e0, CHUNK)
-                words = keep.tile([P, CHUNK * C], U32, name="words%d_%d" % (a, e0), align_bytes=64)
-                scale_bytes = keep.tile([P, CHUNK * C], U8, name="bytes%d_%d" % (a, e0), align_bytes=64)
-                if a == LAST_PASS - 1 and e0 + CHUNK == E:
-                    deferred = (words, scale_bytes, rounded[:], e0, CHUNK, a)
-                else:
-                    quantise(words, scale_bytes, rounded[:], e0, CHUNK, a)
-            if a == 0:
-                for group in range(E // CHUNK):
-                    columns = CHUNK * PASSES * N
-                    w_tile = placed("w%d" % group, columns, U32, weights_at + 4 * group * columns)
-                    nc.sync.dma_start(
-                        w_tile[:].bitcast(I32).rearrange("p (g n) -> p g n", n=N),
-                        words_src[:, group * CHUNK * PASSES : (group + 1) * CHUNK * PASSES, :],
+        def round_and_interleave(a, gathered, e0, experts):
+            for chunk in range(CHUNKS):
+                lo, hi = max(e0, chunk * CHUNK), min(e0 + experts, (chunk + 1) * CHUNK)
+                if lo < hi:
+                    if (chunk, a) not in rounded:
+                        rounded[chunk, a] = placed("rounded%d_%d" % (chunk, a), PACK * WIDTH, BF16, rounded_at[a] + 2 * PACK * WIDTH * chunk)
+                    first = chunk * CHUNK
+                    nc.scalar.copy(
+                        rounded[chunk, a][:, PACK * (lo - first) * C : PACK * (hi - first) * C].rearrange("p (c i r) -> p c r i", r=PACK, i=LINE),
+                        gathered[:].rearrange("p (r c i) -> p c r i", r=PACK, i=LINE)[:, (lo - e0) * C // LINE : (hi - e0) * C // LINE],
                     )
-                    w_tiles.append(w_tile)
+
+        w_tiles = []
+
+        def load_weights(chunk):
+            w_tile = placed("w%d" % chunk, CHUNK * PASSES * N, U32, weights_at[chunk])
+            nc.sync.dma_start(
+                w_tile[:].bitcast(I32).rearrange("p (g n) -> p g n", n=N),
+                words_src[:, chunk * CHUNK * PASSES : (chunk + 1) * CHUNK * PASSES, :],
+            )
+            w_tiles.append(w_tile)
+
+        load_weights(0)
+        load_weights(1)
+        for a in range(LAST_PASS):
+            gathered = placed("gathered%d" % a, PACK * S, F32, (even_at, odd_at)[a])
+            for plane in range(PACK * a, PACK * (a + 1)):
+                gather(gathered, plane, 0, E, HEAD_CUTS if plane == 0 else (0, S))
+                load_plane(plane + WINDOWS)
+            round_and_interleave(a, gathered, 0, E)
+        load_weights(2)
+        pieces = []
+        for piece, (e0, experts) in enumerate(PIECES):
+            gathered = placed("piece%d" % piece, PACK * experts * C, F32, pieces_at[piece])
+            for plane in range(whole_planes, PLANES):
+                gather(gathered, plane, e0, experts, (0, experts * C))
+            pieces.append(gathered)
+        for piece, (e0, experts) in enumerate(PIECES):
+            round_and_interleave(LAST_PASS, pieces[piece], e0, experts)
 
         y = placed("y", S, F32, y_at)
+        banks = {}
+        for first, count in BANK_GROUPS:
+            bank = psum.tile([P, count * C], F32, name="bank%d" % first)
+            for e in range(first, first + count):
+                banks[e] = (bank[:, (e - first) * C : (e - first + 1) * C], e == first, e == first + count - 1)
 
-        def multiply(e0, experts):
-            for e in range(e0, e0 + experts):
-                acc = psum.tile([P, C], F32, name="acc", bufs=BANKS)
+        def quantise_and_multiply(a, e0, count):
+            chunk, first = divmod(e0, CHUNK)
+            if chunk == 0:
+                codes_at = pieces_at[0] + 5 * WIDTH * a
+            else:
+                codes_at = rounded_at[a] + 2 * PACK * WIDTH * (chunk - 1) + 5 * first * C
+            words = placed("words%d_%d" % (e0, a), count * C, U32, codes_at)
+            scale_bytes = placed("bytes%d_%d" % (e0, a), count * C, U8, codes_at + 4 * count * C)
+            nc.vector.quantize_mx(words[:].bitcast(FP8X4), scale_bytes[:], rounded[chunk, a][:, PACK * first * C : PACK * (first + count) * C])
+            for j in range(count):
+                e = e0 + j
+                acc, opens, closes = banks[e]
+                column = (e % CHUNK * PASSES + a) * N
+                nc.tensor.matmul_mx(
+                    acc,
+                    lhsT=w_tiles[chunk][:, column : column + N].bitcast(FP8X4),
+                    lhsT_scale=w_scale[:, (e * PASSES + a) * N : (e * PASSES + a + 1) * N],
+                    rhs=words[:, j * C : (j + 1) * C].bitcast(FP8X4),
+                    rhs_scale=scale_bytes[:, j * C : (j + 1) * C],
+                    start=(a == 0 and opens),
+                    stop=(a == LAST_PASS and closes),
+                )
+
+        for chunk in range(CHUNKS):
+            e0 = chunk * CHUNK
+            if chunk < CHUNKS - 1:
                 for a in range(PASSES):
-                    column = (e % CHUNK * PASSES + a) * N
-                    nc.tensor.matmul_mx(
-                        acc[:],
-                        lhsT=w_tiles[e // CHUNK][:, column : column + N].bitcast(FP8X4),
-                        lhsT_scale=w_scale[:, (e * PASSES + a) * N : (e * PASSES + a + 1) * N],
-                        rhs=codes[e, a].bitcast(FP8X4),
-                        rhs_scale=scales[e, a],
-                        start=(a == 0),
-                        stop=(a == LAST_PASS),
-                    )
-                nc.scalar.activation(y[:, e * C : (e + 1) * C], acc[:], RELU, bias=bias[:, e : e + 1])
-
-        last = len(PIECES) - 1
-        rounded_tiles = []
-
-        def quantise_run(piece, first, count):
-            e = PIECES[piece][0] + first
-            words = placed("words2_%d" % e, count * C, U32, codes_at + 5 * C * e)
-            scale_bytes = placed("bytes2_%d" % e, count * C, U8, codes_at + 5 * C * e + 4 * count * C)
-            run = rounded_tiles[piece][:, PACK * first * C : PACK * (first + count) * C]
-            quantise(words, scale_bytes, run, e, count, LAST_PASS)
-
-        for piece, (e0, experts) in enumerate(PIECES):
-            if piece < 2:
-                gathered = placed("piece%d" % piece, PACK * experts * C, F32, (piece0_at, piece1_at)[piece])
+                    quantise_and_multiply(a, e0, CHUNK)
             else:
-                skip = PACK * CHUNK * C // 2 if piece == 2 else 0
-                gathered = rounded_tiles[piece - 2][:].bitcast(F32)[:, skip : skip + PACK * experts * C]
-            for r in range(PACK):
-                early = piece == 0 and r == PACK - 1
-                gather(gathered, last_windows[r], r, e0, experts, (0, CHUNK * C, experts * C) if early else (0, experts * C))
-            if piece == 1:
-                quantise(*deferred)
-            if piece < last:
-                rounded = placed("rounded%d" % piece, PACK * experts * C, BF16, rounded_at[piece])
-            else:
-                rounded = rounded_tiles[piece - 3][:, PACK * CHUNK * C : PACK * (CHUNK + experts) * C]
-            rounded_tiles.append(rounded)
-            if piece == 0:
-                round_and_interleave(nc.scalar.copy, rounded[:, 0 : PACK * CHUNK * C], gathered, 0, CHUNK)
-                round_and_interleave(nc.scalar.copy, rounded[:, PACK * CHUNK * C : PACK * experts * C], gathered, CHUNK, experts - CHUNK)
-            elif piece < last:
-                round_and_interleave(nc.scalar.copy, rounded[:], gathered, 0, experts)
-            if piece < last - 1:
-                for first, count in runs(experts):
-                    quantise_run(piece, first, count)
-            if 0 < piece < last:
-                multiply(*PIECES[piece - 1])
-        before, behind = runs(PIECES[last - 1][1])
-        quantise_run(last - 1, *before)
-        round_and_interleave(nc.vector.tensor_copy, rounded, gathered, 0, PIECES[last][1])
-        quantise_run(last - 1, *behind)
-        quantise_run(last, 0, PIECES[last][1])
-        multiply(*PIECES[last - 1])
-        multiply(*PIECES[last])
+                half = CHUNK // 2
+                quantise_and_multiply(0, e0, CHUNK)
+                quantise_and_multiply(1, e0, half)
+                quantise_and_multiply(LAST_PASS, e0, half)
+                quantise_and_multiply(1, e0 + half, half)
+                for first, count in BANK_GROUPS[-3:]:
+                    quantise_and_multiply(LAST_PASS, first, count)
+            for e in range(e0, e0 + CHUNK):
+                if e in ON_VECTOR:
+                    nc.vector.tensor_scalar(y[:, e * C : (e + 1) * C], banks[e][0], bias[:, e : e + 1], 0.0, ADD, MAX)
+                else:
+                    nc.scalar.activation(y[:, e * C : (e + 1) * C], banks[e][0], RELU, bias=bias[:, e : e + 1])
 
         sums = placed("sums", 3 * T, F32, sums_at)
 

@@ -9,20 +9,13 @@ PACK = 4
 K_PASS = P * PACK
 PASSES = K // K_PASS
 LAST_PASS = PASSES - 1
-PLANES = PASSES * PACK
 PER_COLUMN = 16
-LINE = 4
-CHUNK = 8
-CHUNKS = E // CHUNK
-WIDTH = CHUNK * C
-BANK_GROUPS = ((0, 4), (4, 4), (8, 4), (12, 4), (16, 4), (20, 2), (22, 1), (23, 1))
-ON_VECTOR = (20, 21)
-WIDE = S + 8
-FIRST = 14
-PIECES = ((0, FIRST), (FIRST, E - FIRST))
-WINDOWS = PACK
-REGION = 4 * WIDE + 32
-HEAD_CUTS = (0, 128, 384, 896, 1920, S)
+RUN = 2
+HALF = E // 2
+OWN = 6
+PIECES = (((6, 12), (12, 18), (18, 24)), ((6, 12), (12, 18), (18, 24)), ((6, 12), (12, 19), (19, 24)))
+BANK_GROUPS = ((0, 4), (4, 8), (8, 12), (12, 16), (16, 19), (19, 22), (22, 23), (23, 24))
+HEAD_CUTS = (0, 256, OWN * C)
 
 FLOPS = 2 * K * S * N
 BYTES = 4 * K * T + E * K * N + E * K * N // 32 + 4 * N * E + 4 * S + 2 * P * (S + 3 * T) // PER_COLUMN + 4 * N * T
@@ -35,6 +28,7 @@ U16 = mybir.dt.uint16
 U8 = mybir.dt.uint8
 FP8X4 = mybir.dt.float8_e4m3fn_x4
 RELU = mybir.ActivationFunctionType.Relu
+COPY = mybir.ActivationFunctionType.Copy
 ADD = mybir.AluOpType.add
 MULT = mybir.AluOpType.mult
 MAX = mybir.AluOpType.max
@@ -48,47 +42,53 @@ def tile_moe_pre_lin_relu_kernel(tc, xT, w_words, w_scales, b, gate, offs, pos1,
     nc = tc.nc
     with ExitStack() as ctx:
         keep = ctx.enter_context(tc.tile_pool(name="keep", bufs=1))
-        stage = ctx.enter_context(tc.tile_pool(name="stage", bufs=1))
+        ring = ctx.enter_context(tc.tile_pool(name="ring", bufs=1))
         psum = ctx.enter_context(tc.psum_pool(name="psum", bufs=1))
-
-        def placed(name, columns, dtype, offset):
-            return stage.tile([P, columns], dtype, name=name, offset=offset, align_bytes=64)
-
-        early_weights_at = WINDOWS * REGION
-        even_at = early_weights_at + 2 * 4 * CHUNK * PASSES * N
-        odd_at = even_at + 4 * PACK * S
-        rounded_at = (odd_at + 4 * PACK * S, odd_at + 6 * PACK * S, odd_at)
-        y_at = odd_at + 2 * PACK * S
-        weights_at = (early_weights_at, early_weights_at + 4 * CHUNK * PASSES * N, y_at + 4 * S)
-        pieces_at = (even_at, even_at + 4 * PACK * FIRST * C)
-        sums_at = pieces_at[1]
 
         offs_t = keep.tile([P, S // PER_COLUMN], U16, name="offs_t")
         gate_t = keep.tile([P, S], F32, name="gate_t")
-
         windows = {}
-        whole_planes = LAST_PASS * PACK
 
-        def load_plane(plane):
-            window = placed("window%d" % plane, WIDE, F32, plane % WINDOWS * REGION)
-            a, r = divmod(plane, PACK)
-            nc.sync.dma_start(window[:, 0:T], xT[K_PASS * a + r : K_PASS * (a + 1) : PACK, :])
-            windows[plane] = window
+        def load_plane(a, r):
+            window = keep.tile([P, T], F32, name="window%d_%d" % (a, r))
+            nc.sync.dma_start(window[:], xT[K_PASS * a + r : K_PASS * (a + 1) : PACK, :])
+            windows[a, r] = window
 
-        load_plane(0)
+        def load_gate(lo, hi):
+            nc.sync.dma_start(gate_t[:, lo:hi], gate[0:P, lo:hi])
+
+        w_tiles = []
+
+        def load_weights(a):
+            w_tile = keep.tile([P, E * N], U32, name="w%d" % a, align_bytes=64)
+            nc.sync.dma_start(
+                w_tile[:].bitcast(I32).rearrange("p (e n) -> p e n", n=N),
+                w_words[:, a].rearrange("e p n r -> p e (n r)").bitcast(I32),
+            )
+            w_tiles.append(w_tile)
+
+        load_plane(0, 0)
         nc.sync.dma_start(offs_t[:], offs)
         for lo, hi in zip(HEAD_CUTS[:-1], HEAD_CUTS[1:]):
-            nc.sync.dma_start(gate_t[:, lo:hi], gate[0:P, lo:hi])
-        for plane in range(1, WINDOWS):
-            load_plane(plane)
+            load_gate(lo, hi)
+        for r in range(1, PACK):
+            load_plane(0, r)
+        load_gate(OWN * C, HALF * C)
+        for r in range(PACK):
+            load_plane(1, r)
 
         w_scale = keep.tile([P, E * PASSES * N], U8, name="w_scale", align_bytes=64)
         nc.vector.memset(w_scale[:].bitcast(I32), 0)
-        words_src = w_words.rearrange("e a p n r -> p (e a) (n r)").bitcast(I32)
         scale_src = w_scales.rearrange("e a q n -> q (e a) n").bitcast(I32)
         scale_dst = w_scale[:].bitcast(I32).rearrange("p (g n) -> p g n", n=N // 4)
         for quadrant in range(4):
             nc.sync.dma_start(scale_dst[32 * quadrant : 32 * quadrant + 4, :, :], scale_src[4 * quadrant : 4 * quadrant + 4, :, :])
+        load_weights(0)
+        load_gate(HALF * C, S)
+        load_weights(1)
+        for r in range(PACK):
+            load_plane(LAST_PASS, r)
+        load_weights(LAST_PASS)
         bias = keep.tile([P, E], F32, name="bias")
         nc.sync.dma_start(bias[:], b)
         pos_t = []
@@ -97,126 +97,135 @@ def tile_moe_pre_lin_relu_kernel(tc, xT, w_words, w_scales, b, gate, offs, pos1,
             nc.sync.dma_start(list_tile[:], pos)
             pos_t.append(list_tile)
 
-        def gather(gathered, plane, e0, experts, cuts):
-            width = experts * C
-            r = plane % PACK
-            for lo, hi in zip(cuts[:-1], cuts[1:]):
-                nc.vector.tensor_tensor(
-                    gathered[:, r * width + lo : r * width + hi],
-                    windows[plane][:].indirect(entries(offs_t, e0 * C + lo, e0 * C + hi)),
-                    gate_t[:, e0 * C + lo : e0 * C + hi],
-                    MULT,
-                )
+        y = keep.tile([P, S], F32, name="y")
+        banks = {}
+        for first, end in BANK_GROUPS:
+            bank = psum.tile([P, (end - first) * C], F32, name="bank%d" % first)
+            for e in range(first, end):
+                banks[e] = (bank[:, (e - first) * C : (e - first + 1) * C], e == first, e == end - 1)
 
         rounded = {}
 
-        def round_and_interleave(a, gathered, e0, experts):
-            for chunk in range(CHUNKS):
-                lo, hi = max(e0, chunk * CHUNK), min(e0 + experts, (chunk + 1) * CHUNK)
-                if lo < hi:
-                    if (chunk, a) not in rounded:
-                        rounded[chunk, a] = placed("rounded%d_%d" % (chunk, a), PACK * WIDTH, BF16, rounded_at[a] + 2 * PACK * WIDTH * chunk)
-                    first = chunk * CHUNK
-                    nc.scalar.copy(
-                        rounded[chunk, a][:, PACK * (lo - first) * C : PACK * (hi - first) * C].rearrange("p (c i r) -> p c r i", r=PACK, i=LINE),
-                        gathered[:].rearrange("p (r c i) -> p c r i", r=PACK, i=LINE)[:, (lo - e0) * C // LINE : (hi - e0) * C // LINE],
+        def rounded_view(a, e0, e1):
+            half = e0 // HALF
+            if (a, half) not in rounded:
+                rounded[a, half] = ring.tile([P, PACK * HALF * C], BF16, name="rounded%d_%d" % (a, half), tag="rounded", bufs=3, align_bytes=64)
+            return rounded[a, half][:, PACK * (e0 - half * HALF) * C : PACK * (e1 - half * HALF) * C]
+
+        own = {}
+
+        def gather_own(a):
+            own[a] = ring.tile([P, PACK * OWN * C], F32, name="own%d" % a, tag="own", bufs=1)
+            for r in range(PACK):
+                cuts = HEAD_CUTS if (a, r) == (0, 0) else (0, OWN * C)
+                for lo, hi in zip(cuts[:-1], cuts[1:]):
+                    nc.vector.tensor_tensor(
+                        own[a][:, r * OWN * C + lo : r * OWN * C + hi],
+                        windows[a, r][:].indirect(entries(offs_t, lo, hi)),
+                        gate_t[:, lo:hi],
+                        MULT,
                     )
 
-        w_tiles = []
-
-        def load_weights(chunk):
-            w_tile = placed("w%d" % chunk, CHUNK * PASSES * N, U32, weights_at[chunk])
-            nc.sync.dma_start(
-                w_tile[:].bitcast(I32).rearrange("p (g n) -> p g n", n=N),
-                words_src[:, chunk * CHUNK * PASSES : (chunk + 1) * CHUNK * PASSES, :],
+        def round_own(a):
+            nc.vector.tensor_copy(
+                rounded_view(a, 0, OWN).rearrange("p (c i r) -> p c r i", r=PACK, i=RUN),
+                own[a][:].rearrange("p (r c i) -> p c r i", r=PACK, i=RUN),
             )
-            w_tiles.append(w_tile)
 
-        load_weights(0)
-        load_weights(1)
-        for a in range(LAST_PASS):
-            gathered = placed("gathered%d" % a, PACK * S, F32, (even_at, odd_at)[a])
-            for plane in range(PACK * a, PACK * (a + 1)):
-                gather(gathered, plane, 0, E, HEAD_CUTS if plane == 0 else (0, S))
-                load_plane(plane + WINDOWS)
-            round_and_interleave(a, gathered, 0, E)
-        load_weights(2)
-        pieces = []
-        for piece, (e0, experts) in enumerate(PIECES):
-            gathered = placed("piece%d" % piece, PACK * experts * C, F32, pieces_at[piece])
-            for plane in range(whole_planes, PLANES):
-                gather(gathered, plane, e0, experts, (0, experts * C))
-            pieces.append(gathered)
-        for piece, (e0, experts) in enumerate(PIECES):
-            round_and_interleave(LAST_PASS, pieces[piece], e0, experts)
+        fetched = {}
 
-        y = placed("y", S, F32, y_at)
-        banks = {}
-        for first, count in BANK_GROUPS:
-            bank = psum.tile([P, count * C], F32, name="bank%d" % first)
-            for e in range(first, first + count):
-                banks[e] = (bank[:, (e - first) * C : (e - first + 1) * C], e == first, e == first + count - 1)
+        def gather_piece(a, piece):
+            e0, e1 = PIECES[a][piece]
+            width = (e1 - e0) * C
+            fetched[a, piece] = ring.tile([P, PACK * width], F32, name="fetched%d_%d" % (a, piece), tag="fetched", bufs=3)
+            for r in range(PACK):
+                nc.scalar.activation(
+                    fetched[a, piece][:, r * width : (r + 1) * width],
+                    windows[a, r][:].indirect(entries(offs_t, e0 * C, e1 * C)),
+                    COPY,
+                )
 
-        def quantise_and_multiply(a, e0, count):
-            chunk, first = divmod(e0, CHUNK)
-            if chunk == 0:
-                codes_at = pieces_at[0] + 5 * WIDTH * a
-            else:
-                codes_at = rounded_at[a] + 2 * PACK * WIDTH * (chunk - 1) + 5 * first * C
-            words = placed("words%d_%d" % (e0, a), count * C, U32, codes_at)
-            scale_bytes = placed("bytes%d_%d" % (e0, a), count * C, U8, codes_at + 4 * count * C)
-            nc.vector.quantize_mx(words[:].bitcast(FP8X4), scale_bytes[:], rounded[chunk, a][:, PACK * first * C : PACK * (first + count) * C])
-            for j in range(count):
-                e = e0 + j
+        def multiply(a, piece, e0, e1):
+            first = PIECES[a][piece][0]
+            runs = (e1 - e0) * C // RUN
+            nc.vector.tensor_tensor(
+                rounded_view(a, e0, e1).rearrange("p (c i r) -> p c r i", r=PACK, i=RUN),
+                fetched[a, piece][:].rearrange("p (r c i) -> p c r i", r=PACK, i=RUN)[:, (e0 - first) * C // RUN : (e1 - first) * C // RUN],
+                gate_t[:, e0 * C : e1 * C].rearrange("p (c i) -> p c i", i=RUN).unsqueeze(2).broadcast_to([P, runs, PACK, RUN]),
+                MULT,
+            )
+
+        def quantise(a, e0, e1):
+            count = e1 - e0
+            words = ring.tile([P, count * C], U32, name="words%d_%d" % (a, e0), tag="words", bufs=3, align_bytes=64)
+            scale_bytes = ring.tile([P, count * C], U8, name="bytes%d_%d" % (a, e0), tag="bytes", bufs=3, align_bytes=64)
+            nc.vector.quantize_mx(words[:].bitcast(FP8X4), scale_bytes[:], rounded_view(a, e0, e1))
+            for e in range(e0, e1):
                 acc, opens, closes = banks[e]
-                column = (e % CHUNK * PASSES + a) * N
                 nc.tensor.matmul_mx(
                     acc,
-                    lhsT=w_tiles[chunk][:, column : column + N].bitcast(FP8X4),
+                    lhsT=w_tiles[a][:, e * N : (e + 1) * N].bitcast(FP8X4),
                     lhsT_scale=w_scale[:, (e * PASSES + a) * N : (e * PASSES + a + 1) * N],
-                    rhs=words[:, j * C : (j + 1) * C].bitcast(FP8X4),
-                    rhs_scale=scale_bytes[:, j * C : (j + 1) * C],
+                    rhs=words[:, (e - e0) * C : (e - e0 + 1) * C].bitcast(FP8X4),
+                    rhs_scale=scale_bytes[:, (e - e0) * C : (e - e0 + 1) * C],
                     start=(a == 0 and opens),
                     stop=(a == LAST_PASS and closes),
                 )
 
-        for chunk in range(CHUNKS):
-            e0 = chunk * CHUNK
-            if chunk < CHUNKS - 1:
-                for a in range(PASSES):
-                    quantise_and_multiply(a, e0, CHUNK)
+        def finish(e, on_vector):
+            if on_vector:
+                nc.vector.tensor_scalar(y[:, e * C : (e + 1) * C], banks[e][0], bias[:, e : e + 1], 0.0, ADD, MAX)
             else:
-                half = CHUNK // 2
-                quantise_and_multiply(0, e0, CHUNK)
-                quantise_and_multiply(1, e0, half)
-                quantise_and_multiply(LAST_PASS, e0, half)
-                quantise_and_multiply(1, e0 + half, half)
-                for first, count in BANK_GROUPS[-3:]:
-                    quantise_and_multiply(LAST_PASS, first, count)
-            for e in range(e0, e0 + CHUNK):
-                if e in ON_VECTOR:
-                    nc.vector.tensor_scalar(y[:, e * C : (e + 1) * C], banks[e][0], bias[:, e : e + 1], 0.0, ADD, MAX)
-                else:
-                    nc.scalar.activation(y[:, e * C : (e + 1) * C], banks[e][0], RELU, bias=bias[:, e : e + 1])
+                nc.scalar.activation(y[:, e * C : (e + 1) * C], banks[e][0], RELU, bias=bias[:, e : e + 1])
 
-        sums = placed("sums", 3 * T, F32, sums_at)
+        gather_own(0)
+        for a in range(PASSES):
+            gather_piece(a, 0)
+            gather_piece(a, 1)
+            gather_piece(a, 2)
+            multiply(a, 0, *PIECES[a][0])
+            round_own(a)
+            if a > 0:
+                quantise(a - 1, 12, 20)
+                quantise(a - 1, 20, 24)
+            if a < LAST_PASS:
+                gather_own(a + 1)
+                quantise(a, 0, 8)
+                quantise(a, 8, 12)
+                multiply(a, 1, *PIECES[a][1])
+                multiply(a, 2, *PIECES[a][2])
+        a = LAST_PASS
+        quantise(a, 0, 8)
+        quantise(a, 8, 12)
+        multiply(a, 1, 12, 19)
+        multiply(a, 2, 19, 22)
+        quantise(a, 12, 16)
+        quantise(a, 16, 19)
+        multiply(a, 2, 22, 24)
+        quantise(a, 19, 22)
+        quantise(a, 22, 23)
+        quantise(a, 23, 24)
+        for e in range(E):
+            finish(e, e in (19, 20))
+
+        sums = ring.tile([P, 3 * T], F32, name="sums", tag="own", bufs=1)
 
         def combine(choice, lo, hi):
-            fetched = y[:].indirect(entries(pos_t[choice], lo, hi))
+            looked_up = y[:].indirect(entries(pos_t[choice], lo, hi))
             total = sums[:, choice * T + lo : choice * T + hi]
             if choice == 0:
-                nc.vector.tensor_copy(total, fetched)
+                nc.scalar.activation(total, looked_up, COPY)
             else:
-                nc.vector.tensor_tensor(total, fetched, sums[:, (choice - 1) * T + lo : (choice - 1) * T + hi], ADD)
+                nc.vector.tensor_tensor(total, looked_up, sums[:, (choice - 1) * T + lo : (choice - 1) * T + hi], ADD)
             if choice == 2:
                 nc.sync.dma_start(out[:, lo:hi], total)
 
-        a, b2 = 640, T - 128
-        combine(0, 0, a)
-        combine(0, a, T)
-        combine(1, 0, a)
-        combine(1, a, b2)
-        combine(2, 0, a)
-        combine(1, b2, T)
-        combine(2, a, b2)
-        combine(2, b2, T)
+        combine(0, 0, 128)
+        combine(0, 128, 384)
+        combine(0, 384, T)
+        combine(1, 0, 128)
+        combine(1, 128, 384)
+        combine(2, 0, 384)
+        combine(1, 384, T)
+        combine(2, 384, 896)
+        combine(2, 896, T)

@@ -1,6 +1,7 @@
 from contextlib import ExitStack
 
 import concourse.mybir as mybir
+from concourse.masks import make_identity
 
 K, T, E, C, N = 1536, 1024, 24, 128, 128
 S = E * C
@@ -11,11 +12,14 @@ PASSES = K // K_PASS
 LAST_PASS = PASSES - 1
 PER_COLUMN = 16
 RUN = 2
-HALF = E // 2
-OWN = 6
-PIECES = (((6, 12), (12, 18), (18, 24)), ((6, 12), (12, 18), (18, 24)), ((6, 12), (12, 19), (19, 24)))
-BANK_GROUPS = ((0, 4), (4, 8), (8, 12), (12, 16), (16, 19), (19, 22), (22, 23), (23, 24))
-HEAD_CUTS = (0, 256, OWN * C)
+GROUP = 8
+HALF = GROUP // 2
+WIDE = T + 8
+BANK = 2048
+BLOCK = 2 * PACK * GROUP * C
+OWN = 2 * GROUP
+SCALAR_PIECES = ((0, 0, 8), (1, 0, 8), (2, 0, 8), (0, 8, 16), (1, 8, 16), (2, 8, 12), (2, 12, 14), (2, 14, 16))
+BANK_GROUPS = ((16, 20, 4), (20, 24, 5), (0, 4, 6), (4, 8, 7), (8, 12, 0), (12, 16, 1))
 
 FLOPS = 2 * K * S * N
 BYTES = 4 * K * T + E * K * N + E * K * N // 32 + 4 * N * E + 4 * S + 2 * P * (S + 3 * T) // PER_COLUMN + 4 * N * T
@@ -42,40 +46,45 @@ def tile_moe_pre_lin_relu_kernel(tc, xT, w_words, w_scales, b, gate, offs, pos1,
     nc = tc.nc
     with ExitStack() as ctx:
         keep = ctx.enter_context(tc.tile_pool(name="keep", bufs=1))
-        ring = ctx.enter_context(tc.tile_pool(name="ring", bufs=1))
+        stage = ctx.enter_context(tc.tile_pool(name="stage", bufs=1))
         psum = ctx.enter_context(tc.psum_pool(name="psum", bufs=1))
 
+        def placed(name, columns, dtype, offset):
+            return stage.tile([P, columns], dtype, name=name, offset=offset, align_bytes=64)
+
+        pass_bytes = PACK * 4 * WIDE + 128
+        own_at = PASSES * pass_bytes
+        fetched_at = own_at + 5 * BLOCK
+        rounded_at = fetched_at + 6 * BLOCK
+
+        warm = keep.tile([P, 16], F32, name="warm")
+        nc.gpsimd.memset(warm[:, 0:8], 0.0)
+        nc.scalar.activation(warm[:, 8:9], warm[:, 0:1], RELU)
+
         offs_t = keep.tile([P, S // PER_COLUMN], U16, name="offs_t")
-        gate_t = keep.tile([P, S], F32, name="gate_t")
+        gate_first = keep.tile([P, GROUP * C], F32, name="gate_first")
+        gate_own = keep.tile([P, GROUP * C], F32, name="gate_own")
         windows = {}
 
         def load_plane(a, r):
-            window = keep.tile([P, T], F32, name="window%d_%d" % (a, r))
-            nc.sync.dma_start(window[:], xT[K_PASS * a + r : K_PASS * (a + 1) : PACK, :])
+            window = placed("window%d_%d" % (a, r), WIDE, F32, a * pass_bytes + r * (4 * WIDE + 32))
+            nc.sync.dma_start(window[:, 0:T], xT[K_PASS * a + r : K_PASS * (a + 1) : PACK, :])
             windows[a, r] = window
-
-        def load_gate(lo, hi):
-            nc.sync.dma_start(gate_t[:, lo:hi], gate[0:P, lo:hi])
-
-        w_tiles = []
-
-        def load_weights(a):
-            w_tile = keep.tile([P, E * N], U32, name="w%d" % a, align_bytes=64)
-            nc.sync.dma_start(
-                w_tile[:].bitcast(I32).rearrange("p (e n) -> p e n", n=N),
-                w_words[:, a].rearrange("e p n r -> p e (n r)").bitcast(I32),
-            )
-            w_tiles.append(w_tile)
 
         load_plane(0, 0)
         nc.sync.dma_start(offs_t[:], offs)
-        for lo, hi in zip(HEAD_CUTS[:-1], HEAD_CUTS[1:]):
-            load_gate(lo, hi)
         for r in range(1, PACK):
             load_plane(0, r)
-        load_gate(OWN * C, HALF * C)
-        for r in range(PACK):
+        nc.sync.dma_start(gate_own[:, 0 : HALF * C], gate[0:P, OWN * C : (OWN + HALF) * C])
+        load_plane(1, 0)
+        nc.sync.dma_start(gate_first[:], gate[0:P, 0 : GROUP * C])
+        for r in range(1, PACK):
             load_plane(1, r)
+        nc.sync.dma_start(gate_own[:, HALF * C :], gate[0:P, (OWN + HALF) * C :])
+        for r in range(PACK):
+            load_plane(LAST_PASS, r)
+        gate_rows = keep.tile([P, C], F32, name="gate_rows")
+        nc.sync.dma_start(gate_rows[:], gate.rearrange("k (e c) -> (k e) c", c=C)[0:P, :])
 
         w_scale = keep.tile([P, E * PASSES * N], U8, name="w_scale", align_bytes=64)
         nc.vector.memset(w_scale[:].bitcast(I32), 0)
@@ -83,12 +92,14 @@ def tile_moe_pre_lin_relu_kernel(tc, xT, w_words, w_scales, b, gate, offs, pos1,
         scale_dst = w_scale[:].bitcast(I32).rearrange("p (g n) -> p g n", n=N // 4)
         for quadrant in range(4):
             nc.sync.dma_start(scale_dst[32 * quadrant : 32 * quadrant + 4, :, :], scale_src[4 * quadrant : 4 * quadrant + 4, :, :])
-        load_weights(0)
-        load_gate(HALF * C, S)
-        load_weights(1)
-        for r in range(PACK):
-            load_plane(LAST_PASS, r)
-        load_weights(LAST_PASS)
+        w_tiles = []
+        for a in range(PASSES):
+            w_tile = keep.tile([P, E * N], U32, name="w%d" % a, align_bytes=64)
+            nc.sync.dma_start(
+                w_tile[:].bitcast(I32).rearrange("p (e n) -> p e n", n=N),
+                w_words[:, a].rearrange("e p n r -> p e (n r)").bitcast(I32),
+            )
+            w_tiles.append(w_tile)
         bias = keep.tile([P, E], F32, name="bias")
         nc.sync.dma_start(bias[:], b)
         pos_t = []
@@ -97,68 +108,79 @@ def tile_moe_pre_lin_relu_kernel(tc, xT, w_words, w_scales, b, gate, offs, pos1,
             nc.sync.dma_start(list_tile[:], pos)
             pos_t.append(list_tile)
 
-        y = keep.tile([P, S], F32, name="y")
-        banks = {}
-        for first, end in BANK_GROUPS:
-            bank = psum.tile([P, (end - first) * C], F32, name="bank%d" % first)
-            for e in range(first, end):
-                banks[e] = (bank[:, (e - first) * C : (e - first + 1) * C], e == first, e == end - 1)
+        gathered = {}
+
+        def gather(a, e0, e1, at, on_vector):
+            width = (e1 - e0) * C
+            gathered[a, e0] = placed("gathered%d_%d" % (a, e0), PACK * width, F32, at)
+            for r in range(PACK):
+                values = gathered[a, e0][:, r * width : (r + 1) * width]
+                looked_up = windows[a, r][:].indirect(entries(offs_t, e0 * C, e1 * C))
+                if on_vector:
+                    nc.vector.tensor_copy(values, looked_up)
+                else:
+                    nc.scalar.activation(values, looked_up, COPY)
 
         rounded = {}
 
         def rounded_view(a, e0, e1):
-            half = e0 // HALF
-            if (a, half) not in rounded:
-                rounded[a, half] = ring.tile([P, PACK * HALF * C], BF16, name="rounded%d_%d" % (a, half), tag="rounded", bufs=3, align_bytes=64)
-            return rounded[a, half][:, PACK * (e0 - half * HALF) * C : PACK * (e1 - half * HALF) * C]
+            first = e0 // GROUP * GROUP
+            return rounded[a, first][:, PACK * (e0 - first) * C : PACK * (e1 - first) * C]
 
-        own = {}
+        def place_rounded(a, first, at):
+            rounded[a, first] = placed("rounded%d_%d" % (a, first), PACK * GROUP * C, BF16, at)
 
-        def gather_own(a):
-            own[a] = ring.tile([P, PACK * OWN * C], F32, name="own%d" % a, tag="own", bufs=1)
-            for r in range(PACK):
-                cuts = HEAD_CUTS if (a, r) == (0, 0) else (0, OWN * C)
-                for lo, hi in zip(cuts[:-1], cuts[1:]):
-                    nc.vector.tensor_tensor(
-                        own[a][:, r * OWN * C + lo : r * OWN * C + hi],
-                        windows[a, r][:].indirect(entries(offs_t, lo, hi)),
-                        gate_t[:, lo:hi],
-                        MULT,
-                    )
-
-        def round_own(a):
-            nc.vector.tensor_copy(
-                rounded_view(a, 0, OWN).rearrange("p (c i r) -> p c r i", r=PACK, i=RUN),
-                own[a][:].rearrange("p (r c i) -> p c r i", r=PACK, i=RUN),
-            )
-
-        fetched = {}
-
-        def gather_piece(a, piece):
-            e0, e1 = PIECES[a][piece]
-            width = (e1 - e0) * C
-            fetched[a, piece] = ring.tile([P, PACK * width], F32, name="fetched%d_%d" % (a, piece), tag="fetched", bufs=3)
-            for r in range(PACK):
-                nc.scalar.activation(
-                    fetched[a, piece][:, r * width : (r + 1) * width],
-                    windows[a, r][:].indirect(entries(offs_t, e0 * C, e1 * C)),
-                    COPY,
-                )
-
-        def multiply(a, piece, e0, e1):
-            first = PIECES[a][piece][0]
-            runs = (e1 - e0) * C // RUN
-            nc.vector.tensor_tensor(
-                rounded_view(a, e0, e1).rearrange("p (c i r) -> p c r i", r=PACK, i=RUN),
-                fetched[a, piece][:].rearrange("p (r c i) -> p c r i", r=PACK, i=RUN)[:, (e0 - first) * C // RUN : (e1 - first) * C // RUN],
-                gate_t[:, e0 * C : e1 * C].rearrange("p (c i) -> p c i", i=RUN).unsqueeze(2).broadcast_to([P, runs, PACK, RUN]),
+        def multiply_on_gpsimd(a, first, e0, e1, gate_tile):
+            lo, hi = e0 % GROUP * C, (e1 - 1) % GROUP * C + C
+            nc.gpsimd.tensor_tensor(
+                rounded_view(a, e0, e1).rearrange("p (c r) -> p c r", r=PACK),
+                gathered[a, first][:].rearrange("p (r c) -> p c r", r=PACK)[:, (e0 - first) * C : (e1 - first) * C],
+                gate_tile[:, lo:hi].unsqueeze(2).broadcast_to([P, hi - lo, PACK]),
                 MULT,
             )
 
+        identity = keep.tile([P, P], F32, name="identity")
+        make_identity(nc, identity[:])
+        turned = psum.tile([P, P], F32, name="turned", offset=4 * BANK)
+        gate_columns = keep.tile([P, OWN], F32, name="gate_columns")
+        gate_banks = []
+
+        def spread_gate():
+            nc.tensor.transpose(turned[:], gate_rows[:], identity[:])
+            nc.vector.tensor_copy(gate_columns[:], turned[:, 0:OWN])
+            for q in range(OWN // HALF):
+                gate_bank = psum.tile([P, HALF * C], F32, name="gate_bank%d" % q, offset=q * BANK if q < 2 else q * BANK)
+                for j in range(HALF):
+                    e = q * HALF + j
+                    nc.tensor.transpose(gate_bank[:, j * C : (j + 1) * C], gate_columns[:, e : e + 1].to_broadcast([P, P]), identity[:])
+                gate_banks.append(gate_bank)
+
+        def multiply(a, first, e0, e1):
+            runs = (e1 - e0) * C // RUN
+            lo = e0 % HALF * C
+            nc.vector.tensor_tensor(
+                rounded_view(a, e0, e1).rearrange("p (c i r) -> p c r i", r=PACK, i=RUN),
+                gathered[a, first][:].rearrange("p (r c i) -> p c r i", r=PACK, i=RUN)[:, (e0 - first) * C // RUN : (e1 - first) * C // RUN],
+                gate_banks[e0 // HALF][:, lo : lo + (e1 - e0) * C].rearrange("p (c i) -> p c i", i=RUN).unsqueeze(2).broadcast_to([P, runs, PACK, RUN]),
+                MULT,
+            )
+
+        banks = {}
+
+        def open_banks(groups):
+            for first, end, index in groups:
+                bank = psum.tile([P, (end - first) * C], F32, name="bank%d" % first, offset=index * BANK)
+                for e in range(first, end):
+                    banks[e] = (bank[:, (e - first) * C : (e - first + 1) * C], e == first, e == end - 1)
+
+        quantised = []
+
         def quantise(a, e0, e1):
             count = e1 - e0
-            words = ring.tile([P, count * C], U32, name="words%d_%d" % (a, e0), tag="words", bufs=3, align_bytes=64)
-            scale_bytes = ring.tile([P, count * C], U8, name="bytes%d_%d" % (a, e0), tag="bytes", bufs=3, align_bytes=64)
+            at = own_at + 3 * BLOCK + len(quantised) % 3 * 5 * GROUP * C
+            quantised.append((a, e0))
+            words = placed("words%d_%d" % (a, e0), count * C, U32, at)
+            scale_bytes = placed("bytes%d_%d" % (a, e0), count * C, U8, at + 4 * GROUP * C)
             nc.vector.quantize_mx(words[:].bitcast(FP8X4), scale_bytes[:], rounded_view(a, e0, e1))
             for e in range(e0, e1):
                 acc, opens, closes = banks[e]
@@ -172,43 +194,66 @@ def tile_moe_pre_lin_relu_kernel(tc, xT, w_words, w_scales, b, gate, offs, pos1,
                     stop=(a == LAST_PASS and closes),
                 )
 
-        def finish(e, on_vector):
-            if on_vector:
-                nc.vector.tensor_scalar(y[:, e * C : (e + 1) * C], banks[e][0], bias[:, e : e + 1], 0.0, ADD, MAX)
-            else:
+        def fetch(step):
+            a, e0, e1 = SCALAR_PIECES[step]
+            at = fetched_at + min(step, 5) % 3 * 2 * BLOCK + (e0 % GROUP) * C * PACK * 4
+            gather(a, e0, e1, at, False)
+
+        gather(0, OWN, OWN + HALF, own_at, True)
+        fetch(0)
+        place_rounded(0, OWN, rounded_at)
+        multiply_on_gpsimd(0, OWN, OWN, OWN + HALF, gate_own)
+        gather(1, OWN, E, own_at + BLOCK, True)
+        fetch(1)
+        place_rounded(0, 0, rounded_at + BLOCK)
+        multiply_on_gpsimd(0, 0, 0, HALF, gate_first)
+        multiply_on_gpsimd(0, 0, HALF, GROUP, gate_first)
+        gather(0, OWN + HALF, E, own_at, True)
+        gather(LAST_PASS, OWN, E, own_at + 3 * BLOCK, True)
+        fetch(2)
+        place_rounded(1, OWN, rounded_at + 2 * BLOCK)
+        multiply_on_gpsimd(1, OWN, OWN, OWN + HALF, gate_own)
+        multiply_on_gpsimd(1, OWN, OWN + HALF, E, gate_own)
+        multiply_on_gpsimd(0, OWN + HALF, OWN + HALF, E, gate_own)
+        place_rounded(LAST_PASS, OWN, own_at + BLOCK)
+        multiply_on_gpsimd(LAST_PASS, OWN, OWN, OWN + HALF, gate_own)
+        multiply_on_gpsimd(LAST_PASS, OWN, OWN + HALF, E, gate_own)
+        spread_gate()
+        fetch(3)
+        for a in (1, 2):
+            place_rounded(a, 0, rounded_at + (2 + a) * BLOCK)
+            multiply(a, 0, 0, HALF)
+            multiply(a, 0, HALF, GROUP)
+            if a == 1:
+                fetch(4)
+        for step in range(5, len(SCALAR_PIECES)):
+            fetch(step)
+        place_rounded(0, GROUP, own_at + 2 * BLOCK)
+        multiply(0, GROUP, GROUP, GROUP + HALF)
+        multiply(0, GROUP, GROUP + HALF, OWN)
+        open_banks(BANK_GROUPS)
+        for first in (OWN, 0):
+            for a in range(PASSES):
+                quantise(a, first, first + GROUP)
+        place_rounded(1, GROUP, rounded_at + 3 * BLOCK)
+        multiply(1, GROUP, GROUP, GROUP + HALF)
+        multiply(1, GROUP, GROUP + HALF, OWN)
+        quantise(0, GROUP, OWN)
+        place_rounded(LAST_PASS, GROUP, rounded_at + 4 * BLOCK)
+        multiply(LAST_PASS, 8, 8, 12)
+        quantise(1, GROUP, OWN)
+        multiply(LAST_PASS, 12, 12, 14)
+        quantise(LAST_PASS, 8, 12)
+        multiply(LAST_PASS, 14, 14, 16)
+        quantise(LAST_PASS, 12, 14)
+        quantise(LAST_PASS, 14, 16)
+
+        y = placed("y", S, F32, 0)
+        for first, end, index in BANK_GROUPS:
+            for e in range(first, end):
                 nc.scalar.activation(y[:, e * C : (e + 1) * C], banks[e][0], RELU, bias=bias[:, e : e + 1])
 
-        gather_own(0)
-        for a in range(PASSES):
-            gather_piece(a, 0)
-            gather_piece(a, 1)
-            gather_piece(a, 2)
-            multiply(a, 0, *PIECES[a][0])
-            round_own(a)
-            if a > 0:
-                quantise(a - 1, 12, 20)
-                quantise(a - 1, 20, 24)
-            if a < LAST_PASS:
-                gather_own(a + 1)
-                quantise(a, 0, 8)
-                quantise(a, 8, 12)
-                multiply(a, 1, *PIECES[a][1])
-                multiply(a, 2, *PIECES[a][2])
-        a = LAST_PASS
-        quantise(a, 0, 8)
-        quantise(a, 8, 12)
-        multiply(a, 1, 12, 19)
-        multiply(a, 2, 19, 22)
-        quantise(a, 12, 16)
-        quantise(a, 16, 19)
-        multiply(a, 2, 22, 24)
-        quantise(a, 19, 22)
-        quantise(a, 22, 23)
-        quantise(a, 23, 24)
-        for e in range(E):
-            finish(e, e in (19, 20))
-
-        sums = ring.tile([P, 3 * T], F32, name="sums", tag="own", bufs=1)
+        sums = placed("sums", 3 * T, F32, pass_bytes)
 
         def combine(choice, lo, hi):
             looked_up = y[:].indirect(entries(pos_t[choice], lo, hi))

@@ -19,7 +19,8 @@ BANK = 2048
 BLOCK = 2 * PACK * GROUP * C
 OWN = 2 * GROUP
 SCALAR_PIECES = ((0, 0, 8), (1, 0, 8), (2, 0, 8), (0, 8, 16), (1, 8, 16), (2, 8, 12), (2, 12, 14), (2, 14, 16))
-BANK_GROUPS = ((16, 20, 4), (20, 24, 5), (0, 4, 6), (4, 8, 7), (8, 12, 0), (12, 16, 1))
+BANK_GROUPS = ((16, 20, 4), (20, 24, 5), (0, 4, 6), (4, 8, 7), (8, 12, 0), (12, 14, 1), (14, 15, 4), (15, 16, 5))
+LATE = 14
 
 FLOPS = 2 * K * S * N
 BYTES = 4 * K * T + E * K * N + E * K * N // 32 + 4 * N * E + 4 * S + 2 * P * (S + 3 * T) // PER_COLUMN + 4 * N * T
@@ -133,9 +134,9 @@ def tile_moe_pre_lin_relu_kernel(tc, xT, w_words, w_scales, b, gate, offs, pos1,
         def multiply_on_gpsimd(a, first, e0, e1, gate_tile):
             lo, hi = e0 % GROUP * C, (e1 - 1) % GROUP * C + C
             nc.gpsimd.tensor_tensor(
-                rounded_view(a, e0, e1).rearrange("p (c r) -> p c r", r=PACK),
-                gathered[a, first][:].rearrange("p (r c) -> p c r", r=PACK)[:, (e0 - first) * C : (e1 - first) * C],
-                gate_tile[:, lo:hi].unsqueeze(2).broadcast_to([P, hi - lo, PACK]),
+                rounded_view(a, e0, e1).rearrange("p (c i r) -> p c r i", r=PACK, i=RUN),
+                gathered[a, first][:].rearrange("p (r c i) -> p c r i", r=PACK, i=RUN)[:, (e0 - first) * C // RUN : (e1 - first) * C // RUN],
+                gate_tile[:, lo:hi].rearrange("p (c i) -> p c i", i=RUN).unsqueeze(2).broadcast_to([P, (hi - lo) // RUN, PACK, RUN]),
                 MULT,
             )
 
@@ -175,21 +176,29 @@ def tile_moe_pre_lin_relu_kernel(tc, xT, w_words, w_scales, b, gate, offs, pos1,
 
         quantised = []
 
-        def quantise(a, e0, e1):
+        codes = {}
+
+        def quantise(a, e0, e1, at=None):
             count = e1 - e0
-            at = own_at + 3 * BLOCK + len(quantised) % 3 * 5 * GROUP * C
-            quantised.append((a, e0))
+            if at is None:
+                at = own_at + 3 * BLOCK + len(quantised) % 3 * 5 * GROUP * C
+                quantised.append((a, e0))
             words = placed("words%d_%d" % (a, e0), count * C, U32, at)
             scale_bytes = placed("bytes%d_%d" % (a, e0), count * C, U8, at + 4 * GROUP * C)
             nc.vector.quantize_mx(words[:].bitcast(FP8X4), scale_bytes[:], rounded_view(a, e0, e1))
             for e in range(e0, e1):
+                codes[a, e] = (words[:, (e - e0) * C : (e - e0 + 1) * C], scale_bytes[:, (e - e0) * C : (e - e0 + 1) * C])
+            contract(a, [e for e in range(e0, e1) if e in banks])
+
+        def contract(a, experts):
+            for e in experts:
                 acc, opens, closes = banks[e]
                 nc.tensor.matmul_mx(
                     acc,
                     lhsT=w_tiles[a][:, e * N : (e + 1) * N].bitcast(FP8X4),
                     lhsT_scale=w_scale[:, (e * PASSES + a) * N : (e * PASSES + a + 1) * N],
-                    rhs=words[:, (e - e0) * C : (e - e0 + 1) * C].bitcast(FP8X4),
-                    rhs_scale=scale_bytes[:, (e - e0) * C : (e - e0 + 1) * C],
+                    rhs=codes[a, e][0].bitcast(FP8X4),
+                    rhs_scale=codes[a, e][1],
                     start=(a == 0 and opens),
                     stop=(a == LAST_PASS and closes),
                 )
@@ -231,46 +240,70 @@ def tile_moe_pre_lin_relu_kernel(tc, xT, w_words, w_scales, b, gate, offs, pos1,
         place_rounded(0, GROUP, own_at + 2 * BLOCK)
         multiply(0, GROUP, GROUP, GROUP + HALF)
         multiply(0, GROUP, GROUP + HALF, OWN)
-        open_banks(BANK_GROUPS)
+        open_banks(BANK_GROUPS[:-2])
         for first in (OWN, 0):
             for a in range(PASSES):
                 quantise(a, first, first + GROUP)
+        y = placed("y", S, F32, 0)
+
+        def finish(e):
+            if e == LATE:
+                nc.vector.tensor_scalar(y[:, e * C : (e + 1) * C], banks[e][0], bias[:, e : e + 1], 0.0, ADD, MAX)
+            else:
+                nc.scalar.activation(y[:, e * C : (e + 1) * C], banks[e][0], RELU, bias=bias[:, e : e + 1])
+
+        for first in (OWN, 0):
+            for e in range(first, first + GROUP):
+                finish(e)
         place_rounded(1, GROUP, rounded_at + 3 * BLOCK)
         multiply(1, GROUP, GROUP, GROUP + HALF)
         multiply(1, GROUP, GROUP + HALF, OWN)
-        quantise(0, GROUP, OWN)
+        quantise(0, GROUP, OWN, rounded_at)
         place_rounded(LAST_PASS, GROUP, rounded_at + 4 * BLOCK)
         multiply(LAST_PASS, 8, 8, 12)
-        quantise(1, GROUP, OWN)
+        quantise(1, GROUP, OWN, rounded_at + BLOCK)
+        open_banks(BANK_GROUPS[-2:])
+        for a in range(LAST_PASS):
+            contract(a, range(LATE, OWN))
         multiply(LAST_PASS, 12, 12, 14)
         quantise(LAST_PASS, 8, 12)
         multiply(LAST_PASS, 14, 14, 16)
         quantise(LAST_PASS, 12, 14)
         quantise(LAST_PASS, 14, 16)
+        for e in range(GROUP, OWN):
+            finish(e)
 
-        y = placed("y", S, F32, 0)
-        for first, end, index in BANK_GROUPS:
-            for e in range(first, end):
-                nc.scalar.activation(y[:, e * C : (e + 1) * C], banks[e][0], RELU, bias=bias[:, e : e + 1])
+        sums = placed("sums", 4 * T, F32, pass_bytes)
 
-        sums = placed("sums", 3 * T, F32, pass_bytes)
+        def looked_up(choice, lo, hi):
+            return y[:].indirect(entries(pos_t[choice], lo, hi))
 
-        def combine(choice, lo, hi):
-            looked_up = y[:].indirect(entries(pos_t[choice], lo, hi))
-            total = sums[:, choice * T + lo : choice * T + hi]
-            if choice == 0:
-                nc.scalar.activation(total, looked_up, COPY)
-            else:
-                nc.vector.tensor_tensor(total, looked_up, sums[:, (choice - 1) * T + lo : (choice - 1) * T + hi], ADD)
-            if choice == 2:
-                nc.sync.dma_start(out[:, lo:hi], total)
+        def part(index, lo, hi):
+            return sums[:, index * T + lo : index * T + hi]
 
-        combine(0, 0, 128)
-        combine(0, 128, 384)
-        combine(0, 384, T)
-        combine(1, 0, 128)
-        combine(1, 128, 384)
-        combine(2, 0, 384)
-        combine(1, 384, T)
-        combine(2, 384, 896)
-        combine(2, 896, T)
+        def fetch_on_scalar(choice, lo, hi):
+            nc.scalar.activation(part(choice, lo, hi), looked_up(choice, lo, hi), COPY)
+
+        def fetch_and_add(target, choice, source, lo, hi):
+            nc.vector.tensor_tensor(part(target, lo, hi), looked_up(choice, lo, hi), part(source, lo, hi), ADD)
+
+        def add_and_store(lo, hi, other):
+            nc.vector.tensor_tensor(part(3, lo, hi), part(2, lo, hi), part(other, lo, hi), ADD)
+            nc.sync.dma_start(out[:, lo:hi], part(3, lo, hi))
+
+        t1, t2, t3 = 256, 448, 800
+        fetch_on_scalar(0, 0, t1)
+        fetch_on_scalar(0, t1, t3)
+        fetch_on_scalar(1, t2, t3)
+        fetch_on_scalar(0, t3, T)
+        fetch_on_scalar(1, t3, T)
+        nc.vector.tensor_copy(part(1, t1, t2), looked_up(2, t1, t2))
+        fetch_and_add(1, 1, 0, 0, t1)
+        fetch_and_add(2, 1, 1, t1, t2)
+        fetch_and_add(3, 2, 1, 0, t1)
+        nc.vector.tensor_tensor(part(3, t1, t2), part(2, t1, t2), part(0, t1, t2), ADD)
+        nc.sync.dma_start(out[:, 0:t2], part(3, 0, t2))
+        fetch_and_add(2, 2, 0, t2, t3)
+        fetch_and_add(2, 2, 0, t3, T)
+        add_and_store(t2, t3, 1)
+        add_and_store(t3, T, 1)

@@ -18,9 +18,11 @@ WIDE = T + 8
 BANK = 2048
 BLOCK = 2 * PACK * GROUP * C
 OWN = 2 * GROUP
-SCALAR_PIECES = ((0, 0, 8), (1, 0, 8), (2, 0, 8), (0, 8, 16), (1, 8, 16), (2, 8, 12), (2, 12, 14), (2, 14, 16))
-BANK_GROUPS = ((16, 20, 4), (20, 24, 5), (0, 4, 6), (4, 8, 7), (8, 12, 0), (12, 14, 1), (14, 15, 4), (15, 16, 5))
-LATE = 14
+EARLY = 7
+HELPED = (3, 2, 1)
+SCALAR_PIECES = ((0, 0, 8), (1, 0, 8), (2, 0, 8), (0, 8, 16), (1, 8, 16), (2, 8, 12))
+BANK_GROUPS = ((16, 20, 4), (20, 24, 5), (0, 4, 6), (4, 8, 7), (12, 16, 0), (8, 10, 1), (10, 11, 4), (11, 12, 5))
+LATE = (10, 11)
 
 FLOPS = 2 * K * S * N
 BYTES = 4 * K * T + E * K * N + E * K * N // 32 + 4 * N * E + 4 * S + 2 * P * (S + 3 * T) // PER_COLUMN + 4 * N * T
@@ -55,7 +57,7 @@ def tile_moe_pre_lin_relu_kernel(tc, xT, w_words, w_scales, b, gate, offs, pos1,
 
         pass_bytes = PACK * 4 * WIDE + 128
         own_at = PASSES * pass_bytes
-        fetched_at = own_at + 5 * BLOCK
+        fetched_at = own_at + 6 * BLOCK
         rounded_at = fetched_at + 6 * BLOCK
 
         warm = keep.tile([P, 16], F32, name="warm")
@@ -63,7 +65,8 @@ def tile_moe_pre_lin_relu_kernel(tc, xT, w_words, w_scales, b, gate, offs, pos1,
         nc.scalar.activation(warm[:, 8:9], warm[:, 0:1], RELU)
 
         offs_t = keep.tile([P, S // PER_COLUMN], U16, name="offs_t")
-        gate_first = keep.tile([P, GROUP * C], F32, name="gate_first")
+        gate_first = keep.tile([P, EARLY * C], F32, name="gate_first")
+        gate_last = keep.tile([P, max(HELPED) * C], F32, name="gate_last")
         gate_own = keep.tile([P, GROUP * C], F32, name="gate_own")
         windows = {}
 
@@ -78,14 +81,15 @@ def tile_moe_pre_lin_relu_kernel(tc, xT, w_words, w_scales, b, gate, offs, pos1,
             load_plane(0, r)
         nc.sync.dma_start(gate_own[:, 0 : HALF * C], gate[0:P, OWN * C : (OWN + HALF) * C])
         load_plane(1, 0)
-        nc.sync.dma_start(gate_first[:], gate[0:P, 0 : GROUP * C])
+        nc.sync.dma_start(gate_first[:], gate[0:P, 0 : EARLY * C])
         for r in range(1, PACK):
             load_plane(1, r)
         nc.sync.dma_start(gate_own[:, HALF * C :], gate[0:P, (OWN + HALF) * C :])
-        for r in range(PACK):
+        for r in range(PACK - 1):
             load_plane(LAST_PASS, r)
         gate_rows = keep.tile([P, C], F32, name="gate_rows")
         nc.sync.dma_start(gate_rows[:], gate.rearrange("k (e c) -> (k e) c", c=C)[0:P, :])
+        load_plane(LAST_PASS, PACK - 1)
 
         w_scale = keep.tile([P, E * PASSES * N], U8, name="w_scale", align_bytes=64)
         nc.vector.memset(w_scale[:].bitcast(I32), 0)
@@ -101,6 +105,7 @@ def tile_moe_pre_lin_relu_kernel(tc, xT, w_words, w_scales, b, gate, offs, pos1,
                 w_words[:, a].rearrange("e p n r -> p e (n r)").bitcast(I32),
             )
             w_tiles.append(w_tile)
+        nc.sync.dma_start(gate_last[:], gate[0:P, GROUP * C : (GROUP + max(HELPED)) * C])
         bias = keep.tile([P, E], F32, name="bias")
         nc.sync.dma_start(bias[:], b)
         pos_t = []
@@ -125,18 +130,18 @@ def tile_moe_pre_lin_relu_kernel(tc, xT, w_words, w_scales, b, gate, offs, pos1,
         rounded = {}
 
         def rounded_view(a, e0, e1):
-            first = e0 // GROUP * GROUP
+            first = max(f for (pass_of, f) in rounded if pass_of == a and f <= e0)
             return rounded[a, first][:, PACK * (e0 - first) * C : PACK * (e1 - first) * C]
 
-        def place_rounded(a, first, at):
-            rounded[a, first] = placed("rounded%d_%d" % (a, first), PACK * GROUP * C, BF16, at)
+        def place_rounded(a, first, at, experts=GROUP):
+            rounded[a, first] = placed("rounded%d_%d" % (a, first), PACK * experts * C, BF16, at)
 
         def multiply_on_gpsimd(a, first, e0, e1, gate_tile):
             lo, hi = e0 % GROUP * C, (e1 - 1) % GROUP * C + C
             nc.gpsimd.tensor_tensor(
-                rounded_view(a, e0, e1).rearrange("p (c i r) -> p c r i", r=PACK, i=RUN),
-                gathered[a, first][:].rearrange("p (r c i) -> p c r i", r=PACK, i=RUN)[:, (e0 - first) * C // RUN : (e1 - first) * C // RUN],
-                gate_tile[:, lo:hi].rearrange("p (c i) -> p c i", i=RUN).unsqueeze(2).broadcast_to([P, (hi - lo) // RUN, PACK, RUN]),
+                rounded_view(a, e0, e1).rearrange("p (c r) -> p c r", r=PACK),
+                gathered[a, first][:].rearrange("p (r c) -> p c r", r=PACK)[:, (e0 - first) * C : (e1 - first) * C],
+                gate_tile[:, lo:hi].unsqueeze(2).broadcast_to([P, hi - lo, PACK]),
                 MULT,
             )
 
@@ -172,17 +177,14 @@ def tile_moe_pre_lin_relu_kernel(tc, xT, w_words, w_scales, b, gate, offs, pos1,
             for first, end, index in groups:
                 bank = psum.tile([P, (end - first) * C], F32, name="bank%d" % first, offset=index * BANK)
                 for e in range(first, end):
-                    banks[e] = (bank[:, (e - first) * C : (e - first + 1) * C], e == first, e == end - 1)
+                    banks[e] = (bank[:, (e - first) * C : (e - first + 1) * C], first, PASSES * (end - first))
 
-        quantised = []
 
         codes = {}
+        issued = {}
 
-        def quantise(a, e0, e1, at=None):
+        def quantise(a, e0, e1, at):
             count = e1 - e0
-            if at is None:
-                at = own_at + 3 * BLOCK + len(quantised) % 3 * 5 * GROUP * C
-                quantised.append((a, e0))
             words = placed("words%d_%d" % (a, e0), count * C, U32, at)
             scale_bytes = placed("bytes%d_%d" % (a, e0), count * C, U8, at + 4 * GROUP * C)
             nc.vector.quantize_mx(words[:].bitcast(FP8X4), scale_bytes[:], rounded_view(a, e0, e1))
@@ -192,15 +194,16 @@ def tile_moe_pre_lin_relu_kernel(tc, xT, w_words, w_scales, b, gate, offs, pos1,
 
         def contract(a, experts):
             for e in experts:
-                acc, opens, closes = banks[e]
+                acc, first, total = banks[e]
+                issued[first] = issued.get(first, 0) + 1
                 nc.tensor.matmul_mx(
                     acc,
                     lhsT=w_tiles[a][:, e * N : (e + 1) * N].bitcast(FP8X4),
                     lhsT_scale=w_scale[:, (e * PASSES + a) * N : (e * PASSES + a + 1) * N],
                     rhs=codes[a, e][0].bitcast(FP8X4),
                     rhs_scale=codes[a, e][1],
-                    start=(a == 0 and opens),
-                    stop=(a == LAST_PASS and closes),
+                    start=issued[first] == 1,
+                    stop=issued[first] == total,
                 )
 
         def fetch(step):
@@ -212,42 +215,44 @@ def tile_moe_pre_lin_relu_kernel(tc, xT, w_words, w_scales, b, gate, offs, pos1,
         fetch(0)
         place_rounded(0, OWN, rounded_at)
         multiply_on_gpsimd(0, OWN, OWN, OWN + HALF, gate_own)
-        gather(1, OWN, E, own_at + BLOCK, True)
+        gather(1, OWN, E, own_at + 2 * BLOCK, True)
         fetch(1)
+        gather(0, OWN + HALF, E, own_at, False)
         place_rounded(0, 0, rounded_at + BLOCK)
-        multiply_on_gpsimd(0, 0, 0, HALF, gate_first)
-        multiply_on_gpsimd(0, 0, HALF, GROUP, gate_first)
-        gather(0, OWN + HALF, E, own_at, True)
-        gather(LAST_PASS, OWN, E, own_at + 3 * BLOCK, True)
+        multiply_on_gpsimd(0, 0, 0, EARLY, gate_first)
+        gather(LAST_PASS, OWN, E, own_at + 4 * BLOCK, True)
+        gather(LAST_PASS, OWN - HALF, OWN, own_at + BLOCK, True)
         fetch(2)
         place_rounded(1, OWN, rounded_at + 2 * BLOCK)
-        multiply_on_gpsimd(1, OWN, OWN, OWN + HALF, gate_own)
-        multiply_on_gpsimd(1, OWN, OWN + HALF, E, gate_own)
+        multiply_on_gpsimd(1, OWN, OWN, E, gate_own)
         multiply_on_gpsimd(0, OWN + HALF, OWN + HALF, E, gate_own)
-        place_rounded(LAST_PASS, OWN, own_at + BLOCK)
-        multiply_on_gpsimd(LAST_PASS, OWN, OWN, OWN + HALF, gate_own)
-        multiply_on_gpsimd(LAST_PASS, OWN, OWN + HALF, E, gate_own)
+        place_rounded(LAST_PASS, OWN, own_at + 2 * BLOCK)
+        multiply_on_gpsimd(LAST_PASS, OWN, OWN, E, gate_own)
         spread_gate()
+        multiply(0, 0, EARLY, GROUP)
         fetch(3)
-        for a in (1, 2):
-            place_rounded(a, 0, rounded_at + (2 + a) * BLOCK)
-            multiply(a, 0, 0, HALF)
-            multiply(a, 0, HALF, GROUP)
-            if a == 1:
-                fetch(4)
-        for step in range(5, len(SCALAR_PIECES)):
-            fetch(step)
-        place_rounded(0, GROUP, own_at + 2 * BLOCK)
-        multiply(0, GROUP, GROUP, GROUP + HALF)
-        multiply(0, GROUP, GROUP + HALF, OWN)
+        place_rounded(LAST_PASS, OWN - HALF, rounded_at + 4 * BLOCK, HALF)
+        multiply(LAST_PASS, OWN - HALF, OWN - HALF, OWN)
+        place_rounded(1, 0, rounded_at + 3 * BLOCK)
+        multiply(1, 0, 0, HALF)
+        multiply(1, 0, HALF, GROUP)
+        fetch(4)
+        place_rounded(LAST_PASS, 0, own_at + BLOCK)
+        multiply(LAST_PASS, 0, 0, HALF)
+        multiply(LAST_PASS, 0, HALF, GROUP)
+        fetch(5)
         open_banks(BANK_GROUPS[:-2])
-        for first in (OWN, 0):
-            for a in range(PASSES):
-                quantise(a, first, first + GROUP)
+        codes_at = [own_at + 4 * BLOCK + a * 5 * GROUP * C for a in range(PASSES)]
+        for a in range(PASSES):
+            quantise(a, OWN, E, codes_at[a])
+        quantise(LAST_PASS, OWN - HALF, OWN, rounded_at)
+        quantise(0, 0, GROUP, rounded_at + 2 * BLOCK)
+        quantise(1, 0, GROUP, own_at + 2 * BLOCK)
+        quantise(LAST_PASS, 0, GROUP, rounded_at + BLOCK)
         y = placed("y", S, F32, 0)
 
         def finish(e):
-            if e == LATE:
+            if e == LATE[0]:
                 nc.vector.tensor_scalar(y[:, e * C : (e + 1) * C], banks[e][0], bias[:, e : e + 1], 0.0, ADD, MAX)
             else:
                 nc.scalar.activation(y[:, e * C : (e + 1) * C], banks[e][0], RELU, bias=bias[:, e : e + 1])
@@ -255,22 +260,23 @@ def tile_moe_pre_lin_relu_kernel(tc, xT, w_words, w_scales, b, gate, offs, pos1,
         for first in (OWN, 0):
             for e in range(first, first + GROUP):
                 finish(e)
-        place_rounded(1, GROUP, rounded_at + 3 * BLOCK)
-        multiply(1, GROUP, GROUP, GROUP + HALF)
-        multiply(1, GROUP, GROUP + HALF, OWN)
-        quantise(0, GROUP, OWN, rounded_at)
-        place_rounded(LAST_PASS, GROUP, rounded_at + 4 * BLOCK)
-        multiply(LAST_PASS, 8, 8, 12)
-        quantise(1, GROUP, OWN, rounded_at + BLOCK)
+        both = placed("rounded_both", LAST_PASS * PACK * GROUP * C, BF16, own_at)
+        for a in range(LAST_PASS):
+            rounded[a, GROUP] = both[:, a * PACK * GROUP * C : (a + 1) * PACK * GROUP * C]
+            multiply_on_gpsimd(a, GROUP, GROUP, GROUP + HELPED[a], gate_last)
+            multiply(a, GROUP, GROUP + HELPED[a], GROUP + HALF)
+            multiply(a, GROUP, GROUP + HALF, OWN)
+        for a in range(LAST_PASS):
+            quantise(a, GROUP, OWN, (rounded_at, own_at)[a] + 3 * BLOCK)
         open_banks(BANK_GROUPS[-2:])
         for a in range(LAST_PASS):
-            contract(a, range(LATE, OWN))
-        multiply(LAST_PASS, 12, 12, 14)
-        quantise(LAST_PASS, 8, 12)
-        multiply(LAST_PASS, 14, 14, 16)
-        quantise(LAST_PASS, 12, 14)
-        quantise(LAST_PASS, 14, 16)
-        for e in range(GROUP, OWN):
+            contract(a, LATE)
+        place_rounded(LAST_PASS, GROUP, own_at + BLOCK, HALF)
+        multiply_on_gpsimd(LAST_PASS, GROUP, GROUP, GROUP + HELPED[LAST_PASS], gate_last)
+        multiply(LAST_PASS, GROUP, GROUP + HELPED[LAST_PASS], GROUP + HALF)
+        quantise(LAST_PASS, 8, 10, codes_at[0])
+        quantise(LAST_PASS, 10, 12, codes_at[1])
+        for e in (12, 13, 14, 15, 8, 9, 10, 11):
             finish(e)
 
         sums = placed("sums", 4 * T, F32, pass_bytes)

@@ -17,12 +17,10 @@ HALF = GROUP // 2
 WIDE = T + 8
 BANK = 2048
 BLOCK = 2 * PACK * GROUP * C
-OWN = 2 * GROUP
-EARLY = 7
-HELPED = (3, 2, 1)
-SCALAR_PIECES = ((0, 0, 8), (1, 0, 8), (2, 0, 8), (0, 8, 16), (1, 8, 16), (2, 8, 12))
-BANK_GROUPS = ((16, 20, 4), (20, 24, 5), (0, 4, 6), (4, 8, 7), (12, 16, 0), (8, 10, 1), (10, 11, 4), (11, 12, 5))
-LATE = (10, 11)
+SLOW, EARLY, LAST = 8, 16, 0
+HELPED = (3, 2, 2)
+BANK_GROUPS = ((8, 12, 4), (12, 16, 5), (16, 20, 6), (20, 24, 7), (0, 4, 0), (4, 6, 1), (6, 7, 4), (7, 8, 5))
+LATE = (6, 7)
 
 FLOPS = 2 * K * S * N
 BYTES = 4 * K * T + E * K * N + E * K * N // 32 + 4 * N * E + 4 * S + 2 * P * (S + 3 * T) // PER_COLUMN + 4 * N * T
@@ -56,18 +54,18 @@ def tile_moe_pre_lin_relu_kernel(tc, xT, w_words, w_scales, b, gate, offs, pos1,
             return stage.tile([P, columns], dtype, name=name, offset=offset, align_bytes=64)
 
         pass_bytes = PACK * 4 * WIDE + 128
-        own_at = PASSES * pass_bytes
-        fetched_at = own_at + 6 * BLOCK
-        rounded_at = fetched_at + 6 * BLOCK
+        small_at = PASSES * pass_bytes
+        own_at = (small_at, small_at + 2 * BLOCK, small_at + 6 * BLOCK)
+        fetched_at = (small_at + 10 * BLOCK, small_at + 4 * BLOCK, small_at + 8 * BLOCK)
+        rounded_at = small_at + 12 * BLOCK
 
         warm = keep.tile([P, 16], F32, name="warm")
         nc.gpsimd.memset(warm[:, 0:8], 0.0)
         nc.scalar.activation(warm[:, 8:9], warm[:, 0:1], RELU)
 
         offs_t = keep.tile([P, S // PER_COLUMN], U16, name="offs_t")
-        gate_first = keep.tile([P, EARLY * C], F32, name="gate_first")
+        gate_slow = keep.tile([P, (GROUP + HALF) * C], F32, name="gate_slow")
         gate_last = keep.tile([P, max(HELPED) * C], F32, name="gate_last")
-        gate_own = keep.tile([P, GROUP * C], F32, name="gate_own")
         windows = {}
 
         def load_plane(a, r):
@@ -79,12 +77,12 @@ def tile_moe_pre_lin_relu_kernel(tc, xT, w_words, w_scales, b, gate, offs, pos1,
         nc.sync.dma_start(offs_t[:], offs)
         for r in range(1, PACK):
             load_plane(0, r)
-        nc.sync.dma_start(gate_own[:, 0 : HALF * C], gate[0:P, OWN * C : (OWN + HALF) * C])
         load_plane(1, 0)
-        nc.sync.dma_start(gate_first[:], gate[0:P, 0 : EARLY * C])
-        for r in range(1, PACK):
+        nc.sync.dma_start(gate_slow[:, 0 : HALF * C], gate[0:P, SLOW * C : (SLOW + HALF) * C])
+        load_plane(1, 1)
+        nc.sync.dma_start(gate_slow[:, HALF * C :], gate[0:P, (SLOW + HALF) * C : (EARLY + HALF) * C])
+        for r in range(2, PACK):
             load_plane(1, r)
-        nc.sync.dma_start(gate_own[:, HALF * C :], gate[0:P, (OWN + HALF) * C :])
         for r in range(PACK - 1):
             load_plane(LAST_PASS, r)
         gate_rows = keep.tile([P, C], F32, name="gate_rows")
@@ -105,7 +103,7 @@ def tile_moe_pre_lin_relu_kernel(tc, xT, w_words, w_scales, b, gate, offs, pos1,
                 w_words[:, a].rearrange("e p n r -> p e (n r)").bitcast(I32),
             )
             w_tiles.append(w_tile)
-        nc.sync.dma_start(gate_last[:], gate[0:P, GROUP * C : (GROUP + max(HELPED)) * C])
+        nc.sync.dma_start(gate_last[:], gate[0:P, LAST * C : (LAST + max(HELPED)) * C])
         bias = keep.tile([P, E], F32, name="bias")
         nc.sync.dma_start(bias[:], b)
         pos_t = []
@@ -116,16 +114,20 @@ def tile_moe_pre_lin_relu_kernel(tc, xT, w_words, w_scales, b, gate, offs, pos1,
 
         gathered = {}
 
-        def gather(a, e0, e1, at, on_vector):
-            width = (e1 - e0) * C
+        def gather(a, e0, at, *parts):
+            width = (parts[-1][0] - e0) * C
             gathered[a, e0] = placed("gathered%d_%d" % (a, e0), PACK * width, F32, at)
-            for r in range(PACK):
-                values = gathered[a, e0][:, r * width : (r + 1) * width]
-                looked_up = windows[a, r][:].indirect(entries(offs_t, e0 * C, e1 * C))
-                if on_vector:
-                    nc.vector.tensor_copy(values, looked_up)
-                else:
-                    nc.scalar.activation(values, looked_up, COPY)
+            lo = 0
+            for end, on_vector in parts:
+                hi = (end - e0) * C
+                for r in range(PACK):
+                    values = gathered[a, e0][:, r * width + lo : r * width + hi]
+                    looked_up = windows[a, r][:].indirect(entries(offs_t, e0 * C + lo, e0 * C + hi))
+                    if on_vector:
+                        nc.vector.tensor_copy(values, looked_up)
+                    else:
+                        nc.scalar.activation(values, looked_up, COPY)
+                lo = hi
 
         rounded = {}
 
@@ -136,8 +138,9 @@ def tile_moe_pre_lin_relu_kernel(tc, xT, w_words, w_scales, b, gate, offs, pos1,
         def place_rounded(a, first, at, experts=GROUP):
             rounded[a, first] = placed("rounded%d_%d" % (a, first), PACK * experts * C, BF16, at)
 
-        def multiply_on_gpsimd(a, first, e0, e1, gate_tile):
-            lo, hi = e0 % GROUP * C, (e1 - 1) % GROUP * C + C
+        def multiply_on_gpsimd(a, first, e0, e1):
+            gate_tile, base = (gate_last, LAST) if e0 < SLOW else (gate_slow, SLOW)
+            lo, hi = (e0 - base) * C, (e1 - base) * C
             nc.gpsimd.tensor_tensor(
                 rounded_view(a, e0, e1).rearrange("p (c r) -> p c r", r=PACK),
                 gathered[a, first][:].rearrange("p (r c) -> p c r", r=PACK)[:, (e0 - first) * C : (e1 - first) * C],
@@ -148,18 +151,18 @@ def tile_moe_pre_lin_relu_kernel(tc, xT, w_words, w_scales, b, gate, offs, pos1,
         identity = keep.tile([P, P], F32, name="identity")
         make_identity(nc, identity[:])
         turned = psum.tile([P, P], F32, name="turned", offset=4 * BANK)
-        gate_columns = keep.tile([P, OWN], F32, name="gate_columns")
-        gate_banks = []
+        gate_columns = keep.tile([P, E], F32, name="gate_columns")
+        gate_banks = {}
 
         def spread_gate():
             nc.tensor.transpose(turned[:], gate_rows[:], identity[:])
-            nc.vector.tensor_copy(gate_columns[:], turned[:, 0:OWN])
-            for q in range(OWN // HALF):
-                gate_bank = psum.tile([P, HALF * C], F32, name="gate_bank%d" % q, offset=q * BANK if q < 2 else q * BANK)
+            nc.vector.tensor_copy(gate_columns[:], turned[:, 0:E])
+            for index, first in enumerate((EARLY + HALF, EARLY, LAST, LAST + HALF)):
+                gate_bank = psum.tile([P, HALF * C], F32, name="gate_bank%d" % first, offset=index * BANK)
                 for j in range(HALF):
-                    e = q * HALF + j
+                    e = first + j
                     nc.tensor.transpose(gate_bank[:, j * C : (j + 1) * C], gate_columns[:, e : e + 1].to_broadcast([P, P]), identity[:])
-                gate_banks.append(gate_bank)
+                gate_banks[first // HALF] = gate_bank
 
         def multiply(a, first, e0, e1):
             runs = (e1 - e0) * C // RUN
@@ -206,49 +209,38 @@ def tile_moe_pre_lin_relu_kernel(tc, xT, w_words, w_scales, b, gate, offs, pos1,
                     stop=issued[first] == total,
                 )
 
-        def fetch(step):
-            a, e0, e1 = SCALAR_PIECES[step]
-            at = fetched_at + min(step, 5) % 3 * 2 * BLOCK + (e0 % GROUP) * C * PACK * 4
-            gather(a, e0, e1, at, False)
-
-        gather(0, OWN, OWN + HALF, own_at, True)
-        fetch(0)
-        place_rounded(0, OWN, rounded_at)
-        multiply_on_gpsimd(0, OWN, OWN, OWN + HALF, gate_own)
-        gather(1, OWN, E, own_at + 2 * BLOCK, True)
-        fetch(1)
-        gather(0, OWN + HALF, E, own_at, False)
-        place_rounded(0, 0, rounded_at + BLOCK)
-        multiply_on_gpsimd(0, 0, 0, EARLY, gate_first)
-        gather(LAST_PASS, OWN, E, own_at + 4 * BLOCK, True)
-        gather(LAST_PASS, OWN - HALF, OWN, own_at + BLOCK, True)
-        fetch(2)
-        place_rounded(1, OWN, rounded_at + 2 * BLOCK)
-        multiply_on_gpsimd(1, OWN, OWN, E, gate_own)
-        multiply_on_gpsimd(0, OWN + HALF, OWN + HALF, E, gate_own)
-        place_rounded(LAST_PASS, OWN, own_at + 2 * BLOCK)
-        multiply_on_gpsimd(LAST_PASS, OWN, OWN, E, gate_own)
+        gather(0, SLOW, own_at[0], (SLOW + HALF, True))
+        gather(0, SLOW + HALF, fetched_at[0], (EARLY + HALF, False))
+        place_rounded(0, SLOW, rounded_at)
+        multiply_on_gpsimd(0, SLOW, SLOW, SLOW + HALF)
+        gather(1, SLOW, own_at[1], (EARLY, True))
+        gather(1, EARLY, fetched_at[1], (E, False))
+        place_rounded(0, EARLY, rounded_at + BLOCK)
+        multiply_on_gpsimd(0, SLOW + HALF, SLOW + HALF, EARLY)
+        multiply_on_gpsimd(0, SLOW + HALF, EARLY, EARLY + HALF)
+        gather(LAST_PASS, SLOW, own_at[2], (EARLY, True))
+        gather(0, EARLY + HALF, own_at[0], (EARLY + HALF + 1, False), (E, True))
+        gather(LAST_PASS, EARLY, fetched_at[2], (E, False))
+        place_rounded(1, SLOW, rounded_at + 2 * BLOCK)
+        multiply_on_gpsimd(1, SLOW, SLOW, EARLY)
+        place_rounded(LAST_PASS, SLOW, own_at[1])
+        multiply_on_gpsimd(LAST_PASS, SLOW, SLOW, EARLY)
         spread_gate()
-        multiply(0, 0, EARLY, GROUP)
-        fetch(3)
-        place_rounded(LAST_PASS, OWN - HALF, rounded_at + 4 * BLOCK, HALF)
-        multiply(LAST_PASS, OWN - HALF, OWN - HALF, OWN)
-        place_rounded(1, 0, rounded_at + 3 * BLOCK)
-        multiply(1, 0, 0, HALF)
-        multiply(1, 0, HALF, GROUP)
-        fetch(4)
-        place_rounded(LAST_PASS, 0, own_at + BLOCK)
-        multiply(LAST_PASS, 0, 0, HALF)
-        multiply(LAST_PASS, 0, HALF, GROUP)
-        fetch(5)
+        gather(0, LAST, fetched_at[0], (SLOW, False))
+        place_rounded(1, EARLY, rounded_at + 3 * BLOCK)
+        place_rounded(LAST_PASS, EARLY, small_at + BLOCK)
+        for a in (1, LAST_PASS):
+            multiply(a, EARLY, EARLY + HALF, E)
+            multiply(a, EARLY, EARLY, EARLY + HALF)
+        multiply(0, EARLY + HALF, EARLY + HALF, E)
+        gather(1, LAST, fetched_at[1] - 64, (SLOW, False))
+        gather(LAST_PASS, LAST, fetched_at[2] - 64, (LAST + HALF, False), (SLOW, False))
         open_banks(BANK_GROUPS[:-2])
-        codes_at = [own_at + 4 * BLOCK + a * 5 * GROUP * C for a in range(PASSES)]
+        codes_at = [own_at[2] + a * 5 * GROUP * C for a in range(PASSES)]
         for a in range(PASSES):
-            quantise(a, OWN, E, codes_at[a])
-        quantise(LAST_PASS, OWN - HALF, OWN, rounded_at)
-        quantise(0, 0, GROUP, rounded_at + 2 * BLOCK)
-        quantise(1, 0, GROUP, own_at + 2 * BLOCK)
-        quantise(LAST_PASS, 0, GROUP, rounded_at + BLOCK)
+            quantise(a, SLOW, EARLY, codes_at[a])
+        for a, at in enumerate((rounded_at, rounded_at + 2 * BLOCK, own_at[1])):
+            quantise(a, EARLY, E, at)
         y = placed("y", S, F32, 0)
 
         def finish(e):
@@ -257,26 +249,27 @@ def tile_moe_pre_lin_relu_kernel(tc, xT, w_words, w_scales, b, gate, offs, pos1,
             else:
                 nc.scalar.activation(y[:, e * C : (e + 1) * C], banks[e][0], RELU, bias=bias[:, e : e + 1])
 
-        for first in (OWN, 0):
-            for e in range(first, first + GROUP):
-                finish(e)
-        both = placed("rounded_both", LAST_PASS * PACK * GROUP * C, BF16, own_at)
+        for e in range(SLOW, E):
+            finish(e)
+        both = placed("rounded_both", LAST_PASS * PACK * GROUP * C, BF16, small_at)
         for a in range(LAST_PASS):
-            rounded[a, GROUP] = both[:, a * PACK * GROUP * C : (a + 1) * PACK * GROUP * C]
-            multiply_on_gpsimd(a, GROUP, GROUP, GROUP + HELPED[a], gate_last)
-            multiply(a, GROUP, GROUP + HELPED[a], GROUP + HALF)
-            multiply(a, GROUP, GROUP + HALF, OWN)
+            rounded[a, LAST] = both[:, a * PACK * GROUP * C : (a + 1) * PACK * GROUP * C]
+            multiply_on_gpsimd(a, LAST, LAST, LAST + HELPED[a])
+            multiply(a, LAST, LAST + HELPED[a], LAST + HALF)
+            multiply(a, LAST, LAST + HALF, SLOW)
         for a in range(LAST_PASS):
-            quantise(a, GROUP, OWN, (rounded_at, own_at)[a] + 3 * BLOCK)
+            quantise(a, LAST, SLOW, rounded_at + (2 * a + 1) * BLOCK)
         open_banks(BANK_GROUPS[-2:])
         for a in range(LAST_PASS):
             contract(a, LATE)
-        place_rounded(LAST_PASS, GROUP, own_at + BLOCK, HALF)
-        multiply_on_gpsimd(LAST_PASS, GROUP, GROUP, GROUP + HELPED[LAST_PASS], gate_last)
-        multiply(LAST_PASS, GROUP, GROUP + HELPED[LAST_PASS], GROUP + HALF)
-        quantise(LAST_PASS, 8, 10, codes_at[0])
-        quantise(LAST_PASS, 10, 12, codes_at[1])
-        for e in (12, 13, 14, 15, 8, 9, 10, 11):
+        place_rounded(LAST_PASS, LAST, small_at)
+        multiply_on_gpsimd(LAST_PASS, LAST, LAST, LAST + HELPED[LAST_PASS])
+        multiply(LAST_PASS, LAST, LAST + HELPED[LAST_PASS], LAST + HALF)
+        multiply(LAST_PASS, LAST, LAST + HALF, SLOW)
+        quantise(LAST_PASS, 0, 4, codes_at[0])
+        quantise(LAST_PASS, 4, 6, codes_at[1])
+        quantise(LAST_PASS, 6, 8, codes_at[2])
+        for e in range(LAST, SLOW):
             finish(e)
 
         sums = placed("sums", 4 * T, F32, pass_bytes)

@@ -18,6 +18,8 @@ WIDE = T + 8
 BANK = 2048
 BLOCK = 2 * PACK * GROUP * C
 SLOW, EARLY, LAST = 8, 16, 0
+EXTRA = HALF
+LINE = 4
 HELPED = (3, 2, 2)
 BANK_GROUPS = ((8, 12, 4), (12, 16, 5), (16, 20, 6), (20, 24, 7), (0, 4, 0), (4, 6, 1), (6, 7, 4), (7, 8, 5))
 LATE = (6, 7)
@@ -64,7 +66,7 @@ def tile_moe_pre_lin_relu_kernel(tc, xT, w_words, w_scales, b, gate, offs, pos1,
         nc.scalar.activation(warm[:, 8:9], warm[:, 0:1], RELU)
 
         offs_t = keep.tile([P, S // PER_COLUMN], U16, name="offs_t")
-        gate_slow = keep.tile([P, (GROUP + HALF) * C], F32, name="gate_slow")
+        gate_slow = keep.tile([P, (GROUP + HALF + EXTRA) * C], F32, name="gate_slow")
         gate_last = keep.tile([P, max(HELPED) * C], F32, name="gate_last")
         windows = {}
 
@@ -80,7 +82,7 @@ def tile_moe_pre_lin_relu_kernel(tc, xT, w_words, w_scales, b, gate, offs, pos1,
         load_plane(1, 0)
         nc.sync.dma_start(gate_slow[:, 0 : HALF * C], gate[0:P, SLOW * C : (SLOW + HALF) * C])
         load_plane(1, 1)
-        nc.sync.dma_start(gate_slow[:, HALF * C :], gate[0:P, (SLOW + HALF) * C : (EARLY + HALF) * C])
+        nc.sync.dma_start(gate_slow[:, HALF * C :], gate[0:P, (SLOW + HALF) * C : (EARLY + HALF + EXTRA) * C])
         for r in range(2, PACK):
             load_plane(1, r)
         for r in range(PACK - 1):
@@ -142,9 +144,9 @@ def tile_moe_pre_lin_relu_kernel(tc, xT, w_words, w_scales, b, gate, offs, pos1,
             gate_tile, base = (gate_last, LAST) if e0 < SLOW else (gate_slow, SLOW)
             lo, hi = (e0 - base) * C, (e1 - base) * C
             nc.gpsimd.tensor_tensor(
-                rounded_view(a, e0, e1).rearrange("p (c r) -> p c r", r=PACK),
-                gathered[a, first][:].rearrange("p (r c) -> p c r", r=PACK)[:, (e0 - first) * C : (e1 - first) * C],
-                gate_tile[:, lo:hi].unsqueeze(2).broadcast_to([P, hi - lo, PACK]),
+                rounded_view(a, e0, e1).rearrange("p (c i r) -> p c r i", r=PACK, i=LINE),
+                gathered[a, first][:].rearrange("p (r c i) -> p c r i", r=PACK, i=LINE)[:, (e0 - first) * C // LINE : (e1 - first) * C // LINE],
+                gate_tile[:, lo:hi].rearrange("p (c i) -> p c i", i=LINE).unsqueeze(2).broadcast_to([P, (hi - lo) // LINE, PACK, LINE]),
                 MULT,
             )
 
@@ -189,7 +191,7 @@ def tile_moe_pre_lin_relu_kernel(tc, xT, w_words, w_scales, b, gate, offs, pos1,
         def quantise(a, e0, e1, at):
             count = e1 - e0
             words = placed("words%d_%d" % (a, e0), count * C, U32, at)
-            scale_bytes = placed("bytes%d_%d" % (a, e0), count * C, U8, at + 4 * GROUP * C)
+            scale_bytes = placed("bytes%d_%d" % (a, e0), count * C, U8, at + 4 * count * C)
             nc.vector.quantize_mx(words[:].bitcast(FP8X4), scale_bytes[:], rounded_view(a, e0, e1))
             for e in range(e0, e1):
                 codes[a, e] = (words[:, (e - e0) * C : (e - e0 + 1) * C], scale_bytes[:, (e - e0) * C : (e - e0 + 1) * C])
@@ -219,10 +221,12 @@ def tile_moe_pre_lin_relu_kernel(tc, xT, w_words, w_scales, b, gate, offs, pos1,
         multiply_on_gpsimd(0, SLOW + HALF, SLOW + HALF, EARLY)
         multiply_on_gpsimd(0, SLOW + HALF, EARLY, EARLY + HALF)
         gather(LAST_PASS, SLOW, own_at[2], (EARLY, True))
-        gather(0, EARLY + HALF, own_at[0], (EARLY + HALF + 1, False), (E, True))
+        gather(0, EARLY + HALF, own_at[0], (E, True))
+        gather(LAST_PASS, SLOW - 1, rounded_at + 4 * BLOCK, (SLOW, True))
         gather(LAST_PASS, EARLY, fetched_at[2], (E, False))
         place_rounded(1, SLOW, rounded_at + 2 * BLOCK)
         multiply_on_gpsimd(1, SLOW, SLOW, EARLY)
+        multiply_on_gpsimd(0, EARLY + HALF, EARLY + HALF, EARLY + HALF + EXTRA)
         place_rounded(LAST_PASS, SLOW, own_at[1])
         multiply_on_gpsimd(LAST_PASS, SLOW, SLOW, EARLY)
         spread_gate()
@@ -232,13 +236,15 @@ def tile_moe_pre_lin_relu_kernel(tc, xT, w_words, w_scales, b, gate, offs, pos1,
         for a in (1, LAST_PASS):
             multiply(a, EARLY, EARLY + HALF, E)
             multiply(a, EARLY, EARLY, EARLY + HALF)
-        multiply(0, EARLY + HALF, EARLY + HALF, E)
+        place_rounded(LAST_PASS, SLOW - 1, rounded_at + 4 * BLOCK + BLOCK // 4, 1)
+        multiply(LAST_PASS, SLOW - 1, SLOW - 1, SLOW)
         gather(1, LAST, fetched_at[1] - 64, (SLOW, False))
-        gather(LAST_PASS, LAST, fetched_at[2] - 64, (LAST + HALF, False), (SLOW, False))
+        gather(LAST_PASS, LAST, fetched_at[2] - 64, (LAST + HALF, False), (SLOW - 1, False))
         open_banks(BANK_GROUPS[:-2])
         codes_at = [own_at[2] + a * 5 * GROUP * C for a in range(PASSES)]
         for a in range(PASSES):
             quantise(a, SLOW, EARLY, codes_at[a])
+        quantise(LAST_PASS, SLOW - 1, SLOW, own_at[2] + PASSES * 5 * GROUP * C)
         for a, at in enumerate((rounded_at, rounded_at + 2 * BLOCK, own_at[1])):
             quantise(a, EARLY, E, at)
         y = placed("y", S, F32, 0)
@@ -262,14 +268,15 @@ def tile_moe_pre_lin_relu_kernel(tc, xT, w_words, w_scales, b, gate, offs, pos1,
         open_banks(BANK_GROUPS[-2:])
         for a in range(LAST_PASS):
             contract(a, LATE)
-        place_rounded(LAST_PASS, LAST, small_at)
+        contract(LAST_PASS, LATE[1:])
+        place_rounded(LAST_PASS, LAST, small_at, GROUP - 1)
         multiply_on_gpsimd(LAST_PASS, LAST, LAST, LAST + HELPED[LAST_PASS])
         multiply(LAST_PASS, LAST, LAST + HELPED[LAST_PASS], LAST + HALF)
-        multiply(LAST_PASS, LAST, LAST + HALF, SLOW)
+        multiply(LAST_PASS, LAST, LAST + HALF, SLOW - 1)
         quantise(LAST_PASS, 0, 4, codes_at[0])
         quantise(LAST_PASS, 4, 6, codes_at[1])
-        quantise(LAST_PASS, 6, 8, codes_at[2])
-        for e in range(LAST, SLOW):
+        quantise(LAST_PASS, 6, 7, codes_at[2])
+        for e in (7, 0, 1, 2, 3, 4, 5, 6):
             finish(e)
 
         sums = placed("sums", 4 * T, F32, pass_bytes)

@@ -18,9 +18,9 @@ WIDE = T + 8
 BANK = 2048
 BLOCK = 2 * PACK * GROUP * C
 SLOW, EARLY, LAST = 8, 16, 0
-EXTRA = HALF
+EXTRA = 3
 LINE = 4
-HELPED = (3, 2, 2)
+HELPED = (4, 1, 2)
 BANK_GROUPS = ((8, 12, 4), (12, 16, 5), (16, 20, 6), (20, 24, 7), (0, 4, 0), (4, 6, 1), (6, 7, 4), (7, 8, 5))
 LATE = (6, 7)
 
@@ -236,6 +236,7 @@ def tile_moe_pre_lin_relu_kernel(tc, xT, w_words, w_scales, b, gate, offs, pos1,
         for a in (1, LAST_PASS):
             multiply(a, EARLY, EARLY + HALF, E)
             multiply(a, EARLY, EARLY, EARLY + HALF)
+        multiply(0, EARLY + HALF, EARLY + HALF + EXTRA, E)
         place_rounded(LAST_PASS, SLOW - 1, rounded_at + 4 * BLOCK + BLOCK // 4, 1)
         multiply(LAST_PASS, SLOW - 1, SLOW - 1, SLOW)
         gather(1, LAST, fetched_at[1] - 64, (SLOW, False))
@@ -261,7 +262,8 @@ def tile_moe_pre_lin_relu_kernel(tc, xT, w_words, w_scales, b, gate, offs, pos1,
         for a in range(LAST_PASS):
             rounded[a, LAST] = both[:, a * PACK * GROUP * C : (a + 1) * PACK * GROUP * C]
             multiply_on_gpsimd(a, LAST, LAST, LAST + HELPED[a])
-            multiply(a, LAST, LAST + HELPED[a], LAST + HALF)
+            if HELPED[a] < HALF:
+                multiply(a, LAST, LAST + HELPED[a], LAST + HALF)
             multiply(a, LAST, LAST + HALF, SLOW)
         for a in range(LAST_PASS):
             quantise(a, LAST, SLOW, rounded_at + (2 * a + 1) * BLOCK)

@@ -11,18 +11,24 @@ K_PASS = P * PACK
 PASSES = K // K_PASS
 LAST_PASS = PASSES - 1
 PER_COLUMN = 16
-RUN = 2
-GROUP = 8
-HALF = GROUP // 2
 WIDE = T + 8
 BANK = 2048
-BLOCK = 2 * PACK * GROUP * C
-SLOW, EARLY, LAST = 8, 16, 0
-EXTRA = 3
-LINE = 4
-HELPED = (4, 1, 2)
-BANK_GROUPS = ((8, 12, 4), (12, 16, 5), (16, 20, 6), (20, 24, 7), (0, 4, 0), (4, 6, 1), (6, 7, 4), (7, 8, 5))
-LATE = (6, 7)
+QUAD = 4 * C
+GROUP = 2 * QUAD
+BLOCK = 2 * PACK * GROUP
+CODES = 5 * GROUP
+EDGE = 64
+
+LAST, SLOW, MIDDLE = 0, GROUP, 2 * GROUP
+SCALAR_END = MIDDLE + QUAD - 64
+GPSIMD_END = MIDDLE + QUAD + 2 * C
+HELPED = (QUAD, C, 2 * C)
+LAST_CUT = 6 * C
+VECTOR_RUN = 2
+GPSIMD_RUN = 4
+BANK_GROUPS = ((8, 12, 4), (12, 16, 5), (16, 20, 6), (20, 24, 7), (0, 4, 0), (4, 6, 1))
+LATE_GROUPS = ((6, 7, 4), (7, 8, 5))
+TWICE, ALONE, STORE_CUT = 256, 448, 800
 
 FLOPS = 2 * K * S * N
 BYTES = 4 * K * T + E * K * N + E * K * N // 32 + 4 * N * E + 4 * S + 2 * P * (S + 3 * T) // PER_COLUMN + 4 * N * T
@@ -55,23 +61,26 @@ def tile_moe_pre_lin_relu_kernel(tc, xT, w_words, w_scales, b, gate, offs, pos1,
         def placed(name, columns, dtype, offset):
             return stage.tile([P, columns], dtype, name=name, offset=offset, align_bytes=64)
 
-        pass_bytes = PACK * 4 * WIDE + 128
-        small_at = PASSES * pass_bytes
-        own_at = (small_at, small_at + 2 * BLOCK, small_at + 6 * BLOCK)
-        fetched_at = (small_at + 10 * BLOCK, small_at + 4 * BLOCK, small_at + 8 * BLOCK)
-        rounded_at = small_at + 12 * BLOCK
+        window_bytes = 4 * WIDE + 32
+        pass_bytes = PACK * window_bytes
+        first_at = PASSES * pass_bytes
+        middle_at = first_at + 4 * PACK * (S - SCALAR_END)
+        late_at = middle_at - BLOCK
+        own_at = (middle_at + BLOCK, middle_at + 5 * BLOCK)
+        fetched_at = (middle_at + 9 * BLOCK, middle_at + 3 * BLOCK, middle_at + 7 * BLOCK)
+        rounded_at = [middle_at + (11 + q) * BLOCK for q in range(4)]
 
         warm = keep.tile([P, 16], F32, name="warm")
         nc.gpsimd.memset(warm[:, 0:8], 0.0)
         nc.scalar.activation(warm[:, 8:9], warm[:, 0:1], RELU)
 
         offs_t = keep.tile([P, S // PER_COLUMN], U16, name="offs_t")
-        gate_slow = keep.tile([P, (GROUP + HALF + EXTRA) * C], F32, name="gate_slow")
-        gate_last = keep.tile([P, max(HELPED) * C], F32, name="gate_last")
+        gate_slow = keep.tile([P, GPSIMD_END - SLOW], F32, name="gate_slow")
+        gate_last = keep.tile([P, max(HELPED)], F32, name="gate_last")
         windows = {}
 
         def load_plane(a, r):
-            window = placed("window%d_%d" % (a, r), WIDE, F32, a * pass_bytes + r * (4 * WIDE + 32))
+            window = placed("window%d_%d" % (a, r), WIDE, F32, a * pass_bytes + r * window_bytes)
             nc.sync.dma_start(window[:, 0:T], xT[K_PASS * a + r : K_PASS * (a + 1) : PACK, :])
             windows[a, r] = window
 
@@ -80,9 +89,9 @@ def tile_moe_pre_lin_relu_kernel(tc, xT, w_words, w_scales, b, gate, offs, pos1,
         for r in range(1, PACK):
             load_plane(0, r)
         load_plane(1, 0)
-        nc.sync.dma_start(gate_slow[:, 0 : HALF * C], gate[0:P, SLOW * C : (SLOW + HALF) * C])
+        nc.sync.dma_start(gate_slow[:, 0:QUAD], gate[0:P, SLOW : SLOW + QUAD])
         load_plane(1, 1)
-        nc.sync.dma_start(gate_slow[:, HALF * C :], gate[0:P, (SLOW + HALF) * C : (EARLY + HALF + EXTRA) * C])
+        nc.sync.dma_start(gate_slow[:, QUAD:], gate[0:P, SLOW + QUAD : GPSIMD_END])
         for r in range(2, PACK):
             load_plane(1, r)
         for r in range(PACK - 1):
@@ -105,7 +114,7 @@ def tile_moe_pre_lin_relu_kernel(tc, xT, w_words, w_scales, b, gate, offs, pos1,
                 w_words[:, a].rearrange("e p n r -> p e (n r)").bitcast(I32),
             )
             w_tiles.append(w_tile)
-        nc.sync.dma_start(gate_last[:], gate[0:P, LAST * C : (LAST + max(HELPED)) * C])
+        nc.sync.dma_start(gate_last[:], gate[0:P, LAST : LAST + max(HELPED)])
         bias = keep.tile([P, E], F32, name="bias")
         nc.sync.dma_start(bias[:], b)
         pos_t = []
@@ -116,91 +125,74 @@ def tile_moe_pre_lin_relu_kernel(tc, xT, w_words, w_scales, b, gate, offs, pos1,
 
         gathered = {}
 
-        def gather(a, e0, at, *parts):
-            width = (parts[-1][0] - e0) * C
-            gathered[a, e0] = placed("gathered%d_%d" % (a, e0), PACK * width, F32, at)
-            lo = 0
-            for end, on_vector in parts:
-                hi = (end - e0) * C
-                for r in range(PACK):
-                    values = gathered[a, e0][:, r * width + lo : r * width + hi]
-                    looked_up = windows[a, r][:].indirect(entries(offs_t, e0 * C + lo, e0 * C + hi))
-                    if on_vector:
-                        nc.vector.tensor_copy(values, looked_up)
-                    else:
-                        nc.scalar.activation(values, looked_up, COPY)
-                lo = hi
+        def gather(a, on_vector, at, lo, hi):
+            width = hi - lo
+            gathered[a, lo] = placed("gathered%d_%d" % (a, lo), PACK * width, F32, at)
+            for r in range(PACK):
+                values = gathered[a, lo][:, r * width : (r + 1) * width]
+                looked_up = windows[a, r][:].indirect(entries(offs_t, lo, hi))
+                if on_vector:
+                    nc.vector.tensor_copy(values, looked_up)
+                else:
+                    nc.scalar.activation(values, looked_up, COPY)
 
         rounded = {}
 
-        def rounded_view(a, e0, e1):
-            first = max(f for (pass_of, f) in rounded if pass_of == a and f <= e0)
-            return rounded[a, first][:, PACK * (e0 - first) * C : PACK * (e1 - first) * C]
+        def place_rounded(a, group, at):
+            rounded[a, group] = placed("rounded%d_%d" % (a, group), PACK * GROUP, BF16, at)
 
-        def place_rounded(a, first, at, experts=GROUP):
-            rounded[a, first] = placed("rounded%d_%d" % (a, first), PACK * experts * C, BF16, at)
+        def rounded_view(a, lo, hi):
+            group = lo // GROUP * GROUP
+            return rounded[a, group][:, PACK * (lo - group) : PACK * (hi - group)]
 
-        def multiply_on_gpsimd(a, first, e0, e1):
-            gate_tile, base = (gate_last, LAST) if e0 < SLOW else (gate_slow, SLOW)
-            lo, hi = (e0 - base) * C, (e1 - base) * C
-            nc.gpsimd.tensor_tensor(
-                rounded_view(a, e0, e1).rearrange("p (c i r) -> p c r i", r=PACK, i=LINE),
-                gathered[a, first][:].rearrange("p (r c i) -> p c r i", r=PACK, i=LINE)[:, (e0 - first) * C // LINE : (e1 - first) * C // LINE],
-                gate_tile[:, lo:hi].rearrange("p (c i) -> p c i", i=LINE).unsqueeze(2).broadcast_to([P, (hi - lo) // LINE, PACK, LINE]),
+        def product(engine, run, a, first, lo, hi, gates):
+            engine.tensor_tensor(
+                rounded_view(a, lo, hi).rearrange("p (c i r) -> p c r i", r=PACK, i=run),
+                gathered[a, first][:].rearrange("p (r c i) -> p c r i", r=PACK, i=run)[:, (lo - first) // run : (hi - first) // run],
+                gates.rearrange("p (c i) -> p c i", i=run).unsqueeze(2).broadcast_to([P, (hi - lo) // run, PACK, run]),
                 MULT,
             )
 
-        identity = keep.tile([P, P], F32, name="identity")
-        make_identity(nc, identity[:])
-        turned = psum.tile([P, P], F32, name="turned", offset=4 * BANK)
-        gate_columns = keep.tile([P, E], F32, name="gate_columns")
+        def multiply_on_gpsimd(a, first, lo, hi):
+            gate_tile, base = (gate_last, LAST) if lo < SLOW else (gate_slow, SLOW)
+            product(nc.gpsimd, GPSIMD_RUN, a, first, lo, hi, gate_tile[:, lo - base : hi - base])
+
         gate_banks = {}
 
-        def spread_gate():
-            nc.tensor.transpose(turned[:], gate_rows[:], identity[:])
-            nc.vector.tensor_copy(gate_columns[:], turned[:, 0:E])
-            for index, first in enumerate((EARLY + HALF, EARLY, LAST, LAST + HALF)):
-                gate_bank = psum.tile([P, HALF * C], F32, name="gate_bank%d" % first, offset=index * BANK)
-                for j in range(HALF):
-                    e = first + j
-                    nc.tensor.transpose(gate_bank[:, j * C : (j + 1) * C], gate_columns[:, e : e + 1].to_broadcast([P, P]), identity[:])
-                gate_banks[first // HALF] = gate_bank
+        def multiply(a, first, *cuts):
+            for lo, hi in zip(cuts[:-1], cuts[1:]):
+                base = lo // QUAD * QUAD
+                product(nc.vector, VECTOR_RUN, a, first, lo, hi, gate_banks[base][:, lo - base : hi - base])
 
-        def multiply(a, first, e0, e1):
-            runs = (e1 - e0) * C // RUN
-            lo = e0 % HALF * C
-            nc.vector.tensor_tensor(
-                rounded_view(a, e0, e1).rearrange("p (c i r) -> p c r i", r=PACK, i=RUN),
-                gathered[a, first][:].rearrange("p (r c i) -> p c r i", r=PACK, i=RUN)[:, (e0 - first) * C // RUN : (e1 - first) * C // RUN],
-                gate_banks[e0 // HALF][:, lo : lo + (e1 - e0) * C].rearrange("p (c i) -> p c i", i=RUN).unsqueeze(2).broadcast_to([P, runs, PACK, RUN]),
-                MULT,
-            )
+        def spread_gate():
+            identity = keep.tile([P, P], F32, name="identity")
+            make_identity(nc, identity[:])
+            turned = psum.tile([P, P], F32, name="turned", offset=4 * BANK)
+            nc.tensor.transpose(turned[:], gate_rows[:], identity[:])
+            gate_columns = keep.tile([P, E], F32, name="gate_columns")
+            nc.vector.tensor_copy(gate_columns[:], turned[:, 0:E])
+            for index, base in enumerate((MIDDLE + QUAD, MIDDLE, LAST, LAST + QUAD)):
+                gate_banks[base] = psum.tile([P, QUAD], F32, name="gate_bank%d" % index, offset=index * BANK)
+                for lo in range(0, QUAD, C):
+                    e = (base + lo) // C
+                    nc.tensor.transpose(gate_banks[base][:, lo : lo + C], gate_columns[:, e : e + 1].to_broadcast([P, P]), identity[:])
 
         banks = {}
+        issued = {}
 
         def open_banks(groups):
             for first, end, index in groups:
                 bank = psum.tile([P, (end - first) * C], F32, name="bank%d" % first, offset=index * BANK)
+                issued[first] = 0
                 for e in range(first, end):
                     banks[e] = (bank[:, (e - first) * C : (e - first + 1) * C], first, PASSES * (end - first))
 
-
         codes = {}
-        issued = {}
-
-        def quantise(a, e0, e1, at):
-            count = e1 - e0
-            words = placed("words%d_%d" % (a, e0), count * C, U32, at)
-            scale_bytes = placed("bytes%d_%d" % (a, e0), count * C, U8, at + 4 * count * C)
-            nc.vector.quantize_mx(words[:].bitcast(FP8X4), scale_bytes[:], rounded_view(a, e0, e1))
-            for e in range(e0, e1):
-                codes[a, e] = (words[:, (e - e0) * C : (e - e0 + 1) * C], scale_bytes[:, (e - e0) * C : (e - e0 + 1) * C])
-            contract(a, [e for e in range(e0, e1) if e in banks])
 
         def contract(a, experts):
             for e in experts:
                 acc, first, total = banks[e]
-                issued[first] = issued.get(first, 0) + 1
+                issued[first] = issued[first] + 1
                 nc.tensor.matmul_mx(
                     acc,
                     lhsT=w_tiles[a][:, e * N : (e + 1) * N].bitcast(FP8X4),
@@ -211,83 +203,92 @@ def tile_moe_pre_lin_relu_kernel(tc, xT, w_words, w_scales, b, gate, offs, pos1,
                     stop=issued[first] == total,
                 )
 
-        gather(0, SLOW, own_at[0], (SLOW + HALF, True))
-        gather(0, SLOW + HALF, fetched_at[0], (EARLY + HALF, False))
-        place_rounded(0, SLOW, rounded_at)
-        multiply_on_gpsimd(0, SLOW, SLOW, SLOW + HALF)
-        gather(1, SLOW, own_at[1], (EARLY, True))
-        gather(1, EARLY, fetched_at[1], (E, False))
-        place_rounded(0, EARLY, rounded_at + BLOCK)
-        multiply_on_gpsimd(0, SLOW + HALF, SLOW + HALF, EARLY)
-        multiply_on_gpsimd(0, SLOW + HALF, EARLY, EARLY + HALF)
-        gather(LAST_PASS, SLOW, own_at[2], (EARLY, True))
-        gather(0, EARLY + HALF, own_at[0], (E, True))
-        gather(LAST_PASS, SLOW - 1, rounded_at + 4 * BLOCK, (SLOW, True))
-        gather(LAST_PASS, EARLY, fetched_at[2], (E, False))
-        place_rounded(1, SLOW, rounded_at + 2 * BLOCK)
-        multiply_on_gpsimd(1, SLOW, SLOW, EARLY)
-        multiply_on_gpsimd(0, EARLY + HALF, EARLY + HALF, EARLY + HALF + EXTRA)
-        place_rounded(LAST_PASS, SLOW, own_at[1])
-        multiply_on_gpsimd(LAST_PASS, SLOW, SLOW, EARLY)
+        def quantise(a, lo, hi, at):
+            words = placed("words%d_%d" % (a, lo), hi - lo, U32, at)
+            scale_bytes = placed("bytes%d_%d" % (a, lo), hi - lo, U8, at + 4 * (hi - lo))
+            nc.vector.quantize_mx(words[:].bitcast(FP8X4), scale_bytes[:], rounded_view(a, lo, hi))
+            for slot in range(lo, hi, C):
+                codes[a, slot // C] = (words[:, slot - lo : slot - lo + C], scale_bytes[:, slot - lo : slot - lo + C])
+            contract(a, [e for e in range(lo // C, hi // C) if e in banks])
+
+        gather(0, True, first_at, SLOW, SLOW + QUAD)
+        gather(0, False, fetched_at[0], SLOW + QUAD, SCALAR_END)
+        place_rounded(0, SLOW, rounded_at[0])
+        multiply_on_gpsimd(0, SLOW, SLOW, SLOW + QUAD)
+        gather(1, True, own_at[0], SLOW, MIDDLE)
+        gather(1, False, fetched_at[1], MIDDLE, S)
+        place_rounded(0, MIDDLE, rounded_at[1])
+        multiply_on_gpsimd(0, SLOW + QUAD, SLOW + QUAD, MIDDLE)
+        multiply_on_gpsimd(0, SLOW + QUAD, MIDDLE, SCALAR_END)
+        gather(LAST_PASS, True, own_at[1], SLOW, MIDDLE)
+        gather(0, True, first_at, SCALAR_END, S)
+        gather(LAST_PASS, False, fetched_at[2], MIDDLE, S)
+        place_rounded(1, SLOW, rounded_at[2])
+        multiply_on_gpsimd(1, SLOW, SLOW, MIDDLE)
+        multiply_on_gpsimd(0, SCALAR_END, SCALAR_END, GPSIMD_END)
+        place_rounded(LAST_PASS, SLOW, own_at[0])
+        multiply_on_gpsimd(LAST_PASS, SLOW, SLOW, MIDDLE)
         spread_gate()
-        gather(0, LAST, fetched_at[0], (SLOW, False))
-        place_rounded(1, EARLY, rounded_at + 3 * BLOCK)
-        place_rounded(LAST_PASS, EARLY, small_at + BLOCK)
+        gather(0, False, fetched_at[0], LAST, SLOW)
+        place_rounded(1, MIDDLE, rounded_at[3])
+        place_rounded(LAST_PASS, MIDDLE, middle_at)
         for a in (1, LAST_PASS):
-            multiply(a, EARLY, EARLY + HALF, E)
-            multiply(a, EARLY, EARLY, EARLY + HALF)
-        multiply(0, EARLY + HALF, EARLY + HALF + EXTRA, E)
-        place_rounded(LAST_PASS, SLOW - 1, rounded_at + 4 * BLOCK + BLOCK // 4, 1)
-        multiply(LAST_PASS, SLOW - 1, SLOW - 1, SLOW)
-        gather(1, LAST, fetched_at[1] - 64, (SLOW, False))
-        gather(LAST_PASS, LAST, fetched_at[2] - 64, (LAST + HALF, False), (SLOW - 1, False))
-        open_banks(BANK_GROUPS[:-2])
-        codes_at = [own_at[2] + a * 5 * GROUP * C for a in range(PASSES)]
+            multiply(a, MIDDLE, MIDDLE + QUAD, S)
+            multiply(a, MIDDLE, MIDDLE, MIDDLE + QUAD)
+        multiply(0, SCALAR_END, GPSIMD_END, S)
+        gather(1, False, fetched_at[1] - EDGE, LAST, SLOW)
+        gather(LAST_PASS, False, fetched_at[2] - EDGE, LAST, LAST_CUT)
+
+        open_banks(BANK_GROUPS)
+        codes_at = [own_at[1] + a * CODES for a in range(PASSES)]
         for a in range(PASSES):
-            quantise(a, SLOW, EARLY, codes_at[a])
-        quantise(LAST_PASS, SLOW - 1, SLOW, own_at[2] + PASSES * 5 * GROUP * C)
-        for a, at in enumerate((rounded_at, rounded_at + 2 * BLOCK, own_at[1])):
-            quantise(a, EARLY, E, at)
+            quantise(a, SLOW, MIDDLE, codes_at[a])
+        for a, at in enumerate((rounded_at[0], rounded_at[2], own_at[0])):
+            quantise(a, MIDDLE, S, at)
         y = placed("y", S, F32, 0)
 
-        def finish(e):
-            if e == LATE[0]:
+        def finish(e, on_vector):
+            if on_vector:
                 nc.vector.tensor_scalar(y[:, e * C : (e + 1) * C], banks[e][0], bias[:, e : e + 1], 0.0, ADD, MAX)
             else:
                 nc.scalar.activation(y[:, e * C : (e + 1) * C], banks[e][0], RELU, bias=bias[:, e : e + 1])
 
-        for e in range(SLOW, E):
-            finish(e)
-        both = placed("rounded_both", LAST_PASS * PACK * GROUP * C, BF16, small_at)
+        between = (8, 20)
+        for e in range(SLOW // C, MIDDLE // C):
+            finish(e, e == between[0])
+        gather(LAST_PASS, False, codes_at[LAST_PASS], LAST_CUT, SLOW)
+        for e in range(MIDDLE // C, between[1]):
+            finish(e, False)
+
+        both = placed("rounded_both", LAST_PASS * PACK * GROUP, BF16, late_at)
         for a in range(LAST_PASS):
-            rounded[a, LAST] = both[:, a * PACK * GROUP * C : (a + 1) * PACK * GROUP * C]
-            multiply_on_gpsimd(a, LAST, LAST, LAST + HELPED[a])
-            if HELPED[a] < HALF:
-                multiply(a, LAST, LAST + HELPED[a], LAST + HALF)
-            multiply(a, LAST, LAST + HALF, SLOW)
+            rounded[a, LAST] = both[:, a * PACK * GROUP : (a + 1) * PACK * GROUP]
+            multiply_on_gpsimd(a, LAST, LAST, HELPED[a])
+            multiply(a, LAST, *sorted({HELPED[a], QUAD, SLOW}))
         for a in range(LAST_PASS):
-            quantise(a, LAST, SLOW, rounded_at + (2 * a + 1) * BLOCK)
-        open_banks(BANK_GROUPS[-2:])
+            quantise(a, LAST, SLOW, rounded_at[2 * a + 1])
+        for e in range(between[1], E):
+            finish(e, e == between[1])
+        open_banks(LATE_GROUPS)
         for a in range(LAST_PASS):
-            contract(a, LATE)
-        contract(LAST_PASS, LATE[1:])
-        place_rounded(LAST_PASS, LAST, small_at, GROUP - 1)
-        multiply_on_gpsimd(LAST_PASS, LAST, LAST, LAST + HELPED[LAST_PASS])
-        multiply(LAST_PASS, LAST, LAST + HELPED[LAST_PASS], LAST + HALF)
-        multiply(LAST_PASS, LAST, LAST + HALF, SLOW - 1)
-        quantise(LAST_PASS, 0, 4, codes_at[0])
-        quantise(LAST_PASS, 4, 6, codes_at[1])
-        quantise(LAST_PASS, 6, 7, codes_at[2])
-        for e in (7, 0, 1, 2, 3, 4, 5, 6):
-            finish(e)
+            contract(a, [first for first, end, index in LATE_GROUPS])
+
+        place_rounded(LAST_PASS, LAST, late_at)
+        multiply_on_gpsimd(LAST_PASS, LAST, LAST, HELPED[LAST_PASS])
+        multiply(LAST_PASS, LAST, HELPED[LAST_PASS], QUAD, LAST_CUT)
+        multiply(LAST_PASS, LAST_CUT, LAST_CUT, SLOW)
+        for at, (lo, hi) in zip(codes_at, ((LAST, QUAD), (QUAD, QUAD + 2 * C), (QUAD + 2 * C, SLOW))):
+            quantise(LAST_PASS, lo, hi, at)
+        for e in range(LAST // C, SLOW // C):
+            finish(e, e == LATE_GROUPS[0][0])
 
         sums = placed("sums", 4 * T, F32, pass_bytes)
 
         def looked_up(choice, lo, hi):
             return y[:].indirect(entries(pos_t[choice], lo, hi))
 
-        def part(index, lo, hi):
-            return sums[:, index * T + lo : index * T + hi]
+        def part(row, lo, hi):
+            return sums[:, row * T + lo : row * T + hi]
 
         def fetch_on_scalar(choice, lo, hi):
             nc.scalar.activation(part(choice, lo, hi), looked_up(choice, lo, hi), COPY)
@@ -295,23 +296,22 @@ def tile_moe_pre_lin_relu_kernel(tc, xT, w_words, w_scales, b, gate, offs, pos1,
         def fetch_and_add(target, choice, source, lo, hi):
             nc.vector.tensor_tensor(part(target, lo, hi), looked_up(choice, lo, hi), part(source, lo, hi), ADD)
 
-        def add_and_store(lo, hi, other):
+        def add_last(other, lo, hi):
             nc.vector.tensor_tensor(part(3, lo, hi), part(2, lo, hi), part(other, lo, hi), ADD)
-            nc.sync.dma_start(out[:, lo:hi], part(3, lo, hi))
 
-        t1, t2, t3 = 256, 448, 800
-        fetch_on_scalar(0, 0, t1)
-        fetch_on_scalar(0, t1, t3)
-        fetch_on_scalar(1, t2, t3)
-        fetch_on_scalar(0, t3, T)
-        fetch_on_scalar(1, t3, T)
-        nc.vector.tensor_copy(part(1, t1, t2), looked_up(2, t1, t2))
-        fetch_and_add(1, 1, 0, 0, t1)
-        fetch_and_add(2, 1, 1, t1, t2)
-        fetch_and_add(3, 2, 1, 0, t1)
-        nc.vector.tensor_tensor(part(3, t1, t2), part(2, t1, t2), part(0, t1, t2), ADD)
-        nc.sync.dma_start(out[:, 0:t2], part(3, 0, t2))
-        fetch_and_add(2, 2, 0, t2, t3)
-        fetch_and_add(2, 2, 0, t3, T)
-        add_and_store(t2, t3, 1)
-        add_and_store(t3, T, 1)
+        fetch_on_scalar(0, 0, TWICE)
+        fetch_on_scalar(0, TWICE, STORE_CUT)
+        fetch_on_scalar(1, ALONE, STORE_CUT)
+        fetch_on_scalar(0, STORE_CUT, T)
+        fetch_on_scalar(1, STORE_CUT, T)
+        nc.vector.tensor_copy(part(1, TWICE, ALONE), looked_up(2, TWICE, ALONE))
+        fetch_and_add(1, 1, 0, 0, TWICE)
+        fetch_and_add(2, 1, 1, TWICE, ALONE)
+        fetch_and_add(3, 2, 1, 0, TWICE)
+        add_last(0, TWICE, ALONE)
+        nc.sync.dma_start(out[:, 0:ALONE], part(3, 0, ALONE))
+        fetch_and_add(2, 2, 0, ALONE, STORE_CUT)
+        fetch_and_add(2, 2, 0, STORE_CUT, T)
+        for lo, hi in ((ALONE, STORE_CUT), (STORE_CUT, T)):
+            add_last(1, lo, hi)
+            nc.sync.dma_start(out[:, lo:hi], part(3, lo, hi))

@@ -20,14 +20,12 @@ CODES = 5 * GROUP
 EDGE = 64
 
 LAST, SLOW, MIDDLE = 0, GROUP, 2 * GROUP
-SCALAR_END = MIDDLE + QUAD - 64
-GPSIMD_END = MIDDLE + QUAD + 2 * C
-HELPED = (QUAD, C, 2 * C)
-LAST_CUT = 6 * C
+GPSIMD_END = S
+HELPED = (QUAD, C, C)
 VECTOR_RUN = 2
 GPSIMD_RUN = 4
-BANK_GROUPS = ((8, 12, 4), (12, 16, 5), (16, 20, 6), (20, 24, 7), (0, 4, 0), (4, 6, 1))
-LATE_GROUPS = ((6, 7, 4), (7, 8, 5))
+EARLY_BANKS = ((8, 12, 4), (12, 16, 5), (16, 20, 6), (20, 24, 7), (4, 8, 2))
+LAST_BANKS = ((0, 2, 3), (2, 4, 0))
 TWICE, ALONE, STORE_CUT = 256, 448, 800
 
 FLOPS = 2 * K * S * N
@@ -64,11 +62,10 @@ def tile_moe_pre_lin_relu_kernel(tc, xT, w_words, w_scales, b, gate, offs, pos1,
         window_bytes = 4 * WIDE + 32
         pass_bytes = PACK * window_bytes
         first_at = PASSES * pass_bytes
-        middle_at = first_at + 4 * PACK * (S - SCALAR_END)
-        late_at = middle_at - BLOCK
+        middle_at = first_at + BLOCK
         own_at = (middle_at + BLOCK, middle_at + 5 * BLOCK)
         fetched_at = (middle_at + 9 * BLOCK, middle_at + 3 * BLOCK, middle_at + 7 * BLOCK)
-        rounded_at = [middle_at + (11 + q) * BLOCK for q in range(4)]
+        rounded_at = [middle_at + (11 + q) * BLOCK for q in range(5)]
 
         warm = keep.tile([P, 16], F32, name="warm")
         nc.gpsimd.memset(warm[:, 0:8], 0.0)
@@ -138,12 +135,14 @@ def tile_moe_pre_lin_relu_kernel(tc, xT, w_words, w_scales, b, gate, offs, pos1,
 
         rounded = {}
 
-        def place_rounded(a, group, at):
-            rounded[a, group] = placed("rounded%d_%d" % (a, group), PACK * GROUP, BF16, at)
+        def place_rounded(a, lo, hi, at):
+            tile = placed("rounded%d_%d" % (a, lo), PACK * (hi - lo), BF16, at)
+            for base in range(lo, hi, QUAD):
+                rounded[a, base] = (tile[:], lo)
 
         def rounded_view(a, lo, hi):
-            group = lo // GROUP * GROUP
-            return rounded[a, group][:, PACK * (lo - group) : PACK * (hi - group)]
+            tile, first = rounded[a, lo // QUAD * QUAD]
+            return tile[:, PACK * (lo - first) : PACK * (hi - first)]
 
         def product(engine, run, a, first, lo, hi, gates):
             engine.tensor_tensor(
@@ -171,7 +170,7 @@ def tile_moe_pre_lin_relu_kernel(tc, xT, w_words, w_scales, b, gate, offs, pos1,
             nc.tensor.transpose(turned[:], gate_rows[:], identity[:])
             gate_columns = keep.tile([P, E], F32, name="gate_columns")
             nc.vector.tensor_copy(gate_columns[:], turned[:, 0:E])
-            for index, base in enumerate((MIDDLE + QUAD, MIDDLE, LAST, LAST + QUAD)):
+            for index, base in enumerate((LAST + QUAD, LAST, MIDDLE, MIDDLE + QUAD)):
                 gate_banks[base] = psum.tile([P, QUAD], F32, name="gate_bank%d" % index, offset=index * BANK)
                 for lo in range(0, QUAD, C):
                     e = (base + lo) // C
@@ -209,78 +208,73 @@ def tile_moe_pre_lin_relu_kernel(tc, xT, w_words, w_scales, b, gate, offs, pos1,
             nc.vector.quantize_mx(words[:].bitcast(FP8X4), scale_bytes[:], rounded_view(a, lo, hi))
             for slot in range(lo, hi, C):
                 codes[a, slot // C] = (words[:, slot - lo : slot - lo + C], scale_bytes[:, slot - lo : slot - lo + C])
-            contract(a, [e for e in range(lo // C, hi // C) if e in banks])
+            contract(a, range(lo // C, hi // C))
 
         gather(0, True, first_at, SLOW, SLOW + QUAD)
-        gather(0, False, fetched_at[0], SLOW + QUAD, SCALAR_END)
-        place_rounded(0, SLOW, rounded_at[0])
+        gather(0, False, fetched_at[0], SLOW + QUAD, MIDDLE + QUAD)
+        place_rounded(0, SLOW, MIDDLE, rounded_at[0])
         multiply_on_gpsimd(0, SLOW, SLOW, SLOW + QUAD)
         gather(1, True, own_at[0], SLOW, MIDDLE)
         gather(1, False, fetched_at[1], MIDDLE, S)
-        place_rounded(0, MIDDLE, rounded_at[1])
+        gather(0, False, first_at, MIDDLE + QUAD, S)
+        place_rounded(0, MIDDLE, S, rounded_at[1])
         multiply_on_gpsimd(0, SLOW + QUAD, SLOW + QUAD, MIDDLE)
-        multiply_on_gpsimd(0, SLOW + QUAD, MIDDLE, SCALAR_END)
+        multiply_on_gpsimd(0, SLOW + QUAD, MIDDLE, MIDDLE + QUAD)
         gather(LAST_PASS, True, own_at[1], SLOW, MIDDLE)
-        gather(0, True, first_at, SCALAR_END, S)
+        gather(LAST_PASS, True, middle_at, QUAD, SLOW)
         gather(LAST_PASS, False, fetched_at[2], MIDDLE, S)
-        place_rounded(1, SLOW, rounded_at[2])
+        place_rounded(1, SLOW, MIDDLE, rounded_at[2])
         multiply_on_gpsimd(1, SLOW, SLOW, MIDDLE)
-        multiply_on_gpsimd(0, SCALAR_END, SCALAR_END, GPSIMD_END)
-        place_rounded(LAST_PASS, SLOW, own_at[0])
+        multiply_on_gpsimd(0, MIDDLE + QUAD, MIDDLE + QUAD, GPSIMD_END)
+        place_rounded(LAST_PASS, SLOW, MIDDLE, own_at[0])
         multiply_on_gpsimd(LAST_PASS, SLOW, SLOW, MIDDLE)
         spread_gate()
         gather(0, False, fetched_at[0], LAST, SLOW)
-        place_rounded(1, MIDDLE, rounded_at[3])
-        place_rounded(LAST_PASS, MIDDLE, middle_at)
-        for a in (1, LAST_PASS):
-            multiply(a, MIDDLE, MIDDLE + QUAD, S)
-            multiply(a, MIDDLE, MIDDLE, MIDDLE + QUAD)
-        multiply(0, SCALAR_END, GPSIMD_END, S)
+        place_rounded(LAST_PASS, QUAD, SLOW, rounded_at[4])
+        multiply(LAST_PASS, QUAD, QUAD, SLOW)
+        place_rounded(1, MIDDLE, S, rounded_at[3])
+        multiply(1, MIDDLE, MIDDLE, MIDDLE + QUAD, S)
+        place_rounded(LAST_PASS, MIDDLE, S, middle_at)
+        multiply(LAST_PASS, MIDDLE, MIDDLE, MIDDLE + QUAD, S)
         gather(1, False, fetched_at[1] - EDGE, LAST, SLOW)
-        gather(LAST_PASS, False, fetched_at[2] - EDGE, LAST, LAST_CUT)
+        gather(LAST_PASS, False, fetched_at[2] - EDGE, LAST, QUAD)
 
-        open_banks(BANK_GROUPS)
+        open_banks(EARLY_BANKS)
         codes_at = [own_at[1] + a * CODES for a in range(PASSES)]
         for a in range(PASSES):
             quantise(a, SLOW, MIDDLE, codes_at[a])
-        for a, at in enumerate((rounded_at[0], rounded_at[2], own_at[0])):
+        quantise(LAST_PASS, QUAD, SLOW, rounded_at[0])
+        for a, at in enumerate((rounded_at[2], own_at[0], rounded_at[1])):
             quantise(a, MIDDLE, S, at)
         y = placed("y", S, F32, 0)
 
-        def finish(e, on_vector):
-            if on_vector:
-                nc.vector.tensor_scalar(y[:, e * C : (e + 1) * C], banks[e][0], bias[:, e : e + 1], 0.0, ADD, MAX)
-            else:
-                nc.scalar.activation(y[:, e * C : (e + 1) * C], banks[e][0], RELU, bias=bias[:, e : e + 1])
+        def finish(first, end, on_vector):
+            for e in range(first, end):
+                if on_vector:
+                    nc.vector.tensor_scalar(y[:, e * C : (e + 1) * C], banks[e][0], bias[:, e : e + 1], 0.0, ADD, MAX)
+                else:
+                    nc.scalar.activation(y[:, e * C : (e + 1) * C], banks[e][0], RELU, bias=bias[:, e : e + 1])
 
-        between = (8, 20)
-        for e in range(SLOW // C, MIDDLE // C):
-            finish(e, e == between[0])
-        gather(LAST_PASS, False, codes_at[LAST_PASS], LAST_CUT, SLOW)
-        for e in range(MIDDLE // C, between[1]):
-            finish(e, False)
+        finish(SLOW // C, E, False)
 
-        both = placed("rounded_both", LAST_PASS * PACK * GROUP, BF16, late_at)
+        both = placed("rounded_both", LAST_PASS * PACK * GROUP, BF16, first_at)
         for a in range(LAST_PASS):
-            rounded[a, LAST] = both[:, a * PACK * GROUP : (a + 1) * PACK * GROUP]
+            for base in (LAST, QUAD):
+                rounded[a, base] = (both[:, a * PACK * GROUP : (a + 1) * PACK * GROUP], LAST)
             multiply_on_gpsimd(a, LAST, LAST, HELPED[a])
             multiply(a, LAST, *sorted({HELPED[a], QUAD, SLOW}))
-        for a in range(LAST_PASS):
-            quantise(a, LAST, SLOW, rounded_at[2 * a + 1])
-        for e in range(between[1], E):
-            finish(e, e == between[1])
-        open_banks(LATE_GROUPS)
-        for a in range(LAST_PASS):
-            contract(a, [first for first, end, index in LATE_GROUPS])
+        open_banks(LAST_BANKS)
+        for a, at in enumerate((rounded_at[3], own_at[0] + BLOCK)):
+            quantise(a, LAST, SLOW, at)
+        finish(QUAD // C, SLOW // C, False)
 
-        place_rounded(LAST_PASS, LAST, late_at)
+        place_rounded(LAST_PASS, LAST, QUAD, first_at)
         multiply_on_gpsimd(LAST_PASS, LAST, LAST, HELPED[LAST_PASS])
-        multiply(LAST_PASS, LAST, HELPED[LAST_PASS], QUAD, LAST_CUT)
-        multiply(LAST_PASS, LAST_CUT, LAST_CUT, SLOW)
-        for at, (lo, hi) in zip(codes_at, ((LAST, QUAD), (QUAD, QUAD + 2 * C), (QUAD + 2 * C, SLOW))):
-            quantise(LAST_PASS, lo, hi, at)
-        for e in range(LAST // C, SLOW // C):
-            finish(e, e == LATE_GROUPS[0][0])
+        multiply(LAST_PASS, LAST, HELPED[LAST_PASS], QUAD)
+        for at, (first, end, index) in zip(codes_at, LAST_BANKS):
+            quantise(LAST_PASS, first * C, end * C, at)
+        for first, end, index in LAST_BANKS:
+            finish(first, end, first > 0)
 
         sums = placed("sums", 4 * T, F32, pass_bytes)
 

@@ -20,7 +20,7 @@ CODES = 5 * GROUP
 EDGE = 64
 
 LAST, SLOW, MIDDLE = 0, GROUP, 2 * GROUP
-GPSIMD_END = S
+FIRST_END = SLOW + QUAD + 32
 HELPED = (QUAD, C, C)
 VECTOR_RUN = 2
 GPSIMD_RUN = 4
@@ -62,7 +62,8 @@ def tile_moe_pre_lin_relu_kernel(tc, xT, w_words, w_scales, b, gate, offs, pos1,
         window_bytes = 4 * WIDE + 32
         pass_bytes = PACK * window_bytes
         first_at = PASSES * pass_bytes
-        middle_at = first_at + BLOCK
+        middle_at = first_at + 4 * PACK * (FIRST_END - SLOW)
+        late_at = middle_at - BLOCK
         own_at = (middle_at + BLOCK, middle_at + 5 * BLOCK)
         fetched_at = (middle_at + 9 * BLOCK, middle_at + 3 * BLOCK, middle_at + 7 * BLOCK)
         rounded_at = [middle_at + (11 + q) * BLOCK for q in range(5)]
@@ -72,7 +73,7 @@ def tile_moe_pre_lin_relu_kernel(tc, xT, w_words, w_scales, b, gate, offs, pos1,
         nc.scalar.activation(warm[:, 8:9], warm[:, 0:1], RELU)
 
         offs_t = keep.tile([P, S // PER_COLUMN], U16, name="offs_t")
-        gate_slow = keep.tile([P, GPSIMD_END - SLOW], F32, name="gate_slow")
+        gate_slow = keep.tile([P, S - SLOW], F32, name="gate_slow")
         gate_last = keep.tile([P, max(HELPED)], F32, name="gate_last")
         windows = {}
 
@@ -86,9 +87,9 @@ def tile_moe_pre_lin_relu_kernel(tc, xT, w_words, w_scales, b, gate, offs, pos1,
         for r in range(1, PACK):
             load_plane(0, r)
         load_plane(1, 0)
-        nc.sync.dma_start(gate_slow[:, 0:QUAD], gate[0:P, SLOW : SLOW + QUAD])
+        nc.sync.dma_start(gate_slow[:, 0 : FIRST_END - SLOW], gate[0:P, SLOW:FIRST_END])
         load_plane(1, 1)
-        nc.sync.dma_start(gate_slow[:, QUAD:], gate[0:P, SLOW + QUAD : GPSIMD_END])
+        nc.sync.dma_start(gate_slow[:, FIRST_END - SLOW :], gate[0:P, FIRST_END:S])
         for r in range(2, PACK):
             load_plane(1, r)
         for r in range(PACK - 1):
@@ -210,22 +211,22 @@ def tile_moe_pre_lin_relu_kernel(tc, xT, w_words, w_scales, b, gate, offs, pos1,
                 codes[a, slot // C] = (words[:, slot - lo : slot - lo + C], scale_bytes[:, slot - lo : slot - lo + C])
             contract(a, range(lo // C, hi // C))
 
-        gather(0, True, first_at, SLOW, SLOW + QUAD)
-        gather(0, False, fetched_at[0], SLOW + QUAD, MIDDLE + QUAD)
+        gather(0, True, first_at, SLOW, FIRST_END)
+        gather(0, False, fetched_at[0], FIRST_END, MIDDLE + QUAD)
         place_rounded(0, SLOW, MIDDLE, rounded_at[0])
-        multiply_on_gpsimd(0, SLOW, SLOW, SLOW + QUAD)
+        multiply_on_gpsimd(0, SLOW, SLOW, FIRST_END)
         gather(1, True, own_at[0], SLOW, MIDDLE)
         gather(1, False, fetched_at[1], MIDDLE, S)
         gather(0, False, first_at, MIDDLE + QUAD, S)
         place_rounded(0, MIDDLE, S, rounded_at[1])
-        multiply_on_gpsimd(0, SLOW + QUAD, SLOW + QUAD, MIDDLE)
-        multiply_on_gpsimd(0, SLOW + QUAD, MIDDLE, MIDDLE + QUAD)
+        multiply_on_gpsimd(0, FIRST_END, FIRST_END, MIDDLE)
+        multiply_on_gpsimd(0, FIRST_END, MIDDLE, MIDDLE + QUAD)
         gather(LAST_PASS, True, own_at[1], SLOW, MIDDLE)
         gather(LAST_PASS, True, middle_at, QUAD, SLOW)
         gather(LAST_PASS, False, fetched_at[2], MIDDLE, S)
         place_rounded(1, SLOW, MIDDLE, rounded_at[2])
         multiply_on_gpsimd(1, SLOW, SLOW, MIDDLE)
-        multiply_on_gpsimd(0, MIDDLE + QUAD, MIDDLE + QUAD, GPSIMD_END)
+        multiply_on_gpsimd(0, MIDDLE + QUAD, MIDDLE + QUAD, S)
         place_rounded(LAST_PASS, SLOW, MIDDLE, own_at[0])
         multiply_on_gpsimd(LAST_PASS, SLOW, SLOW, MIDDLE)
         spread_gate()
@@ -257,7 +258,7 @@ def tile_moe_pre_lin_relu_kernel(tc, xT, w_words, w_scales, b, gate, offs, pos1,
 
         finish(SLOW // C, E, False)
 
-        both = placed("rounded_both", LAST_PASS * PACK * GROUP, BF16, first_at)
+        both = placed("rounded_both", LAST_PASS * PACK * GROUP, BF16, late_at)
         for a in range(LAST_PASS):
             for base in (LAST, QUAD):
                 rounded[a, base] = (both[:, a * PACK * GROUP : (a + 1) * PACK * GROUP], LAST)
@@ -268,7 +269,7 @@ def tile_moe_pre_lin_relu_kernel(tc, xT, w_words, w_scales, b, gate, offs, pos1,
             quantise(a, LAST, SLOW, at)
         finish(QUAD // C, SLOW // C, False)
 
-        place_rounded(LAST_PASS, LAST, QUAD, first_at)
+        place_rounded(LAST_PASS, LAST, QUAD, late_at)
         multiply_on_gpsimd(LAST_PASS, LAST, LAST, HELPED[LAST_PASS])
         multiply(LAST_PASS, LAST, HELPED[LAST_PASS], QUAD)
         for at, (first, end, index) in zip(codes_at, LAST_BANKS):
@@ -306,6 +307,6 @@ def tile_moe_pre_lin_relu_kernel(tc, xT, w_words, w_scales, b, gate, offs, pos1,
         nc.sync.dma_start(out[:, 0:ALONE], part(3, 0, ALONE))
         fetch_and_add(2, 2, 0, ALONE, STORE_CUT)
         fetch_and_add(2, 2, 0, STORE_CUT, T)
-        for lo, hi in ((ALONE, STORE_CUT), (STORE_CUT, T)):
+        for queue, lo, hi in ((nc.sync, ALONE, STORE_CUT), (nc.scalar, STORE_CUT, T)):
             add_last(1, lo, hi)
-            nc.sync.dma_start(out[:, lo:hi], part(3, lo, hi))
+            queue.dma_start(out[:, lo:hi], part(3, lo, hi))

@@ -11,7 +11,6 @@ K_PASS = P * PACK
 PASSES = K // K_PASS
 LAST_PASS = PASSES - 1
 PER_COLUMN = 16
-WIDE = T + 8
 BANK = 2048
 QUAD = 4 * C
 GROUP = 2 * QUAD
@@ -21,12 +20,15 @@ EDGE = 64
 
 LAST, SLOW, MIDDLE = 0, GROUP, 2 * GROUP
 FIRST_END = SLOW + QUAD + 32
-HELPED = (QUAD, C, C)
+OWN_END = MIDDLE + C
+GPSIMD_END = MIDDLE + QUAD + 352
+WIDE = (T + 8, T + 8, OWN_END - SLOW + 8)
+HELPED = (320, 320, C)
 VECTOR_RUN = 2
 GPSIMD_RUN = 4
 EARLY_BANKS = ((8, 12, 4), (12, 16, 5), (16, 20, 6), (20, 24, 7), (4, 8, 2))
-LAST_BANKS = ((0, 2, 3), (2, 4, 0))
-TWICE, ALONE, STORE_CUT = 256, 448, 800
+LAST_BANKS = ((2, 4, 0), (0, 2, 3))
+TWICE, ALONE, STORE_CUT = 192, 448, 800
 
 FLOPS = 2 * K * S * N
 BYTES = 4 * K * T + E * K * N + E * K * N // 32 + 4 * N * E + 4 * S + 2 * P * (S + 3 * T) // PER_COLUMN + 4 * N * T
@@ -59,37 +61,41 @@ def tile_moe_pre_lin_relu_kernel(tc, xT, w_words, w_scales, b, gate, offs, pos1,
         def placed(name, columns, dtype, offset):
             return stage.tile([P, columns], dtype, name=name, offset=offset, align_bytes=64)
 
-        window_bytes = 4 * WIDE + 32
-        pass_bytes = PACK * window_bytes
-        first_at = PASSES * pass_bytes
+        window_bytes = [4 * columns + 32 for columns in WIDE]
+        pass_at = [PACK * sum(window_bytes[:a]) for a in range(PASSES + 1)]
+        first_at = pass_at[PASSES]
         middle_at = first_at + 4 * PACK * (FIRST_END - SLOW)
         late_at = middle_at - BLOCK
         own_at = (middle_at + BLOCK, middle_at + 5 * BLOCK)
-        fetched_at = (middle_at + 9 * BLOCK, middle_at + 3 * BLOCK, middle_at + 7 * BLOCK)
-        rounded_at = [middle_at + (11 + q) * BLOCK for q in range(5)]
+        columns_at = middle_at + 9 * BLOCK
+        fetched_at = (columns_at + 2 * EDGE, middle_at + 3 * BLOCK, own_at[1] + 4 * PACK * (OWN_END - SLOW))
+        rounded_at = [fetched_at[0] + (2 + q) * BLOCK for q in range(5)]
 
         warm = keep.tile([P, 16], F32, name="warm")
         nc.gpsimd.memset(warm[:, 0:8], 0.0)
         nc.scalar.activation(warm[:, 8:9], warm[:, 0:1], RELU)
 
         offs_t = keep.tile([P, S // PER_COLUMN], U16, name="offs_t")
-        gate_slow = keep.tile([P, S - SLOW], F32, name="gate_slow")
+        gate_slow = keep.tile([P, GPSIMD_END - SLOW], F32, name="gate_slow")
         gate_last = keep.tile([P, max(HELPED)], F32, name="gate_last")
         windows = {}
 
         def load_plane(a, r):
-            window = placed("window%d_%d" % (a, r), WIDE, F32, a * pass_bytes + r * window_bytes)
+            window = placed("window%d_%d" % (a, r), WIDE[a], F32, pass_at[a] + r * window_bytes[a])
             nc.sync.dma_start(window[:, 0:T], xT[K_PASS * a + r : K_PASS * (a + 1) : PACK, :])
             windows[a, r] = window
+
+        def load_gate(lo, hi):
+            nc.sync.dma_start(gate_slow[:, lo - SLOW : hi - SLOW], gate[0:P, lo:hi])
 
         load_plane(0, 0)
         nc.sync.dma_start(offs_t[:], offs)
         for r in range(1, PACK):
             load_plane(0, r)
         load_plane(1, 0)
-        nc.sync.dma_start(gate_slow[:, 0 : FIRST_END - SLOW], gate[0:P, SLOW:FIRST_END])
+        load_gate(SLOW, FIRST_END)
         load_plane(1, 1)
-        nc.sync.dma_start(gate_slow[:, FIRST_END - SLOW :], gate[0:P, FIRST_END:S])
+        load_gate(FIRST_END, GPSIMD_END)
         for r in range(2, PACK):
             load_plane(1, r)
         for r in range(PACK - 1):
@@ -169,7 +175,7 @@ def tile_moe_pre_lin_relu_kernel(tc, xT, w_words, w_scales, b, gate, offs, pos1,
             make_identity(nc, identity[:])
             turned = psum.tile([P, P], F32, name="turned", offset=4 * BANK)
             nc.tensor.transpose(turned[:], gate_rows[:], identity[:])
-            gate_columns = keep.tile([P, E], F32, name="gate_columns")
+            gate_columns = placed("gate_columns", E, F32, columns_at)
             nc.vector.tensor_copy(gate_columns[:], turned[:, 0:E])
             for index, base in enumerate((LAST + QUAD, LAST, MIDDLE, MIDDLE + QUAD)):
                 gate_banks[base] = psum.tile([P, QUAD], F32, name="gate_bank%d" % index, offset=index * BANK)
@@ -221,22 +227,24 @@ def tile_moe_pre_lin_relu_kernel(tc, xT, w_words, w_scales, b, gate, offs, pos1,
         place_rounded(0, MIDDLE, S, rounded_at[1])
         multiply_on_gpsimd(0, FIRST_END, FIRST_END, MIDDLE)
         multiply_on_gpsimd(0, FIRST_END, MIDDLE, MIDDLE + QUAD)
-        gather(LAST_PASS, True, own_at[1], SLOW, MIDDLE)
+        gather(LAST_PASS, True, own_at[1], SLOW, OWN_END)
         gather(LAST_PASS, True, middle_at, QUAD, SLOW)
-        gather(LAST_PASS, False, fetched_at[2], MIDDLE, S)
+        gather(LAST_PASS, False, fetched_at[2], OWN_END, S)
         place_rounded(1, SLOW, MIDDLE, rounded_at[2])
         multiply_on_gpsimd(1, SLOW, SLOW, MIDDLE)
-        multiply_on_gpsimd(0, MIDDLE + QUAD, MIDDLE + QUAD, S)
+        multiply_on_gpsimd(0, MIDDLE + QUAD, MIDDLE + QUAD, GPSIMD_END)
         place_rounded(LAST_PASS, SLOW, MIDDLE, own_at[0])
         multiply_on_gpsimd(LAST_PASS, SLOW, SLOW, MIDDLE)
         spread_gate()
-        gather(0, False, fetched_at[0], LAST, SLOW)
+        gather(0, False, fetched_at[0] - EDGE, LAST, SLOW)
         place_rounded(LAST_PASS, QUAD, SLOW, rounded_at[4])
         multiply(LAST_PASS, QUAD, QUAD, SLOW)
         place_rounded(1, MIDDLE, S, rounded_at[3])
         multiply(1, MIDDLE, MIDDLE, MIDDLE + QUAD, S)
         place_rounded(LAST_PASS, MIDDLE, S, middle_at)
-        multiply(LAST_PASS, MIDDLE, MIDDLE, MIDDLE + QUAD, S)
+        multiply(0, MIDDLE + QUAD, GPSIMD_END, S)
+        multiply(LAST_PASS, SLOW, MIDDLE, OWN_END)
+        multiply(LAST_PASS, OWN_END, OWN_END, MIDDLE + QUAD, S)
         gather(1, False, fetched_at[1] - EDGE, LAST, SLOW)
         gather(LAST_PASS, False, fetched_at[2] - EDGE, LAST, QUAD)
 
@@ -271,13 +279,14 @@ def tile_moe_pre_lin_relu_kernel(tc, xT, w_words, w_scales, b, gate, offs, pos1,
 
         place_rounded(LAST_PASS, LAST, QUAD, late_at)
         multiply_on_gpsimd(LAST_PASS, LAST, LAST, HELPED[LAST_PASS])
-        multiply(LAST_PASS, LAST, HELPED[LAST_PASS], QUAD)
+        multiply(LAST_PASS, LAST, QUAD // 2, QUAD)
+        multiply(LAST_PASS, LAST, HELPED[LAST_PASS], QUAD // 2)
         for at, (first, end, index) in zip(codes_at, LAST_BANKS):
             quantise(LAST_PASS, first * C, end * C, at)
         for first, end, index in LAST_BANKS:
             finish(first, end, first > 0)
 
-        sums = placed("sums", 4 * T, F32, pass_bytes)
+        sums = placed("sums", 4 * T, F32, pass_at[1])
 
         def looked_up(choice, lo, hi):
             return y[:].indirect(entries(pos_t[choice], lo, hi))

@@ -9,25 +9,25 @@ P = 128
 PACK = 4
 K_PASS = P * PACK
 PASSES = K // K_PASS
-LAST_PASS = PASSES - 1
 PER_COLUMN = 16
 BANK = 2048
 QUAD = 4 * C
+HALF = QUAD // 2
 GROUP = 2 * QUAD
 BLOCK = 2 * PACK * GROUP
 CODES = 5 * GROUP
 EDGE = 64
+WIDE = T + 8
 
-LAST, SLOW, MIDDLE = 0, GROUP, 2 * GROUP
-FIRST_END = SLOW + QUAD + 32
-OWN_END = MIDDLE + C
-GPSIMD_END = MIDDLE + QUAD + 352
-WIDE = (T + 8, T + 8, OWN_END - SLOW + 8)
-HELPED = (320, 320, C)
+Q0, Q1, Q2, Q3, Q4, Q5, Q6 = range(0, S + 1, QUAD)
+FIRST_END = 576
+OWN_END = Q3 + C
+GPSIMD_END = Q2 + 64
+HELPED = (256, 256, 144)
 VECTOR_RUN = 2
 GPSIMD_RUN = 4
-EARLY_BANKS = ((8, 12, 4), (12, 16, 5), (16, 20, 6), (20, 24, 7), (4, 8, 2))
-LAST_BANKS = ((2, 4, 0), (0, 2, 3))
+EARLY_BANKS = ((0, 4, 4), (4, 8, 5), (8, 12, 6), (12, 16, 7), (16, 20, 0))
+LATE_BANKS = ((22, 24, 2), (20, 22, 1))
 TWICE, ALONE, STORE_CUT = 192, 448, 800
 
 FLOPS = 2 * K * S * N
@@ -61,55 +61,59 @@ def tile_moe_pre_lin_relu_kernel(tc, xT, w_words, w_scales, b, gate, offs, pos1,
         def placed(name, columns, dtype, offset):
             return stage.tile([P, columns], dtype, name=name, offset=offset, align_bytes=64)
 
-        window_bytes = [4 * columns + 32 for columns in WIDE]
-        pass_at = [PACK * sum(window_bytes[:a]) for a in range(PASSES + 1)]
-        first_at = pass_at[PASSES]
-        middle_at = first_at + 4 * PACK * (FIRST_END - SLOW)
-        late_at = middle_at - BLOCK
-        own_at = (middle_at + BLOCK, middle_at + 5 * BLOCK)
-        columns_at = middle_at + 9 * BLOCK
-        fetched_at = (columns_at + 2 * EDGE, middle_at + 3 * BLOCK, own_at[1] + 4 * PACK * (OWN_END - SLOW))
-        rounded_at = [fetched_at[0] + (2 + q) * BLOCK for q in range(5)]
+        window_bytes = 4 * WIDE + 32
+        area_a = PASSES * PACK * window_bytes
+        area_b = area_a + 2 * BLOCK
+        columns_at = area_b + 2 * BLOCK + EDGE
+        area_c = columns_at + 2 * EDGE
+        area_d = area_c + 2 * BLOCK
+        identity_at = area_d + BLOCK
+        area_e = identity_at + 4 * P
+        area_f = area_e + 2 * BLOCK
+        area_g = area_f + 2 * BLOCK
+        rounded_at = [area_g + 2 * CODES + 8 * EDGE + q * BLOCK for q in range(5)]
 
         warm = keep.tile([P, 16], F32, name="warm")
         nc.gpsimd.memset(warm[:, 0:8], 0.0)
         nc.scalar.activation(warm[:, 8:9], warm[:, 0:1], RELU)
 
         offs_t = keep.tile([P, S // PER_COLUMN], U16, name="offs_t")
-        gate_slow = keep.tile([P, GPSIMD_END - SLOW], F32, name="gate_slow")
-        gate_last = keep.tile([P, max(HELPED)], F32, name="gate_last")
+        gate_early = keep.tile([P, Q3], F32, name="gate_early")
+        gate_late = keep.tile([P, max(HELPED)], F32, name="gate_late")
         windows = {}
 
         def load_plane(a, r):
-            window = placed("window%d_%d" % (a, r), WIDE[a], F32, pass_at[a] + r * window_bytes[a])
+            window = placed("window%d_%d" % (a, r), WIDE, F32, (PACK * a + r) * window_bytes)
             nc.sync.dma_start(window[:, 0:T], xT[K_PASS * a + r : K_PASS * (a + 1) : PACK, :])
             windows[a, r] = window
 
         def load_gate(lo, hi):
-            nc.sync.dma_start(gate_slow[:, lo - SLOW : hi - SLOW], gate[0:P, lo:hi])
+            nc.sync.dma_start(gate_early[:, lo:hi], gate[0:P, lo:hi])
 
         load_plane(0, 0)
         nc.sync.dma_start(offs_t[:], offs)
         for r in range(1, PACK):
             load_plane(0, r)
         load_plane(1, 0)
-        load_gate(SLOW, FIRST_END)
+        load_gate(0, FIRST_END)
         load_plane(1, 1)
-        load_gate(FIRST_END, GPSIMD_END)
+        load_gate(FIRST_END, Q3)
         for r in range(2, PACK):
             load_plane(1, r)
         for r in range(PACK - 1):
-            load_plane(LAST_PASS, r)
+            load_plane(2, r)
         gate_rows = keep.tile([P, C], F32, name="gate_rows")
         nc.sync.dma_start(gate_rows[:], gate.rearrange("k (e c) -> (k e) c", c=C)[0:P, :])
-        load_plane(LAST_PASS, PACK - 1)
+        load_plane(2, PACK - 1)
 
-        w_scale = keep.tile([P, E * PASSES * N], U8, name="w_scale", align_bytes=64)
+        w_scale = keep.tile([P, E * N], U8, name="w_scale", align_bytes=64)
         nc.vector.memset(w_scale[:].bitcast(I32), 0)
-        scale_src = w_scales.rearrange("e a q n -> q (e a) n").bitcast(I32)
-        scale_dst = w_scale[:].bitcast(I32).rearrange("p (g n) -> p g n", n=N // 4)
-        for quadrant in range(4):
-            nc.sync.dma_start(scale_dst[32 * quadrant : 32 * quadrant + 4, :, :], scale_src[4 * quadrant : 4 * quadrant + 4, :, :])
+        scale_dst = w_scale[:].bitcast(I32).rearrange("p (e n) -> p e n", n=N // 4)
+        for a in range(PASSES):
+            scale_src = w_scales[:, a].rearrange("e q n -> q e n").bitcast(I32)
+            for quadrant in range(4):
+                row = 32 * quadrant + 4 * a
+                nc.sync.dma_start(scale_dst[row : row + 4, :, :], scale_src[4 * quadrant : 4 * quadrant + 4, :, :])
         w_tiles = []
         for a in range(PASSES):
             w_tile = keep.tile([P, E * N], U32, name="w%d" % a, align_bytes=64)
@@ -118,7 +122,7 @@ def tile_moe_pre_lin_relu_kernel(tc, xT, w_words, w_scales, b, gate, offs, pos1,
                 w_words[:, a].rearrange("e p n r -> p e (n r)").bitcast(I32),
             )
             w_tiles.append(w_tile)
-        nc.sync.dma_start(gate_last[:], gate[0:P, LAST : LAST + max(HELPED)])
+        nc.sync.dma_start(gate_late[:], gate[0:P, Q5 : Q5 + max(HELPED)])
         bias = keep.tile([P, E], F32, name="bias")
         nc.sync.dma_start(bias[:], b)
         pos_t = []
@@ -142,14 +146,14 @@ def tile_moe_pre_lin_relu_kernel(tc, xT, w_words, w_scales, b, gate, offs, pos1,
 
         rounded = {}
 
-        def place_rounded(a, lo, hi, at):
-            tile = placed("rounded%d_%d" % (a, lo), PACK * (hi - lo), BF16, at)
-            for base in range(lo, hi, QUAD):
-                rounded[a, base] = (tile[:], lo)
+        def place_rounded(at, width, *runs):
+            tile = placed("rounded%d_%d" % runs[0], PACK * width, BF16, at)
+            for index, run in enumerate(runs):
+                rounded[run] = tile[:, PACK * (width // len(runs)) * index :]
 
         def rounded_view(a, lo, hi):
-            tile, first = rounded[a, lo // QUAD * QUAD]
-            return tile[:, PACK * (lo - first) : PACK * (hi - first)]
+            base = max(first for a_run, first in rounded if a_run == a and first <= lo)
+            return rounded[a, base][:, PACK * (lo - base) : PACK * (hi - base)]
 
         def product(engine, run, a, first, lo, hi, gates):
             engine.tensor_tensor(
@@ -160,24 +164,24 @@ def tile_moe_pre_lin_relu_kernel(tc, xT, w_words, w_scales, b, gate, offs, pos1,
             )
 
         def multiply_on_gpsimd(a, first, lo, hi):
-            gate_tile, base = (gate_last, LAST) if lo < SLOW else (gate_slow, SLOW)
+            gate_tile, base = (gate_early, 0) if lo < Q5 else (gate_late, Q5)
             product(nc.gpsimd, GPSIMD_RUN, a, first, lo, hi, gate_tile[:, lo - base : hi - base])
 
         gate_banks = {}
 
-        def multiply(a, first, *cuts):
-            for lo, hi in zip(cuts[:-1], cuts[1:]):
-                base = lo // QUAD * QUAD
-                product(nc.vector, VECTOR_RUN, a, first, lo, hi, gate_banks[base][:, lo - base : hi - base])
+        def multiply(a, first, lo, hi):
+            base = lo // QUAD * QUAD
+            product(nc.vector, VECTOR_RUN, a, first, lo, hi, gate_banks[base][:, lo - base : hi - base])
 
         def spread_gate():
-            identity = keep.tile([P, P], F32, name="identity")
+            identity = placed("identity", P, F32, identity_at)
             make_identity(nc, identity[:])
             turned = psum.tile([P, P], F32, name="turned", offset=4 * BANK)
             nc.tensor.transpose(turned[:], gate_rows[:], identity[:])
             gate_columns = placed("gate_columns", E, F32, columns_at)
             nc.vector.tensor_copy(gate_columns[:], turned[:, 0:E])
-            for index, base in enumerate((LAST + QUAD, LAST, MIDDLE, MIDDLE + QUAD)):
+            for base in (Q3, Q4, Q2, Q5):
+                index = (base - Q2) // QUAD
                 gate_banks[base] = psum.tile([P, QUAD], F32, name="gate_bank%d" % index, offset=index * BANK)
                 for lo in range(0, QUAD, C):
                     e = (base + lo) // C
@@ -193,68 +197,74 @@ def tile_moe_pre_lin_relu_kernel(tc, xT, w_words, w_scales, b, gate, offs, pos1,
                 for e in range(first, end):
                     banks[e] = (bank[:, (e - first) * C : (e - first + 1) * C], first, PASSES * (end - first))
 
-        codes = {}
+        def contract(a, e, words, scale_bytes):
+            acc, first, total = banks[e]
+            issued[first] = issued[first] + 1
+            nc.tensor.matmul_mx(
+                acc,
+                lhsT=w_tiles[a][:, e * N : (e + 1) * N].bitcast(FP8X4),
+                lhsT_scale=w_scale[4 * a : P, e * N : (e + 1) * N],
+                rhs=words.bitcast(FP8X4),
+                rhs_scale=scale_bytes,
+                start=issued[first] == 1,
+                stop=issued[first] == total,
+            )
 
-        def contract(a, experts):
-            for e in experts:
-                acc, first, total = banks[e]
-                issued[first] = issued[first] + 1
-                nc.tensor.matmul_mx(
-                    acc,
-                    lhsT=w_tiles[a][:, e * N : (e + 1) * N].bitcast(FP8X4),
-                    lhsT_scale=w_scale[:, (e * PASSES + a) * N : (e * PASSES + a + 1) * N],
-                    rhs=codes[a, e][0].bitcast(FP8X4),
-                    rhs_scale=codes[a, e][1],
-                    start=issued[first] == 1,
-                    stop=issued[first] == total,
-                )
+        def quantise(at, *runs):
+            a, lo = runs[0][0:2]
+            width = sum(end - first for a_run, first, end in runs)
+            words = placed("words%d_%d" % (a, lo), width, U32, at)
+            scale_bytes = placed("bytes%d_%d" % (a, lo), width, U8, at + 4 * width)
+            nc.vector.quantize_mx(words[:].bitcast(FP8X4), scale_bytes[:], rounded_view(a, lo, lo + width))
+            column = 0
+            for a_run, first, end in runs:
+                for slot in range(first, end, C):
+                    contract(a_run, slot // C, words[:, column : column + C], scale_bytes[:, column : column + C])
+                    column = column + C
 
-        def quantise(a, lo, hi, at):
-            words = placed("words%d_%d" % (a, lo), hi - lo, U32, at)
-            scale_bytes = placed("bytes%d_%d" % (a, lo), hi - lo, U8, at + 4 * (hi - lo))
-            nc.vector.quantize_mx(words[:].bitcast(FP8X4), scale_bytes[:], rounded_view(a, lo, hi))
-            for slot in range(lo, hi, C):
-                codes[a, slot // C] = (words[:, slot - lo : slot - lo + C], scale_bytes[:, slot - lo : slot - lo + C])
-            contract(a, range(lo // C, hi // C))
-
-        gather(0, True, first_at, SLOW, FIRST_END)
-        gather(0, False, fetched_at[0], FIRST_END, MIDDLE + QUAD)
-        place_rounded(0, SLOW, MIDDLE, rounded_at[0])
-        multiply_on_gpsimd(0, SLOW, SLOW, FIRST_END)
-        gather(1, True, own_at[0], SLOW, MIDDLE)
-        gather(1, False, fetched_at[1], MIDDLE, S)
-        gather(0, False, first_at, MIDDLE + QUAD, S)
-        place_rounded(0, MIDDLE, S, rounded_at[1])
-        multiply_on_gpsimd(0, FIRST_END, FIRST_END, MIDDLE)
-        multiply_on_gpsimd(0, FIRST_END, MIDDLE, MIDDLE + QUAD)
-        gather(LAST_PASS, True, own_at[1], SLOW, OWN_END)
-        gather(LAST_PASS, True, middle_at, QUAD, SLOW)
-        gather(LAST_PASS, False, fetched_at[2], OWN_END, S)
-        place_rounded(1, SLOW, MIDDLE, rounded_at[2])
-        multiply_on_gpsimd(1, SLOW, SLOW, MIDDLE)
-        multiply_on_gpsimd(0, MIDDLE + QUAD, MIDDLE + QUAD, GPSIMD_END)
-        place_rounded(LAST_PASS, SLOW, MIDDLE, own_at[0])
-        multiply_on_gpsimd(LAST_PASS, SLOW, SLOW, MIDDLE)
+        gather(0, True, area_a, 0, FIRST_END)
+        gather(0, False, area_c, FIRST_END, Q3)
+        gather(1, True, area_e, 0, Q2)
+        gather(1, False, area_d, Q2, Q3)
+        gather(1, False, area_b, Q3, Q5)
+        place_rounded(rounded_at[0], GROUP, (0, Q0), (0, Q1))
+        place_rounded(rounded_at[1], GROUP, (0, Q2), (0, Q3))
+        place_rounded(rounded_at[2], GROUP, (1, Q0), (1, Q1))
+        place_rounded(rounded_at[3], GROUP, (1, Q2), (1, Q3))
+        place_rounded(rounded_at[4], GROUP, (1, Q4), (2, Q4))
+        multiply_on_gpsimd(0, 0, 0, FIRST_END)
+        multiply_on_gpsimd(0, FIRST_END, FIRST_END, Q2)
+        multiply_on_gpsimd(0, FIRST_END, Q2, Q3)
+        gather(2, True, area_f, 0, Q2)
+        gather(2, True, area_g, Q2, OWN_END)
+        gather(2, False, area_a, OWN_END, Q5)
+        multiply_on_gpsimd(1, 0, 0, Q2)
+        multiply_on_gpsimd(1, Q2, Q2, Q3)
+        place_rounded(area_c + BLOCK, GROUP, (2, Q0), (2, Q1))
+        multiply_on_gpsimd(2, 0, 0, Q2)
         spread_gate()
-        gather(0, False, fetched_at[0] - EDGE, LAST, SLOW)
-        place_rounded(LAST_PASS, QUAD, SLOW, rounded_at[4])
-        multiply(LAST_PASS, QUAD, QUAD, SLOW)
-        place_rounded(1, MIDDLE, S, rounded_at[3])
-        multiply(1, MIDDLE, MIDDLE, MIDDLE + QUAD, S)
-        place_rounded(LAST_PASS, MIDDLE, S, middle_at)
-        multiply(0, MIDDLE + QUAD, GPSIMD_END, S)
-        multiply(LAST_PASS, SLOW, MIDDLE, OWN_END)
-        multiply(LAST_PASS, OWN_END, OWN_END, MIDDLE + QUAD, S)
-        gather(1, False, fetched_at[1] - EDGE, LAST, SLOW)
-        gather(LAST_PASS, False, fetched_at[2] - EDGE, LAST, QUAD)
+        gather(0, False, area_c - EDGE, Q3, Q4)
+        gather(0, False, area_e - EDGE, Q4, Q6)
+        gather(1, False, area_d + EDGE, Q5, Q6)
+        gather(2, False, area_f, Q5, Q6)
+        multiply(1, Q3, Q3, Q4)
+        multiply(1, Q3, Q4, Q5)
+        multiply(2, OWN_END, Q4, Q5)
+        place_rounded(area_b, GROUP, (2, Q2), (2, Q3))
+        multiply_on_gpsimd(2, Q2, Q2, GPSIMD_END)
+        multiply(2, Q2, GPSIMD_END, Q3)
+        multiply(2, Q2, Q3, OWN_END)
+        multiply(2, OWN_END, OWN_END, Q4)
+        multiply(0, Q3, Q3, Q4)
 
         open_banks(EARLY_BANKS)
-        codes_at = [own_at[1] + a * CODES for a in range(PASSES)]
-        for a in range(PASSES):
-            quantise(a, SLOW, MIDDLE, codes_at[a])
-        quantise(LAST_PASS, QUAD, SLOW, rounded_at[0])
-        for a, at in enumerate((rounded_at[2], own_at[0], rounded_at[1])):
-            quantise(a, MIDDLE, S, at)
+        quantise(area_g, (0, Q0, Q2))
+        quantise(area_g + CODES, (1, Q0, Q2))
+        quantise(rounded_at[0], (1, Q2, Q4))
+        quantise(rounded_at[2], (1, Q4, Q5), (2, Q4, Q5))
+        quantise(rounded_at[3], (2, Q0, Q2))
+        quantise(rounded_at[4], (0, Q2, Q4))
+        quantise(area_c + BLOCK, (2, Q2, Q4))
         y = placed("y", S, F32, 0)
 
         def finish(first, end, on_vector):
@@ -264,29 +274,32 @@ def tile_moe_pre_lin_relu_kernel(tc, xT, w_words, w_scales, b, gate, offs, pos1,
                 else:
                     nc.scalar.activation(y[:, e * C : (e + 1) * C], banks[e][0], RELU, bias=bias[:, e : e + 1])
 
-        finish(SLOW // C, E, False)
+        finish(0, Q4 // C, False)
 
-        both = placed("rounded_both", LAST_PASS * PACK * GROUP, BF16, late_at)
-        for a in range(LAST_PASS):
-            for base in (LAST, QUAD):
-                rounded[a, base] = (both[:, a * PACK * GROUP : (a + 1) * PACK * GROUP], LAST)
-            multiply_on_gpsimd(a, LAST, LAST, HELPED[a])
-            multiply(a, LAST, *sorted({HELPED[a], QUAD, SLOW}))
-        open_banks(LAST_BANKS)
-        for a, at in enumerate((rounded_at[3], own_at[0] + BLOCK)):
-            quantise(a, LAST, SLOW, at)
-        finish(QUAD // C, SLOW // C, False)
+        place_rounded(area_b + EDGE, GROUP, (0, Q4), (0, Q5))
+        place_rounded(area_b + EDGE - BLOCK // 2, QUAD, (1, Q5))
+        multiply_on_gpsimd(0, Q4, Q5, Q5 + HELPED[0])
+        multiply_on_gpsimd(1, Q5, Q5, Q5 + HELPED[1])
+        multiply(0, Q4, Q4, Q5)
+        multiply(0, Q4, Q5 + HELPED[0], Q6)
+        multiply(1, Q5, Q5 + HELPED[1], Q6)
 
-        place_rounded(LAST_PASS, LAST, QUAD, late_at)
-        multiply_on_gpsimd(LAST_PASS, LAST, LAST, HELPED[LAST_PASS])
-        multiply(LAST_PASS, LAST, QUAD // 2, QUAD)
-        multiply(LAST_PASS, LAST, HELPED[LAST_PASS], QUAD // 2)
-        for at, (first, end, index) in zip(codes_at, LAST_BANKS):
-            quantise(LAST_PASS, first * C, end * C, at)
-        for first, end, index in LAST_BANKS:
-            finish(first, end, first > 0)
+        open_banks(LATE_BANKS)
+        quantise(area_d + EDGE, (0, Q4, Q6))
+        quantise(area_d + EDGE + CODES, (1, Q5, Q6))
+        finish(Q4 // C, Q5 // C, False)
 
-        sums = placed("sums", 4 * T, F32, pass_at[1])
+        place_rounded(area_b + EDGE - BLOCK // 2, HALF, (2, Q5))
+        place_rounded(area_b + EDGE, HALF, (2, Q5 + HALF))
+        multiply_on_gpsimd(2, Q5, Q5, Q5 + HELPED[2])
+        multiply(2, Q5, Q5 + HALF, Q6)
+        multiply(2, Q5, Q5 + HELPED[2], Q5 + HALF)
+        for at, (first, end, index) in zip((rounded_at[1], rounded_at[1] + CODES), LATE_BANKS):
+            quantise(at, (2, first * C, end * C))
+        for first, end, index in LATE_BANKS:
+            finish(first, end, end < E)
+
+        sums = placed("sums", 4 * T, F32, PACK * window_bytes)
 
         def looked_up(choice, lo, hi):
             return y[:].indirect(entries(pos_t[choice], lo, hi))

@@ -21,14 +21,13 @@ WIDE = T + 8
 
 Q0, Q1, Q2, Q3, Q4, Q5, Q6 = range(0, S + 1, QUAD)
 FIRST_END = 576
-OWN_END = Q3 + C
-GPSIMD_END = Q2 + 64
-HELPED = (256, 256, 144)
+GPSIMD_END = Q2 + 288
+HELPED = (240, 240, 128)
 VECTOR_RUN = 2
 GPSIMD_RUN = 4
 EARLY_BANKS = ((0, 4, 4), (4, 8, 5), (8, 12, 6), (12, 16, 7), (16, 20, 0))
 LATE_BANKS = ((22, 24, 2), (20, 22, 1))
-TWICE, ALONE, STORE_CUT = 192, 448, 800
+TWICE, ALONE, STORE_CUT = 160, 352, 736
 
 FLOPS = 2 * K * S * N
 BYTES = 4 * K * T + E * K * N + E * K * N // 32 + 4 * N * E + 4 * S + 2 * P * (S + 3 * T) // PER_COLUMN + 4 * N * T
@@ -71,7 +70,7 @@ def tile_moe_pre_lin_relu_kernel(tc, xT, w_words, w_scales, b, gate, offs, pos1,
         area_e = identity_at + 4 * P
         area_f = area_e + 2 * BLOCK
         area_g = area_f + 2 * BLOCK
-        rounded_at = [area_g + 2 * CODES + 8 * EDGE + q * BLOCK for q in range(5)]
+        rounded_at = [area_g + BLOCK + q * BLOCK for q in range(5)]
 
         warm = keep.tile([P, 16], F32, name="warm")
         nc.gpsimd.memset(warm[:, 0:8], 0.0)
@@ -236,10 +235,10 @@ def tile_moe_pre_lin_relu_kernel(tc, xT, w_words, w_scales, b, gate, offs, pos1,
         multiply_on_gpsimd(0, FIRST_END, FIRST_END, Q2)
         multiply_on_gpsimd(0, FIRST_END, Q2, Q3)
         gather(2, True, area_f, 0, Q2)
-        gather(2, True, area_g, Q2, OWN_END)
-        gather(2, False, area_a, OWN_END, Q5)
+        gather(2, True, area_g, Q2, Q3)
+        gather(2, False, area_a, Q3, Q5)
         multiply_on_gpsimd(1, 0, 0, Q2)
-        multiply_on_gpsimd(1, Q2, Q2, Q3)
+        multiply_on_gpsimd(1, Q2, Q2, GPSIMD_END)
         place_rounded(area_c + BLOCK, GROUP, (2, Q0), (2, Q1))
         multiply_on_gpsimd(2, 0, 0, Q2)
         spread_gate()
@@ -249,22 +248,21 @@ def tile_moe_pre_lin_relu_kernel(tc, xT, w_words, w_scales, b, gate, offs, pos1,
         gather(2, False, area_f, Q5, Q6)
         multiply(1, Q3, Q3, Q4)
         multiply(1, Q3, Q4, Q5)
-        multiply(2, OWN_END, Q4, Q5)
+        multiply(1, Q2, GPSIMD_END, Q3)
         place_rounded(area_b, GROUP, (2, Q2), (2, Q3))
-        multiply_on_gpsimd(2, Q2, Q2, GPSIMD_END)
-        multiply(2, Q2, GPSIMD_END, Q3)
-        multiply(2, Q2, Q3, OWN_END)
-        multiply(2, OWN_END, OWN_END, Q4)
+        multiply(2, Q2, Q2, Q3)
+        multiply(2, Q3, Q4, Q5)
+        multiply(2, Q3, Q3, Q4)
         multiply(0, Q3, Q3, Q4)
 
         open_banks(EARLY_BANKS)
-        quantise(area_g, (0, Q0, Q2))
-        quantise(area_g + CODES, (1, Q0, Q2))
+        quantise(area_a, (0, Q0, Q2))
+        quantise(area_a + CODES, (1, Q0, Q2))
         quantise(rounded_at[0], (1, Q2, Q4))
         quantise(rounded_at[2], (1, Q4, Q5), (2, Q4, Q5))
         quantise(rounded_at[3], (2, Q0, Q2))
-        quantise(rounded_at[4], (0, Q2, Q4))
-        quantise(area_c + BLOCK, (2, Q2, Q4))
+        quantise(rounded_at[4], (2, Q2, Q4))
+        quantise(area_c + BLOCK, (0, Q2, Q4))
         y = placed("y", S, F32, 0)
 
         def finish(first, end, on_vector):
@@ -285,16 +283,16 @@ def tile_moe_pre_lin_relu_kernel(tc, xT, w_words, w_scales, b, gate, offs, pos1,
         multiply(1, Q5, Q5 + HELPED[1], Q6)
 
         open_banks(LATE_BANKS)
-        quantise(area_d + EDGE, (0, Q4, Q6))
-        quantise(area_d + EDGE + CODES, (1, Q5, Q6))
+        quantise(rounded_at[1], (0, Q4, Q6))
+        quantise(rounded_at[1] + CODES, (1, Q5, Q6))
         finish(Q4 // C, Q5 // C, False)
 
-        place_rounded(area_b + EDGE - BLOCK // 2, HALF, (2, Q5))
-        place_rounded(area_b + EDGE, HALF, (2, Q5 + HALF))
+        place_rounded(area_b + EDGE, HALF, (2, Q5))
+        place_rounded(area_b + EDGE + BLOCK // 4, HALF, (2, Q5 + HALF))
         multiply_on_gpsimd(2, Q5, Q5, Q5 + HELPED[2])
         multiply(2, Q5, Q5 + HALF, Q6)
         multiply(2, Q5, Q5 + HELPED[2], Q5 + HALF)
-        for at, (first, end, index) in zip((rounded_at[1], rounded_at[1] + CODES), LATE_BANKS):
+        for at, (first, end, index) in zip((area_g, area_g + CODES), LATE_BANKS):
             quantise(at, (2, first * C, end * C))
         for first, end, index in LATE_BANKS:
             finish(first, end, end < E)
@@ -318,8 +316,8 @@ def tile_moe_pre_lin_relu_kernel(tc, xT, w_words, w_scales, b, gate, offs, pos1,
 
         fetch_on_scalar(0, 0, TWICE)
         fetch_on_scalar(0, TWICE, STORE_CUT)
-        fetch_on_scalar(1, ALONE, STORE_CUT)
         fetch_on_scalar(0, STORE_CUT, T)
+        fetch_on_scalar(1, ALONE, STORE_CUT)
         fetch_on_scalar(1, STORE_CUT, T)
         nc.vector.tensor_copy(part(1, TWICE, ALONE), looked_up(2, TWICE, ALONE))
         fetch_and_add(1, 1, 0, 0, TWICE)

@@ -21,8 +21,7 @@ WIDE = T + 8
 
 Q0, Q1, Q2, Q3, Q4, Q5, Q6 = range(0, S + 1, QUAD)
 FIRST_END = 576
-GPSIMD_END = Q2 + 288
-HELPED = (240, 240, 128)
+HELPED = (256, 256, 160)
 VECTOR_RUN = 2
 GPSIMD_RUN = 4
 EARLY_BANKS = ((0, 4, 4), (4, 8, 5), (8, 12, 6), (12, 16, 7), (16, 20, 0))
@@ -238,7 +237,7 @@ def tile_moe_pre_lin_relu_kernel(tc, xT, w_words, w_scales, b, gate, offs, pos1,
         gather(2, True, area_g, Q2, Q3)
         gather(2, False, area_a, Q3, Q5)
         multiply_on_gpsimd(1, 0, 0, Q2)
-        multiply_on_gpsimd(1, Q2, Q2, GPSIMD_END)
+        multiply_on_gpsimd(1, Q2, Q2, Q3)
         place_rounded(area_c + BLOCK, GROUP, (2, Q0), (2, Q1))
         multiply_on_gpsimd(2, 0, 0, Q2)
         spread_gate()
@@ -248,10 +247,9 @@ def tile_moe_pre_lin_relu_kernel(tc, xT, w_words, w_scales, b, gate, offs, pos1,
         gather(2, False, area_f, Q5, Q6)
         multiply(1, Q3, Q3, Q4)
         multiply(1, Q3, Q4, Q5)
-        multiply(1, Q2, GPSIMD_END, Q3)
+        multiply(2, Q3, Q4, Q5)
         place_rounded(area_b, GROUP, (2, Q2), (2, Q3))
         multiply(2, Q2, Q2, Q3)
-        multiply(2, Q3, Q4, Q5)
         multiply(2, Q3, Q3, Q4)
         multiply(0, Q3, Q3, Q4)
 

@@ -20,13 +20,14 @@ EDGE = 64
 WIDE = T + 8
 
 Q0, Q1, Q2, Q3, Q4, Q5, Q6 = range(0, S + 1, QUAD)
-FIRST_END = 576
-HELPED = (256, 256, 160)
+FIRST_END = 544
+GPSIMD_END = Q3 - 48
+HELPED = (240, 240, 160)
 VECTOR_RUN = 2
 GPSIMD_RUN = 4
 EARLY_BANKS = ((0, 4, 4), (4, 8, 5), (8, 12, 6), (12, 16, 7), (16, 20, 0))
 LATE_BANKS = ((22, 24, 2), (20, 22, 1))
-TWICE, ALONE, STORE_CUT = 160, 352, 736
+TWICE, ALONE, STORE_CUT = 192, 448, 800
 
 FLOPS = 2 * K * S * N
 BYTES = 4 * K * T + E * K * N + E * K * N // 32 + 4 * N * E + 4 * S + 2 * P * (S + 3 * T) // PER_COLUMN + 4 * N * T
@@ -237,7 +238,7 @@ def tile_moe_pre_lin_relu_kernel(tc, xT, w_words, w_scales, b, gate, offs, pos1,
         gather(2, True, area_g, Q2, Q3)
         gather(2, False, area_a, Q3, Q5)
         multiply_on_gpsimd(1, 0, 0, Q2)
-        multiply_on_gpsimd(1, Q2, Q2, Q3)
+        multiply_on_gpsimd(1, Q2, Q2, GPSIMD_END)
         place_rounded(area_c + BLOCK, GROUP, (2, Q0), (2, Q1))
         multiply_on_gpsimd(2, 0, 0, Q2)
         spread_gate()
@@ -247,9 +248,10 @@ def tile_moe_pre_lin_relu_kernel(tc, xT, w_words, w_scales, b, gate, offs, pos1,
         gather(2, False, area_f, Q5, Q6)
         multiply(1, Q3, Q3, Q4)
         multiply(1, Q3, Q4, Q5)
-        multiply(2, Q3, Q4, Q5)
+        multiply(1, Q2, GPSIMD_END, Q3)
         place_rounded(area_b, GROUP, (2, Q2), (2, Q3))
         multiply(2, Q2, Q2, Q3)
+        multiply(2, Q3, Q4, Q5)
         multiply(2, Q3, Q3, Q4)
         multiply(0, Q3, Q3, Q4)
 
@@ -314,8 +316,8 @@ def tile_moe_pre_lin_relu_kernel(tc, xT, w_words, w_scales, b, gate, offs, pos1,
 
         fetch_on_scalar(0, 0, TWICE)
         fetch_on_scalar(0, TWICE, STORE_CUT)
-        fetch_on_scalar(0, STORE_CUT, T)
         fetch_on_scalar(1, ALONE, STORE_CUT)
+        fetch_on_scalar(0, STORE_CUT, T)
         fetch_on_scalar(1, STORE_CUT, T)
         nc.vector.tensor_copy(part(1, TWICE, ALONE), looked_up(2, TWICE, ALONE))
         fetch_and_add(1, 1, 0, 0, TWICE)

@@ -17,12 +17,12 @@ GROUP = 2 * QUAD
 BLOCK = 2 * PACK * GROUP
 CODES = 5 * GROUP
 EDGE = 64
-WIDE = T + 8
 
 Q0, Q1, Q2, Q3, Q4, Q5, Q6 = range(0, S + 1, QUAD)
+WIDE = (T + 8, T + 8, Q3 + 8)
 FIRST_END = 544
-GPSIMD_END = Q3 - 48
-HELPED = (240, 240, 160)
+GPSIMD_END = Q3 - 32
+HELPED = (248, 248, 160)
 VECTOR_RUN = 2
 GPSIMD_RUN = 4
 EARLY_BANKS = ((0, 4, 4), (4, 8, 5), (8, 12, 6), (12, 16, 7), (16, 20, 0))
@@ -60,8 +60,10 @@ def tile_moe_pre_lin_relu_kernel(tc, xT, w_words, w_scales, b, gate, offs, pos1,
         def placed(name, columns, dtype, offset):
             return stage.tile([P, columns], dtype, name=name, offset=offset, align_bytes=64)
 
-        window_bytes = 4 * WIDE + 32
-        area_a = PASSES * PACK * window_bytes
+        window_bytes = [4 * columns + 32 for columns in WIDE]
+        pass_at = [PACK * sum(window_bytes[:a]) for a in range(PASSES + 1)]
+        gate_at = pass_at[PASSES]
+        area_a = gate_at + 4 * Q3
         area_b = area_a + 2 * BLOCK
         columns_at = area_b + 2 * BLOCK + EDGE
         area_c = columns_at + 2 * EDGE
@@ -69,20 +71,18 @@ def tile_moe_pre_lin_relu_kernel(tc, xT, w_words, w_scales, b, gate, offs, pos1,
         identity_at = area_d + BLOCK
         area_e = identity_at + 4 * P
         area_f = area_e + 2 * BLOCK
-        area_g = area_f + 2 * BLOCK
-        rounded_at = [area_g + BLOCK + q * BLOCK for q in range(5)]
+        rounded_at = [area_f + (3 + q) * BLOCK for q in range(5)]
 
         warm = keep.tile([P, 16], F32, name="warm")
         nc.gpsimd.memset(warm[:, 0:8], 0.0)
         nc.scalar.activation(warm[:, 8:9], warm[:, 0:1], RELU)
 
         offs_t = keep.tile([P, S // PER_COLUMN], U16, name="offs_t")
-        gate_early = keep.tile([P, Q3], F32, name="gate_early")
-        gate_late = keep.tile([P, max(HELPED)], F32, name="gate_late")
+        gate_early = placed("gate_early", Q3, F32, gate_at)
         windows = {}
 
         def load_plane(a, r):
-            window = placed("window%d_%d" % (a, r), WIDE, F32, (PACK * a + r) * window_bytes)
+            window = placed("window%d_%d" % (a, r), WIDE[a], F32, pass_at[a] + r * window_bytes[a])
             nc.sync.dma_start(window[:, 0:T], xT[K_PASS * a + r : K_PASS * (a + 1) : PACK, :])
             windows[a, r] = window
 
@@ -101,7 +101,7 @@ def tile_moe_pre_lin_relu_kernel(tc, xT, w_words, w_scales, b, gate, offs, pos1,
             load_plane(1, r)
         for r in range(PACK - 1):
             load_plane(2, r)
-        gate_rows = keep.tile([P, C], F32, name="gate_rows")
+        gate_rows = placed("gate_rows", C, F32, rounded_at[4])
         nc.sync.dma_start(gate_rows[:], gate.rearrange("k (e c) -> (k e) c", c=C)[0:P, :])
         load_plane(2, PACK - 1)
 
@@ -121,7 +121,6 @@ def tile_moe_pre_lin_relu_kernel(tc, xT, w_words, w_scales, b, gate, offs, pos1,
                 w_words[:, a].rearrange("e p n r -> p e (n r)").bitcast(I32),
             )
             w_tiles.append(w_tile)
-        nc.sync.dma_start(gate_late[:], gate[0:P, Q5 : Q5 + max(HELPED)])
         bias = keep.tile([P, E], F32, name="bias")
         nc.sync.dma_start(bias[:], b)
         pos_t = []
@@ -162,8 +161,10 @@ def tile_moe_pre_lin_relu_kernel(tc, xT, w_words, w_scales, b, gate, offs, pos1,
                 MULT,
             )
 
+        gate_tiles = [(gate_early, 0)]
+
         def multiply_on_gpsimd(a, first, lo, hi):
-            gate_tile, base = (gate_early, 0) if lo < Q5 else (gate_late, Q5)
+            gate_tile, base = gate_tiles[lo >= Q5]
             product(nc.gpsimd, GPSIMD_RUN, a, first, lo, hi, gate_tile[:, lo - base : hi - base])
 
         gate_banks = {}
@@ -234,13 +235,15 @@ def tile_moe_pre_lin_relu_kernel(tc, xT, w_words, w_scales, b, gate, offs, pos1,
         multiply_on_gpsimd(0, 0, 0, FIRST_END)
         multiply_on_gpsimd(0, FIRST_END, FIRST_END, Q2)
         multiply_on_gpsimd(0, FIRST_END, Q2, Q3)
-        gather(2, True, area_f, 0, Q2)
-        gather(2, True, area_g, Q2, Q3)
+        gather(2, True, area_f, 0, Q3)
         gather(2, False, area_a, Q3, Q5)
         multiply_on_gpsimd(1, 0, 0, Q2)
         multiply_on_gpsimd(1, Q2, Q2, GPSIMD_END)
         place_rounded(area_c + BLOCK, GROUP, (2, Q0), (2, Q1))
         multiply_on_gpsimd(2, 0, 0, Q2)
+        gate_late = placed("gate_late", max(HELPED), F32, gate_at)
+        nc.sync.dma_start(gate_late[:], gate[0:P, Q5 : Q5 + max(HELPED)])
+        gate_tiles.append((gate_late, Q5))
         spread_gate()
         gather(0, False, area_c - EDGE, Q3, Q4)
         gather(0, False, area_e - EDGE, Q4, Q6)
@@ -250,7 +253,7 @@ def tile_moe_pre_lin_relu_kernel(tc, xT, w_words, w_scales, b, gate, offs, pos1,
         multiply(1, Q3, Q4, Q5)
         multiply(1, Q2, GPSIMD_END, Q3)
         place_rounded(area_b, GROUP, (2, Q2), (2, Q3))
-        multiply(2, Q2, Q2, Q3)
+        multiply(2, 0, Q2, Q3)
         multiply(2, Q3, Q4, Q5)
         multiply(2, Q3, Q3, Q4)
         multiply(0, Q3, Q3, Q4)
@@ -292,12 +295,12 @@ def tile_moe_pre_lin_relu_kernel(tc, xT, w_words, w_scales, b, gate, offs, pos1,
         multiply_on_gpsimd(2, Q5, Q5, Q5 + HELPED[2])
         multiply(2, Q5, Q5 + HALF, Q6)
         multiply(2, Q5, Q5 + HELPED[2], Q5 + HALF)
-        for at, (first, end, index) in zip((area_g, area_g + CODES), LATE_BANKS):
+        for at, (first, end, index) in zip((area_f + BLOCK, area_f + BLOCK + CODES), LATE_BANKS):
             quantise(at, (2, first * C, end * C))
         for first, end, index in LATE_BANKS:
             finish(first, end, end < E)
 
-        sums = placed("sums", 4 * T, F32, PACK * window_bytes)
+        sums = placed("sums", 4 * T, F32, pass_at[1])
 
         def looked_up(choice, lo, hi):
             return y[:].indirect(entries(pos_t[choice], lo, hi))

@@ -65,8 +65,8 @@ def tile_moe_pre_lin_relu_kernel(tc, xT, w_words, w_scales, b, gate, offs, pos1,
         gate_at = pass_at[PASSES]
         area_a = gate_at + 4 * Q3
         area_b = area_a + 2 * BLOCK
-        columns_at = area_b + 2 * BLOCK + EDGE
-        area_c = columns_at + 2 * EDGE
+        columns_at = area_b + 2 * BLOCK + 2 * EDGE
+        area_c = columns_at + EDGE
         area_d = area_c + 2 * BLOCK
         identity_at = area_d + BLOCK
         area_e = identity_at + 4 * P
@@ -178,14 +178,14 @@ def tile_moe_pre_lin_relu_kernel(tc, xT, w_words, w_scales, b, gate, offs, pos1,
             make_identity(nc, identity[:])
             turned = psum.tile([P, P], F32, name="turned", offset=4 * BANK)
             nc.tensor.transpose(turned[:], gate_rows[:], identity[:])
-            gate_columns = placed("gate_columns", E, F32, columns_at)
-            nc.vector.tensor_copy(gate_columns[:], turned[:, 0:E])
+            gate_columns = placed("gate_columns", E - Q2 // C, F32, columns_at)
+            nc.vector.tensor_copy(gate_columns[:], turned[:, Q2 // C : E])
             for base in (Q3, Q4, Q2, Q5):
                 index = (base - Q2) // QUAD
                 gate_banks[base] = psum.tile([P, QUAD], F32, name="gate_bank%d" % index, offset=index * BANK)
                 for lo in range(0, QUAD, C):
-                    e = (base + lo) // C
-                    nc.tensor.transpose(gate_banks[base][:, lo : lo + C], gate_columns[:, e : e + 1].to_broadcast([P, P]), identity[:])
+                    column = (base - Q2 + lo) // C
+                    nc.tensor.transpose(gate_banks[base][:, lo : lo + C], gate_columns[:, column : column + 1].to_broadcast([P, P]), identity[:])
 
         banks = {}
         issued = {}
@@ -298,7 +298,7 @@ def tile_moe_pre_lin_relu_kernel(tc, xT, w_words, w_scales, b, gate, offs, pos1,
         for at, (first, end, index) in zip((area_f + BLOCK, area_f + BLOCK + CODES), LATE_BANKS):
             quantise(at, (2, first * C, end * C))
         for first, end, index in LATE_BANKS:
-            finish(first, end, end < E)
+            finish(first, end, end == E)
 
         sums = placed("sums", 4 * T, F32, pass_at[1])
 

@@ -14,19 +14,23 @@ BANK = 2048
 QUAD = 4 * C
 HALF = QUAD // 2
 GROUP = 2 * QUAD
-BLOCK = 2 * PACK * GROUP
+GATHERED = 4 * PACK
+ROUNDED = 2 * PACK
 CODES = 5 * GROUP
 EDGE = 64
 
 Q0, Q1, Q2, Q3, Q4, Q5, Q6 = range(0, S + 1, QUAD)
-WIDE = (T + 8, T + 8, Q3 + 8)
 FIRST_END = 544
-GPSIMD_END = Q3 - 32
-HELPED = (248, 248, 160)
+OPENING = C
+SECOND_END = 1504
+OWN_END = 1088
+GPSIMD_END = 1312
+LAST_EARLY = 2208
+WIDE = (T + 8, SECOND_END + 8, OWN_END + 8)
 VECTOR_RUN = 2
 GPSIMD_RUN = 4
 EARLY_BANKS = ((0, 4, 4), (4, 8, 5), (8, 12, 6), (12, 16, 7), (16, 20, 0))
-LATE_BANKS = ((22, 24, 2), (20, 22, 1))
+LATE_BANKS = ((22, 24, 1), (20, 21, 2), (21, 22, 3))
 TWICE, ALONE, STORE_CUT = 192, 448, 800
 
 FLOPS = 2 * K * S * N
@@ -64,14 +68,17 @@ def tile_moe_pre_lin_relu_kernel(tc, xT, w_words, w_scales, b, gate, offs, pos1,
         pass_at = [PACK * sum(window_bytes[:a]) for a in range(PASSES + 1)]
         gate_at = pass_at[PASSES]
         area_a = gate_at + 4 * Q3
-        area_b = area_a + 2 * BLOCK
-        columns_at = area_b + 2 * BLOCK + 2 * EDGE
-        area_c = columns_at + EDGE
-        area_d = area_c + 2 * BLOCK
-        identity_at = area_d + BLOCK
-        area_e = identity_at + 4 * P
-        area_f = area_e + 2 * BLOCK
-        rounded_at = [area_f + (3 + q) * BLOCK for q in range(5)]
+        area_e = area_a + ROUNDED * Q4
+        columns_at = area_e + GATHERED * (LAST_EARLY - SECOND_END)
+        area_b = columns_at + EDGE
+        area_d = area_b + GATHERED * SECOND_END
+        area_c = area_d + GATHERED * GROUP
+        area_f = area_c + GATHERED * Q3
+        rounded_0 = area_f + GATHERED * GROUP
+        rounded_1 = area_a
+        rounded_2 = area_d - EDGE - ROUNDED * Q4
+        rounded_3 = rounded_0 + ROUNDED * Q4
+        rounded_4 = rounded_3 + ROUNDED * GROUP
 
         warm = keep.tile([P, 16], F32, name="warm")
         nc.gpsimd.memset(warm[:, 0:8], 0.0)
@@ -93,17 +100,17 @@ def tile_moe_pre_lin_relu_kernel(tc, xT, w_words, w_scales, b, gate, offs, pos1,
         nc.sync.dma_start(offs_t[:], offs)
         for r in range(1, PACK):
             load_plane(0, r)
+        load_gate(0, OPENING)
         load_plane(1, 0)
-        load_gate(0, FIRST_END)
+        load_gate(OPENING, FIRST_END)
         load_plane(1, 1)
         load_gate(FIRST_END, Q3)
         for r in range(2, PACK):
             load_plane(1, r)
-        for r in range(PACK - 1):
+        for r in range(PACK):
             load_plane(2, r)
-        gate_rows = placed("gate_rows", C, F32, rounded_at[4])
+        gate_rows = placed("gate_rows", C, F32, area_f)
         nc.sync.dma_start(gate_rows[:], gate.rearrange("k (e c) -> (k e) c", c=C)[0:P, :])
-        load_plane(2, PACK - 1)
 
         w_scale = keep.tile([P, E * N], U8, name="w_scale", align_bytes=64)
         nc.vector.memset(w_scale[:].bitcast(I32), 0)
@@ -131,23 +138,30 @@ def tile_moe_pre_lin_relu_kernel(tc, xT, w_words, w_scales, b, gate, offs, pos1,
 
         gathered = {}
 
-        def gather(a, on_vector, at, lo, hi):
-            width = hi - lo
-            gathered[a, lo] = placed("gathered%d_%d" % (a, lo), PACK * width, F32, at)
-            for r in range(PACK):
-                values = gathered[a, lo][:, r * width : (r + 1) * width]
+        def place_gathered(a, lo, hi, at):
+            tile = placed("gathered%d_%d" % (a, lo), PACK * (hi - lo), F32, at)
+            gathered[a, lo] = tile[:]
+
+        def gather(a, on_vector, first, lo, hi, planes=range(PACK)):
+            tile = gathered[a, first].rearrange("p (r c) -> p r c", r=PACK)
+            for r in planes:
+                values = tile[:, r, lo - first : hi - first]
                 looked_up = windows[a, r][:].indirect(entries(offs_t, lo, hi))
                 if on_vector:
                     nc.vector.tensor_copy(values, looked_up)
                 else:
                     nc.scalar.activation(values, looked_up, COPY)
 
+        def gather_on_scalar(a, lo, hi, at):
+            place_gathered(a, lo, hi, at)
+            gather(a, False, lo, lo, hi)
+
         rounded = {}
 
         def place_rounded(at, width, *runs):
-            tile = placed("rounded%d_%d" % runs[0], PACK * width, BF16, at)
+            tile = placed("rounded%d_%d" % runs[0], PACK * width * len(runs), BF16, at)
             for index, run in enumerate(runs):
-                rounded[run] = tile[:, PACK * (width // len(runs)) * index :]
+                rounded[run] = tile[:, PACK * width * index :]
 
         def rounded_view(a, lo, hi):
             base = max(first for a_run, first in rounded if a_run == a and first <= lo)
@@ -156,16 +170,13 @@ def tile_moe_pre_lin_relu_kernel(tc, xT, w_words, w_scales, b, gate, offs, pos1,
         def product(engine, run, a, first, lo, hi, gates):
             engine.tensor_tensor(
                 rounded_view(a, lo, hi).rearrange("p (c i r) -> p c r i", r=PACK, i=run),
-                gathered[a, first][:].rearrange("p (r c i) -> p c r i", r=PACK, i=run)[:, (lo - first) // run : (hi - first) // run],
+                gathered[a, first].rearrange("p (r c i) -> p c r i", r=PACK, i=run)[:, (lo - first) // run : (hi - first) // run],
                 gates.rearrange("p (c i) -> p c i", i=run).unsqueeze(2).broadcast_to([P, (hi - lo) // run, PACK, run]),
                 MULT,
             )
 
-        gate_tiles = [(gate_early, 0)]
-
         def multiply_on_gpsimd(a, first, lo, hi):
-            gate_tile, base = gate_tiles[lo >= Q5]
-            product(nc.gpsimd, GPSIMD_RUN, a, first, lo, hi, gate_tile[:, lo - base : hi - base])
+            product(nc.gpsimd, GPSIMD_RUN, a, first, lo, hi, gate_early[:, lo:hi])
 
         gate_banks = {}
 
@@ -174,18 +185,19 @@ def tile_moe_pre_lin_relu_kernel(tc, xT, w_words, w_scales, b, gate, offs, pos1,
             product(nc.vector, VECTOR_RUN, a, first, lo, hi, gate_banks[base][:, lo - base : hi - base])
 
         def spread_gate():
-            identity = placed("identity", P, F32, identity_at)
+            first_expert = GPSIMD_END // C
+            identity = placed("identity", P, F32, columns_at - 4 * P)
             make_identity(nc, identity[:])
             turned = psum.tile([P, P], F32, name="turned", offset=4 * BANK)
             nc.tensor.transpose(turned[:], gate_rows[:], identity[:])
-            gate_columns = placed("gate_columns", E - Q2 // C, F32, columns_at)
-            nc.vector.tensor_copy(gate_columns[:], turned[:, Q2 // C : E])
+            gate_columns = placed("gate_columns", E - first_expert, F32, columns_at)
+            nc.scalar.copy(gate_columns[:], turned[:, first_expert:E])
             for base in (Q3, Q4, Q2, Q5):
                 index = (base - Q2) // QUAD
                 gate_banks[base] = psum.tile([P, QUAD], F32, name="gate_bank%d" % index, offset=index * BANK)
-                for lo in range(0, QUAD, C):
-                    column = (base - Q2 + lo) // C
-                    nc.tensor.transpose(gate_banks[base][:, lo : lo + C], gate_columns[:, column : column + 1].to_broadcast([P, P]), identity[:])
+                for e in range(max(base // C, first_expert), (base + QUAD) // C):
+                    column = gate_columns[:, e - first_expert : e - first_expert + 1]
+                    nc.tensor.transpose(gate_banks[base][:, e * C - base : (e + 1) * C - base], column.to_broadcast([P, P]), identity[:])
 
         banks = {}
         issued = {}
@@ -210,11 +222,11 @@ def tile_moe_pre_lin_relu_kernel(tc, xT, w_words, w_scales, b, gate, offs, pos1,
                 stop=issued[first] == total,
             )
 
-        def quantise(at, *runs):
+        def quantise(words_at, scales_at, *runs):
             a, lo = runs[0][0:2]
             width = sum(end - first for a_run, first, end in runs)
-            words = placed("words%d_%d" % (a, lo), width, U32, at)
-            scale_bytes = placed("bytes%d_%d" % (a, lo), width, U8, at + 4 * width)
+            words = placed("words%d_%d" % (a, lo), width, U32, words_at)
+            scale_bytes = placed("bytes%d_%d" % (a, lo), width, U8, scales_at)
             nc.vector.quantize_mx(words[:].bitcast(FP8X4), scale_bytes[:], rounded_view(a, lo, lo + width))
             column = 0
             for a_run, first, end in runs:
@@ -222,50 +234,56 @@ def tile_moe_pre_lin_relu_kernel(tc, xT, w_words, w_scales, b, gate, offs, pos1,
                     contract(a_run, slot // C, words[:, column : column + C], scale_bytes[:, column : column + C])
                     column = column + C
 
-        gather(0, True, area_a, 0, FIRST_END)
-        gather(0, False, area_c, FIRST_END, Q3)
-        gather(1, True, area_e, 0, Q2)
-        gather(1, False, area_d, Q2, Q3)
-        gather(1, False, area_b, Q3, Q5)
-        place_rounded(rounded_at[0], GROUP, (0, Q0), (0, Q1))
-        place_rounded(rounded_at[1], GROUP, (0, Q2), (0, Q3))
-        place_rounded(rounded_at[2], GROUP, (1, Q0), (1, Q1))
-        place_rounded(rounded_at[3], GROUP, (1, Q2), (1, Q3))
-        place_rounded(rounded_at[4], GROUP, (1, Q4), (2, Q4))
-        multiply_on_gpsimd(0, 0, 0, FIRST_END)
-        multiply_on_gpsimd(0, FIRST_END, FIRST_END, Q2)
-        multiply_on_gpsimd(0, FIRST_END, Q2, Q3)
-        gather(2, True, area_f, 0, Q3)
-        gather(2, False, area_a, Q3, Q5)
-        multiply_on_gpsimd(1, 0, 0, Q2)
-        multiply_on_gpsimd(1, Q2, Q2, GPSIMD_END)
-        place_rounded(area_c + BLOCK, GROUP, (2, Q0), (2, Q1))
-        multiply_on_gpsimd(2, 0, 0, Q2)
-        gate_late = placed("gate_late", max(HELPED), F32, gate_at)
-        nc.sync.dma_start(gate_late[:], gate[0:P, Q5 : Q5 + max(HELPED)])
-        gate_tiles.append((gate_late, Q5))
+        place_gathered(0, 0, FIRST_END, area_a)
+        gather(0, True, 0, 0, FIRST_END, range(PACK - 1))
+        gather(0, True, 0, 0, OPENING, (PACK - 1,))
+        gather(0, True, 0, OPENING, FIRST_END, (PACK - 1,))
+        gather_on_scalar(0, FIRST_END, Q3, area_a + GATHERED * FIRST_END)
+        place_gathered(1, 0, SECOND_END, area_b)
+        gather(1, True, 0, 0, SECOND_END)
+        gather_on_scalar(0, Q3, Q5, area_d)
+        place_rounded(rounded_0, Q4, (0, Q0))
+        multiply_on_gpsimd(0, 0, 0, OPENING)
+        multiply_on_gpsimd(0, 0, OPENING, FIRST_END)
+        multiply_on_gpsimd(0, FIRST_END, FIRST_END, Q3)
+        place_gathered(2, 0, Q3, area_c)
+        gather(2, True, 0, 0, OWN_END)
+        gather(2, False, 0, OWN_END, Q3)
+        place_rounded(rounded_1, Q4, (1, Q0))
+        multiply_on_gpsimd(1, 0, 0, SECOND_END)
         spread_gate()
-        gather(0, False, area_c - EDGE, Q3, Q4)
-        gather(0, False, area_e - EDGE, Q4, Q6)
-        gather(1, False, area_d + EDGE, Q5, Q6)
-        gather(2, False, area_f, Q5, Q6)
-        multiply(1, Q3, Q3, Q4)
-        multiply(1, Q3, Q4, Q5)
-        multiply(1, Q2, GPSIMD_END, Q3)
-        place_rounded(area_b, GROUP, (2, Q2), (2, Q3))
-        multiply(2, 0, Q2, Q3)
-        multiply(2, Q3, Q4, Q5)
-        multiply(2, Q3, Q3, Q4)
+        gather_on_scalar(2, Q3, Q5, area_f)
+        gather_on_scalar(1, SECOND_END, LAST_EARLY, area_e)
+        gather_on_scalar(1, LAST_EARLY, Q5, columns_at)
+        place_rounded(rounded_2, Q4, (2, Q0))
+        place_rounded(rounded_3, QUAD, (0, Q4), (1, Q4))
+        place_rounded(rounded_4, QUAD, (2, Q4))
         multiply(0, Q3, Q3, Q4)
+        multiply(0, Q3, Q4, Q5)
+        multiply_on_gpsimd(2, 0, 0, GPSIMD_END)
+        multiply(2, 0, GPSIMD_END, Q3)
+        multiply(2, Q3, Q3, Q4)
+        multiply(2, Q3, Q4, Q5)
+        late = placed("gathered_late", 2 * PACK * QUAD, F32, area_d - EDGE)
+        for a in range(2):
+            gathered[a, Q5] = late[:, a * PACK * QUAD : (a + 1) * PACK * QUAD]
+            gather(a, False, Q5, Q5, Q6)
+        multiply(1, SECOND_END, SECOND_END, Q3)
+        multiply(1, SECOND_END, Q3, Q4)
+        multiply(1, SECOND_END, Q4, LAST_EARLY)
+        multiply(1, LAST_EARLY, LAST_EARLY, Q5)
+        gate_late = placed("gate_late", QUAD, F32, gate_at)
+        nc.sync.dma_start(gate_late[:], gate[0:P, Q5:Q6])
+        gather_on_scalar(2, Q5 + HALF, Q6, area_c + GATHERED * QUAD)
+        gather_on_scalar(2, Q5, Q5 + HALF, area_c)
 
         open_banks(EARLY_BANKS)
-        quantise(area_a, (0, Q0, Q2))
-        quantise(area_a + CODES, (1, Q0, Q2))
-        quantise(rounded_at[0], (1, Q2, Q4))
-        quantise(rounded_at[2], (1, Q4, Q5), (2, Q4, Q5))
-        quantise(rounded_at[3], (2, Q0, Q2))
-        quantise(rounded_at[4], (2, Q2, Q4))
-        quantise(area_c + BLOCK, (0, Q2, Q4))
+        for index, run in enumerate(((0, Q0, Q2), (0, Q2, Q4), (1, Q0, Q2))):
+            quantise(area_f + index * 4 * GROUP, index * GROUP, run)
+        for index, runs in enumerate((((1, Q2, Q4),), ((0, Q4, Q5), (1, Q4, Q5)), ((2, Q0, Q2),))):
+            quantise(rounded_0 + index * CODES + GROUP, rounded_0 + index * CODES, *runs)
+        quantise(rounded_1 + GROUP, rounded_1, (2, Q2, Q4))
+        quantise(area_f - 4 * QUAD, rounded_1 + CODES, (2, Q4, Q5))
         y = placed("y", S, F32, 0)
 
         def finish(first, end, on_vector):
@@ -275,30 +293,25 @@ def tile_moe_pre_lin_relu_kernel(tc, xT, w_words, w_scales, b, gate, offs, pos1,
                 else:
                     nc.scalar.activation(y[:, e * C : (e + 1) * C], banks[e][0], RELU, bias=bias[:, e : e + 1])
 
-        finish(0, Q4 // C, False)
+        finish(0, Q5 // C, False)
 
-        place_rounded(area_b + EDGE, GROUP, (0, Q4), (0, Q5))
-        place_rounded(area_b + EDGE - BLOCK // 2, QUAD, (1, Q5))
-        multiply_on_gpsimd(0, Q4, Q5, Q5 + HELPED[0])
-        multiply_on_gpsimd(1, Q5, Q5, Q5 + HELPED[1])
-        multiply(0, Q4, Q4, Q5)
-        multiply(0, Q4, Q5 + HELPED[0], Q6)
-        multiply(1, Q5, Q5 + HELPED[1], Q6)
+        place_rounded(rounded_2, QUAD, (0, Q5), (1, Q5), (2, Q5))
+        product(nc.gpsimd, GPSIMD_RUN, 0, Q5, Q5, Q6, gate_late[:])
+        multiply(1, Q5, Q5, Q6)
+        multiply(2, Q5 + HALF, Q5 + HALF, Q6)
+        multiply(2, Q5, Q5, Q5 + HALF)
 
         open_banks(LATE_BANKS)
-        quantise(rounded_at[1], (0, Q4, Q6))
-        quantise(rounded_at[1] + CODES, (1, Q5, Q6))
-        finish(Q4 // C, Q5 // C, False)
-
-        place_rounded(area_b + EDGE, HALF, (2, Q5))
-        place_rounded(area_b + EDGE + BLOCK // 4, HALF, (2, Q5 + HALF))
-        multiply_on_gpsimd(2, Q5, Q5, Q5 + HELPED[2])
-        multiply(2, Q5, Q5 + HALF, Q6)
-        multiply(2, Q5, Q5 + HELPED[2], Q5 + HALF)
-        for at, (first, end, index) in zip((area_f + BLOCK, area_f + BLOCK + CODES), LATE_BANKS):
-            quantise(at, (2, first * C, end * C))
-        for first, end, index in LATE_BANKS:
-            finish(first, end, end == E)
+        scales_at = area_c + GATHERED * QUAD
+        words_at = scales_at + GATHERED * HALF
+        middle = Q5 + HALF
+        for run in ((1, middle, Q6), (2, middle, Q6), (0, middle, Q6), (1, Q5, middle), (0, Q5, middle), (2, Q5, Q5 + C), (2, Q5 + C, middle)):
+            quantise(words_at, scales_at, run)
+            words_at = words_at + 4 * (run[2] - run[1])
+            scales_at = scales_at + run[2] - run[1]
+        finish(22, 24, True)
+        finish(20, 21, False)
+        finish(21, 22, True)
 
         sums = placed("sums", 4 * T, F32, pass_at[1])
 

@@ -26,6 +26,7 @@ SECOND_END = 1504
 OWN_END = 1088
 GPSIMD_END = 1312
 LAST_EARLY = 2208
+HELPED = 416
 WIDE = (T + 8, SECOND_END + 8, OWN_END + 8)
 VECTOR_RUN = 2
 GPSIMD_RUN = 4
@@ -272,8 +273,8 @@ def tile_moe_pre_lin_relu_kernel(tc, xT, w_words, w_scales, b, gate, offs, pos1,
         multiply(1, SECOND_END, Q3, Q4)
         multiply(1, SECOND_END, Q4, LAST_EARLY)
         multiply(1, LAST_EARLY, LAST_EARLY, Q5)
-        gate_late = placed("gate_late", QUAD, F32, gate_at)
-        nc.sync.dma_start(gate_late[:], gate[0:P, Q5:Q6])
+        gate_late = placed("gate_late", HELPED, F32, gate_at)
+        nc.sync.dma_start(gate_late[:], gate[0:P, Q5 : Q5 + HELPED])
         gather_on_scalar(2, Q5 + HALF, Q6, area_c + GATHERED * QUAD)
         gather_on_scalar(2, Q5, Q5 + HALF, area_c)
 
@@ -295,20 +296,23 @@ def tile_moe_pre_lin_relu_kernel(tc, xT, w_words, w_scales, b, gate, offs, pos1,
 
         finish(0, Q5 // C, False)
 
-        place_rounded(rounded_2, QUAD, (0, Q5), (1, Q5), (2, Q5))
-        product(nc.gpsimd, GPSIMD_RUN, 0, Q5, Q5, Q6, gate_late[:])
+        middle = Q5 + HALF
+        place_rounded(rounded_2, QUAD, (0, Q5), (1, Q5))
+        place_rounded(rounded_2 + ROUNDED * GROUP, HALF, (2, middle))
+        product(nc.gpsimd, GPSIMD_RUN, 0, Q5, Q5, Q5 + HELPED, gate_late[:])
+        multiply(0, Q5, Q5 + HELPED, Q6)
         multiply(1, Q5, Q5, Q6)
-        multiply(2, Q5 + HALF, Q5 + HALF, Q6)
-        multiply(2, Q5, Q5, Q5 + HALF)
+        multiply(2, middle, middle, Q6)
 
         open_banks(LATE_BANKS)
-        scales_at = area_c + GATHERED * QUAD
-        words_at = scales_at + GATHERED * HALF
-        middle = Q5 + HALF
-        for run in ((1, middle, Q6), (2, middle, Q6), (0, middle, Q6), (1, Q5, middle), (0, Q5, middle), (2, Q5, Q5 + C), (2, Q5 + C, middle)):
-            quantise(words_at, scales_at, run)
-            words_at = words_at + 4 * (run[2] - run[1])
-            scales_at = scales_at + run[2] - run[1]
+        codes_at = area_c + GATHERED * GROUP
+        quantise(area_d + GROUP, area_d, (0, Q5, Q6), (1, Q5, Q6))
+        quantise(codes_at + HALF, codes_at, (2, middle, Q6))
+        place_rounded(rounded_2, HALF, (2, Q5))
+        multiply(2, Q5, Q5, middle)
+        for index, slot in enumerate((Q5, Q5 + C)):
+            at = codes_at + 5 * HALF + index * 5 * C
+            quantise(at + C, at, (2, slot, slot + C))
         finish(22, 24, True)
         finish(20, 21, False)
         finish(21, 22, True)

@@ -22,16 +22,15 @@ EDGE = 64
 Q0, Q1, Q2, Q3, Q4, Q5, Q6 = range(0, S + 1, QUAD)
 FIRST_END = 544
 OPENING = C
-SECOND_END = 1504
-OWN_END = 1088
-GPSIMD_END = 1312
-LAST_EARLY = 2208
-HELPED = 416
+SECOND_END = 1440
+OWN_END = 1120
+GPSIMD_END = 1184
+HELPED = 160
 WIDE = (T + 8, SECOND_END + 8, OWN_END + 8)
 VECTOR_RUN = 2
 GPSIMD_RUN = 4
 EARLY_BANKS = ((0, 4, 4), (4, 8, 5), (8, 12, 6), (12, 16, 7), (16, 20, 0))
-LATE_BANKS = ((22, 24, 1), (20, 21, 2), (21, 22, 3))
+LATE_BANKS = ((22, 24, 2), (20, 22, 1))
 TWICE, ALONE, STORE_CUT = 192, 448, 800
 
 FLOPS = 2 * K * S * N
@@ -70,16 +69,15 @@ def tile_moe_pre_lin_relu_kernel(tc, xT, w_words, w_scales, b, gate, offs, pos1,
         gate_at = pass_at[PASSES]
         area_a = gate_at + 4 * Q3
         area_e = area_a + ROUNDED * Q4
-        columns_at = area_e + GATHERED * (LAST_EARLY - SECOND_END)
+        columns_at = area_e + GATHERED * (Q4 - SECOND_END)
         area_b = columns_at + EDGE
         area_d = area_b + GATHERED * SECOND_END
         area_c = area_d + GATHERED * GROUP
         area_f = area_c + GATHERED * Q3
         rounded_0 = area_f + GATHERED * GROUP
         rounded_1 = area_a
-        rounded_2 = area_d - EDGE - ROUNDED * Q4
+        rounded_2 = area_d - ROUNDED * Q4
         rounded_3 = rounded_0 + ROUNDED * Q4
-        rounded_4 = rounded_3 + ROUNDED * GROUP
 
         warm = keep.tile([P, 16], F32, name="warm")
         nc.gpsimd.memset(warm[:, 0:8], 0.0)
@@ -254,37 +252,29 @@ def tile_moe_pre_lin_relu_kernel(tc, xT, w_words, w_scales, b, gate, offs, pos1,
         multiply_on_gpsimd(1, 0, 0, SECOND_END)
         spread_gate()
         gather_on_scalar(2, Q3, Q5, area_f)
-        gather_on_scalar(1, SECOND_END, LAST_EARLY, area_e)
-        gather_on_scalar(1, LAST_EARLY, Q5, columns_at)
+        gather_on_scalar(1, SECOND_END, Q4, area_e)
         place_rounded(rounded_2, Q4, (2, Q0))
-        place_rounded(rounded_3, QUAD, (0, Q4), (1, Q4))
-        place_rounded(rounded_4, QUAD, (2, Q4))
+        place_rounded(rounded_3, QUAD, (0, Q4), (2, Q4))
         multiply(0, Q3, Q3, Q4)
         multiply(0, Q3, Q4, Q5)
         multiply_on_gpsimd(2, 0, 0, GPSIMD_END)
         multiply(2, 0, GPSIMD_END, Q3)
+        gather_on_scalar(1, Q4, Q6, area_d)
         multiply(2, Q3, Q3, Q4)
         multiply(2, Q3, Q4, Q5)
-        late = placed("gathered_late", 2 * PACK * QUAD, F32, area_d - EDGE)
-        for a in range(2):
-            gathered[a, Q5] = late[:, a * PACK * QUAD : (a + 1) * PACK * QUAD]
-            gather(a, False, Q5, Q5, Q6)
         multiply(1, SECOND_END, SECOND_END, Q3)
         multiply(1, SECOND_END, Q3, Q4)
-        multiply(1, SECOND_END, Q4, LAST_EARLY)
-        multiply(1, LAST_EARLY, LAST_EARLY, Q5)
-        gate_late = placed("gate_late", HELPED, F32, gate_at)
-        nc.sync.dma_start(gate_late[:], gate[0:P, Q5 : Q5 + HELPED])
-        gather_on_scalar(2, Q5 + HALF, Q6, area_c + GATHERED * QUAD)
-        gather_on_scalar(2, Q5, Q5 + HALF, area_c)
+        gate_late = placed("gate_late", QUAD + HELPED, F32, gate_at)
+        nc.sync.dma_start(gate_late[:], gate[0:P, Q4 : Q5 + HELPED])
+        gather_on_scalar(0, Q5, Q6, area_e)
+        gather_on_scalar(2, Q5, Q6, area_e + GATHERED * QUAD)
 
         open_banks(EARLY_BANKS)
         for index, run in enumerate(((0, Q0, Q2), (0, Q2, Q4), (1, Q0, Q2))):
-            quantise(area_f + index * 4 * GROUP, index * GROUP, run)
-        for index, runs in enumerate((((1, Q2, Q4),), ((0, Q4, Q5), (1, Q4, Q5)), ((2, Q0, Q2),))):
-            quantise(rounded_0 + index * CODES + GROUP, rounded_0 + index * CODES, *runs)
-        quantise(rounded_1 + GROUP, rounded_1, (2, Q2, Q4))
-        quantise(area_f - 4 * QUAD, rounded_1 + CODES, (2, Q4, Q5))
+            quantise(area_f + index * CODES + GROUP, area_f + index * CODES, run)
+        for index, run in enumerate(((1, Q2, Q4), (2, Q0, Q2), (2, Q2, Q4))):
+            quantise(rounded_0 + index * CODES + GROUP, rounded_0 + index * CODES, run)
+        quantise(area_c, rounded_1, (0, Q4, Q5), (2, Q4, Q5))
         y = placed("y", S, F32, 0)
 
         def finish(first, end, on_vector):
@@ -294,28 +284,30 @@ def tile_moe_pre_lin_relu_kernel(tc, xT, w_words, w_scales, b, gate, offs, pos1,
                 else:
                     nc.scalar.activation(y[:, e * C : (e + 1) * C], banks[e][0], RELU, bias=bias[:, e : e + 1])
 
-        finish(0, Q5 // C, False)
+        finish(0, Q4 // C, False)
 
-        middle = Q5 + HALF
-        place_rounded(rounded_2, QUAD, (0, Q5), (1, Q5))
-        place_rounded(rounded_2 + ROUNDED * GROUP, HALF, (2, middle))
-        product(nc.gpsimd, GPSIMD_RUN, 0, Q5, Q5, Q5 + HELPED, gate_late[:])
-        multiply(0, Q5, Q5 + HELPED, Q6)
-        multiply(1, Q5, Q5, Q6)
-        multiply(2, middle, middle, Q6)
+        place_rounded(rounded_2, GROUP, (1, Q4))
+        place_rounded(rounded_2 + ROUNDED * GROUP, QUAD, (0, Q5))
+        product(nc.gpsimd, GPSIMD_RUN, 1, Q4, Q4, Q5, gate_late[:, 0:QUAD])
+        multiply(1, Q4, Q5, Q6)
+        multiply(0, Q5, Q5, Q6)
 
         open_banks(LATE_BANKS)
-        codes_at = area_c + GATHERED * GROUP
-        quantise(area_d + GROUP, area_d, (0, Q5, Q6), (1, Q5, Q6))
-        quantise(codes_at + HALF, codes_at, (2, middle, Q6))
+        quantise(area_d + GROUP, area_d, (1, Q4, Q6))
+        quantise(area_d + CODES + QUAD, area_d + CODES, (0, Q5, Q6))
+        finish(Q4 // C, Q5 // C, False)
+
+        middle = Q5 + HALF
         place_rounded(rounded_2, HALF, (2, Q5))
-        multiply(2, Q5, Q5, middle)
-        for index, slot in enumerate((Q5, Q5 + C)):
-            at = codes_at + 5 * HALF + index * 5 * C
-            quantise(at + C, at, (2, slot, slot + C))
-        finish(22, 24, True)
-        finish(20, 21, False)
-        finish(21, 22, True)
+        place_rounded(rounded_2 + ROUNDED * HALF, HALF, (2, middle))
+        product(nc.gpsimd, GPSIMD_RUN, 2, Q5, Q5, Q5 + HELPED, gate_late[:, QUAD:])
+        multiply(2, Q5, middle, Q6)
+        multiply(2, Q5, Q5 + HELPED, middle)
+        for index, (first, end, bank_index) in enumerate(LATE_BANKS):
+            at = area_c + CODES + index * 5 * HALF
+            quantise(at + HALF, at, (2, first * C, end * C))
+        for first, end, bank_index in LATE_BANKS:
+            finish(first, end, end == E)
 
         sums = placed("sums", 4 * T, F32, pass_at[1])
 

@@ -23,8 +23,8 @@ Q0, Q1, Q2, Q3, Q4, Q5, Q6 = range(0, S + 1, QUAD)
 FIRST_END = 544
 OPENING = C
 SECOND_END = 1440
-OWN_END = 1120
-GPSIMD_END = 1184
+OWN_END = 1152
+GPSIMD_END = 1120
 HELPED = 160
 WIDE = (T + 8, SECOND_END + 8, OWN_END + 8)
 VECTOR_RUN = 2

@@ -24,9 +24,8 @@ FIRST_END = 544
 OPENING = C
 SECOND_END = 1440
 OWN_END = 1152
-GPSIMD_END = 1120
 HELPED = 160
-WIDE = (T + 8, SECOND_END + 8, OWN_END + 8)
+WIDE = (T + 8, SECOND_END + 8, Q5 - OWN_END + 8)
 VECTOR_RUN = 2
 GPSIMD_RUN = 4
 EARLY_BANKS = ((0, 4, 4), (4, 8, 5), (8, 12, 6), (12, 16, 7), (16, 20, 0))
@@ -73,8 +72,8 @@ def tile_moe_pre_lin_relu_kernel(tc, xT, w_words, w_scales, b, gate, offs, pos1,
         area_b = columns_at + EDGE
         area_d = area_b + GATHERED * SECOND_END
         area_c = area_d + GATHERED * GROUP
-        area_f = area_c + GATHERED * Q3
-        rounded_0 = area_f + GATHERED * GROUP
+        area_f = area_c + GATHERED * OWN_END
+        rounded_0 = area_f + GATHERED * (Q5 - OWN_END)
         rounded_1 = area_a
         rounded_2 = area_d - ROUNDED * Q4
         rounded_3 = rounded_0 + ROUNDED * Q4
@@ -106,10 +105,11 @@ def tile_moe_pre_lin_relu_kernel(tc, xT, w_words, w_scales, b, gate, offs, pos1,
         load_gate(FIRST_END, Q3)
         for r in range(2, PACK):
             load_plane(1, r)
-        for r in range(PACK):
+        for r in range(PACK - 1):
             load_plane(2, r)
-        gate_rows = placed("gate_rows", C, F32, area_f)
+        gate_rows = placed("gate_rows", C, F32, rounded_3)
         nc.sync.dma_start(gate_rows[:], gate.rearrange("k (e c) -> (k e) c", c=C)[0:P, :])
+        load_plane(2, PACK - 1)
 
         w_scale = keep.tile([P, E * N], U8, name="w_scale", align_bytes=64)
         nc.vector.memset(w_scale[:].bitcast(I32), 0)
@@ -184,14 +184,14 @@ def tile_moe_pre_lin_relu_kernel(tc, xT, w_words, w_scales, b, gate, offs, pos1,
             product(nc.vector, VECTOR_RUN, a, first, lo, hi, gate_banks[base][:, lo - base : hi - base])
 
         def spread_gate():
-            first_expert = GPSIMD_END // C
+            first_expert = OWN_END // C
             identity = placed("identity", P, F32, columns_at - 4 * P)
             make_identity(nc, identity[:])
             turned = psum.tile([P, P], F32, name="turned", offset=4 * BANK)
             nc.tensor.transpose(turned[:], gate_rows[:], identity[:])
             gate_columns = placed("gate_columns", E - first_expert, F32, columns_at)
-            nc.scalar.copy(gate_columns[:], turned[:, first_expert:E])
-            for base in (Q3, Q4, Q2, Q5):
+            nc.vector.tensor_copy(gate_columns[:], turned[:, first_expert:E])
+            for base in (Q5, Q2, Q3, Q4):
                 index = (base - Q2) // QUAD
                 gate_banks[base] = psum.tile([P, QUAD], F32, name="gate_bank%d" % index, offset=index * BANK)
                 for e in range(max(base // C, first_expert), (base + QUAD) // C):
@@ -245,23 +245,22 @@ def tile_moe_pre_lin_relu_kernel(tc, xT, w_words, w_scales, b, gate, offs, pos1,
         multiply_on_gpsimd(0, 0, 0, OPENING)
         multiply_on_gpsimd(0, 0, OPENING, FIRST_END)
         multiply_on_gpsimd(0, FIRST_END, FIRST_END, Q3)
-        place_gathered(2, 0, Q3, area_c)
+        place_gathered(2, 0, OWN_END, area_c)
         gather(2, True, 0, 0, OWN_END)
-        gather(2, False, 0, OWN_END, Q3)
+        gather_on_scalar(2, OWN_END, Q5, area_f)
         place_rounded(rounded_1, Q4, (1, Q0))
         multiply_on_gpsimd(1, 0, 0, SECOND_END)
         spread_gate()
-        gather_on_scalar(2, Q3, Q5, area_f)
         gather_on_scalar(1, SECOND_END, Q4, area_e)
         place_rounded(rounded_2, Q4, (2, Q0))
         place_rounded(rounded_3, QUAD, (0, Q4), (2, Q4))
         multiply(0, Q3, Q3, Q4)
         multiply(0, Q3, Q4, Q5)
-        multiply_on_gpsimd(2, 0, 0, GPSIMD_END)
-        multiply(2, 0, GPSIMD_END, Q3)
+        multiply_on_gpsimd(2, 0, 0, OWN_END)
+        multiply(2, OWN_END, OWN_END, Q3)
         gather_on_scalar(1, Q4, Q6, area_d)
-        multiply(2, Q3, Q3, Q4)
-        multiply(2, Q3, Q4, Q5)
+        multiply(2, OWN_END, Q3, Q4)
+        multiply(2, OWN_END, Q4, Q5)
         multiply(1, SECOND_END, SECOND_END, Q3)
         multiply(1, SECOND_END, Q3, Q4)
         gate_late = placed("gate_late", QUAD + HELPED, F32, gate_at)

@@ -22,8 +22,8 @@ EDGE = 64
 Q0, Q1, Q2, Q3, Q4, Q5, Q6 = range(0, S + 1, QUAD)
 FIRST_END = 544
 OPENING = C
-SECOND_END = 1440
-OWN_END = 1152
+SECOND_END = 1312
+OWN_END = 1280
 HELPED = 160
 WIDE = (T + 8, SECOND_END + 8, Q5 - OWN_END + 8)
 VECTOR_RUN = 2

from contextlib import ExitStack

import concourse.mybir as mybir
from concourse.masks import make_identity

K, T, E, C, N = 1536, 1024, 24, 128, 128
S = E * C
P = 128
PACK = 4
K_PASS = P * PACK
PASSES = K // K_PASS
PER_COLUMN = 16
BANK = 2048
QUAD = 4 * C
HALF = QUAD // 2
GROUP = 2 * QUAD
GATHERED = 4 * PACK
ROUNDED = 2 * PACK
CODES = 5 * GROUP
EDGE = 64

Q0, Q1, Q2, Q3, Q4, Q5, Q6 = range(0, S + 1, QUAD)
FIRST_END = 544
OPENING = C
SECOND_END = 1312
OWN_END = 1280
HELPED = 160
WIDE = (T + 8, SECOND_END + 8, Q5 - OWN_END + 8)
VECTOR_RUN = 2
GPSIMD_RUN = 4
EARLY_BANKS = ((0, 4, 4), (4, 8, 5), (8, 12, 6), (12, 16, 7), (16, 20, 0))
LATE_BANKS = ((22, 24, 2), (20, 22, 1))
TWICE, ALONE, STORE_CUT = 192, 448, 800

FLOPS = 2 * K * S * N
BYTES = 4 * K * T + E * K * N + E * K * N // 32 + 4 * N * E + 4 * S + 2 * P * (S + 3 * T) // PER_COLUMN + 4 * N * T

F32 = mybir.dt.float32
BF16 = mybir.dt.bfloat16
I32 = mybir.dt.int32
U32 = mybir.dt.uint32
U16 = mybir.dt.uint16
U8 = mybir.dt.uint8
FP8X4 = mybir.dt.float8_e4m3fn_x4
RELU = mybir.ActivationFunctionType.Relu
COPY = mybir.ActivationFunctionType.Copy
ADD = mybir.AluOpType.add
MULT = mybir.AluOpType.mult
MAX = mybir.AluOpType.max


def entries(list_tile, lo, hi):
    return list_tile[:, lo // PER_COLUMN : hi // PER_COLUMN]


def tile_moe_pre_lin_relu_kernel(tc, xT, w_words, w_scales, b, gate, offs, pos1, pos2, pos3, out):
    nc = tc.nc
    with ExitStack() as ctx:
        keep = ctx.enter_context(tc.tile_pool(name="keep", bufs=1))
        stage = ctx.enter_context(tc.tile_pool(name="stage", bufs=1))
        psum = ctx.enter_context(tc.psum_pool(name="psum", bufs=1))

        def placed(name, columns, dtype, offset):
            return stage.tile([P, columns], dtype, name=name, offset=offset, align_bytes=64)

        window_bytes = [4 * columns + 32 for columns in WIDE]
        pass_at = [PACK * sum(window_bytes[:a]) for a in range(PASSES + 1)]
        gate_at = pass_at[PASSES]
        area_a = gate_at + 4 * Q3
        area_e = area_a + ROUNDED * Q4
        columns_at = area_e + GATHERED * (Q4 - SECOND_END)
        area_b = columns_at + EDGE
        area_d = area_b + GATHERED * SECOND_END
        area_c = area_d + GATHERED * GROUP
        area_f = area_c + GATHERED * OWN_END
        rounded_0 = area_f + GATHERED * (Q5 - OWN_END)
        rounded_1 = area_a
        rounded_2 = area_d - ROUNDED * Q4
        rounded_3 = rounded_0 + ROUNDED * Q4

        warm = keep.tile([P, 16], F32, name="warm")
        nc.gpsimd.memset(warm[:, 0:8], 0.0)
        nc.scalar.activation(warm[:, 8:9], warm[:, 0:1], RELU)

        offs_t = keep.tile([P, S // PER_COLUMN], U16, name="offs_t")
        gate_early = placed("gate_early", Q3, F32, gate_at)
        windows = {}

        def load_plane(a, r):
            window = placed("window%d_%d" % (a, r), WIDE[a], F32, pass_at[a] + r * window_bytes[a])
            nc.sync.dma_start(window[:, 0:T], xT[K_PASS * a + r : K_PASS * (a + 1) : PACK, :])
            windows[a, r] = window

        def load_gate(lo, hi):
            nc.sync.dma_start(gate_early[:, lo:hi], gate[0:P, lo:hi])

        load_plane(0, 0)
        nc.sync.dma_start(offs_t[:], offs)
        for r in range(1, PACK):
            load_plane(0, r)
        load_gate(0, OPENING)
        load_plane(1, 0)
        load_gate(OPENING, FIRST_END)
        load_plane(1, 1)
        load_gate(FIRST_END, Q3)
        for r in range(2, PACK):
            load_plane(1, r)
        for r in range(PACK - 1):
            load_plane(2, r)
        gate_rows = placed("gate_rows", C, F32, rounded_3)
        nc.sync.dma_start(gate_rows[:], gate.rearrange("k (e c) -> (k e) c", c=C)[0:P, :])
        load_plane(2, PACK - 1)

        w_scale = keep.tile([P, E * N], U8, name="w_scale", align_bytes=64)
        nc.vector.memset(w_scale[:].bitcast(I32), 0)
        scale_dst = w_scale[:].bitcast(I32).rearrange("p (e n) -> p e n", n=N // 4)
        for a in range(PASSES):
            scale_src = w_scales[:, a].rearrange("e q n -> q e n").bitcast(I32)
            for quadrant in range(4):
                row = 32 * quadrant + 4 * a
                nc.sync.dma_start(scale_dst[row : row + 4, :, :], scale_src[4 * quadrant : 4 * quadrant + 4, :, :])
        w_tiles = []
        for a in range(PASSES):
            w_tile = keep.tile([P, E * N], U32, name="w%d" % a, align_bytes=64)
            nc.sync.dma_start(
                w_tile[:].bitcast(I32).rearrange("p (e n) -> p e n", n=N),
                w_words[:, a].rearrange("e p n r -> p e (n r)").bitcast(I32),
            )
            w_tiles.append(w_tile)
        bias = keep.tile([P, E], F32, name="bias")
        nc.sync.dma_start(bias[:], b)
        pos_t = []
        for choice, pos in enumerate((pos1, pos2, pos3)):
            list_tile = keep.tile([P, T // PER_COLUMN], U16, name="pos%d" % choice)
            nc.sync.dma_start(list_tile[:], pos)
            pos_t.append(list_tile)

        gathered = {}

        def place_gathered(a, lo, hi, at):
            tile = placed("gathered%d_%d" % (a, lo), PACK * (hi - lo), F32, at)
            gathered[a, lo] = tile[:]

        def gather(a, on_vector, first, lo, hi, planes=range(PACK)):
            tile = gathered[a, first].rearrange("p (r c) -> p r c", r=PACK)
            for r in planes:
                values = tile[:, r, lo - first : hi - first]
                looked_up = windows[a, r][:].indirect(entries(offs_t, lo, hi))
                if on_vector:
                    nc.vector.tensor_copy(values, looked_up)
                else:
                    nc.scalar.activation(values, looked_up, COPY)

        def gather_on_scalar(a, lo, hi, at):
            place_gathered(a, lo, hi, at)
            gather(a, False, lo, lo, hi)

        rounded = {}

        def place_rounded(at, width, *runs):
            tile = placed("rounded%d_%d" % runs[0], PACK * width * len(runs), BF16, at)
            for index, run in enumerate(runs):
                rounded[run] = tile[:, PACK * width * index :]

        def rounded_view(a, lo, hi):
            base = max(first for a_run, first in rounded if a_run == a and first <= lo)
            return rounded[a, base][:, PACK * (lo - base) : PACK * (hi - base)]

        def product(engine, run, a, first, lo, hi, gates):
            engine.tensor_tensor(
                rounded_view(a, lo, hi).rearrange("p (c i r) -> p c r i", r=PACK, i=run),
                gathered[a, first].rearrange("p (r c i) -> p c r i", r=PACK, i=run)[:, (lo - first) // run : (hi - first) // run],
                gates.rearrange("p (c i) -> p c i", i=run).unsqueeze(2).broadcast_to([P, (hi - lo) // run, PACK, run]),
                MULT,
            )

        def multiply_on_gpsimd(a, first, lo, hi):
            product(nc.gpsimd, GPSIMD_RUN, a, first, lo, hi, gate_early[:, lo:hi])

        gate_banks = {}

        def multiply(a, first, lo, hi):
            base = lo // QUAD * QUAD
            product(nc.vector, VECTOR_RUN, a, first, lo, hi, gate_banks[base][:, lo - base : hi - base])

        def spread_gate():
            first_expert = OWN_END // C
            identity = placed("identity", P, F32, columns_at - 4 * P)
            make_identity(nc, identity[:])
            turned = psum.tile([P, P], F32, name="turned", offset=4 * BANK)
            nc.tensor.transpose(turned[:], gate_rows[:], identity[:])
            gate_columns = placed("gate_columns", E - first_expert, F32, columns_at)
            nc.vector.tensor_copy(gate_columns[:], turned[:, first_expert:E])
            for base in (Q5, Q2, Q3, Q4):
                index = (base - Q2) // QUAD
                gate_banks[base] = psum.tile([P, QUAD], F32, name="gate_bank%d" % index, offset=index * BANK)
                for e in range(max(base // C, first_expert), (base + QUAD) // C):
                    column = gate_columns[:, e - first_expert : e - first_expert + 1]
                    nc.tensor.transpose(gate_banks[base][:, e * C - base : (e + 1) * C - base], column.to_broadcast([P, P]), identity[:])

        banks = {}
        issued = {}

        def open_banks(groups):
            for first, end, index in groups:
                bank = psum.tile([P, (end - first) * C], F32, name="bank%d" % first, offset=index * BANK)
                issued[first] = 0
                for e in range(first, end):
                    banks[e] = (bank[:, (e - first) * C : (e - first + 1) * C], first, PASSES * (end - first))

        def contract(a, e, words, scale_bytes):
            acc, first, total = banks[e]
            issued[first] = issued[first] + 1
            nc.tensor.matmul_mx(
                acc,
                lhsT=w_tiles[a][:, e * N : (e + 1) * N].bitcast(FP8X4),
                lhsT_scale=w_scale[4 * a : P, e * N : (e + 1) * N],
                rhs=words.bitcast(FP8X4),
                rhs_scale=scale_bytes,
                start=issued[first] == 1,
                stop=issued[first] == total,
            )

        def quantise(words_at, scales_at, *runs):
            a, lo = runs[0][0:2]
            width = sum(end - first for a_run, first, end in runs)
            words = placed("words%d_%d" % (a, lo), width, U32, words_at)
            scale_bytes = placed("bytes%d_%d" % (a, lo), width, U8, scales_at)
            nc.vector.quantize_mx(words[:].bitcast(FP8X4), scale_bytes[:], rounded_view(a, lo, lo + width))
            column = 0
            for a_run, first, end in runs:
                for slot in range(first, end, C):
                    contract(a_run, slot // C, words[:, column : column + C], scale_bytes[:, column : column + C])
                    column = column + C

        place_gathered(0, 0, FIRST_END, area_a)
        gather(0, True, 0, 0, FIRST_END, range(PACK - 1))
        gather(0, True, 0, 0, OPENING, (PACK - 1,))
        gather(0, True, 0, OPENING, FIRST_END, (PACK - 1,))
        gather_on_scalar(0, FIRST_END, Q3, area_a + GATHERED * FIRST_END)
        place_gathered(1, 0, SECOND_END, area_b)
        gather(1, True, 0, 0, SECOND_END)
        gather_on_scalar(0, Q3, Q5, area_d)
        place_rounded(rounded_0, Q4, (0, Q0))
        multiply_on_gpsimd(0, 0, 0, OPENING)
        multiply_on_gpsimd(0, 0, OPENING, FIRST_END)
        multiply_on_gpsimd(0, FIRST_END, FIRST_END, Q3)
        place_gathered(2, 0, OWN_END, area_c)
        gather(2, True, 0, 0, OWN_END)
        gather_on_scalar(2, OWN_END, Q5, area_f)
        place_rounded(rounded_1, Q4, (1, Q0))
        multiply_on_gpsimd(1, 0, 0, SECOND_END)
        spread_gate()
        gather_on_scalar(1, SECOND_END, Q4, area_e)
        place_rounded(rounded_2, Q4, (2, Q0))
        place_rounded(rounded_3, QUAD, (0, Q4), (2, Q4))
        multiply(0, Q3, Q3, Q4)
        multiply(0, Q3, Q4, Q5)
        multiply_on_gpsimd(2, 0, 0, OWN_END)
        multiply(2, OWN_END, OWN_END, Q3)
        gather_on_scalar(1, Q4, Q6, area_d)
        multiply(2, OWN_END, Q3, Q4)
        multiply(2, OWN_END, Q4, Q5)
        multiply(1, SECOND_END, SECOND_END, Q3)
        multiply(1, SECOND_END, Q3, Q4)
        gate_late = placed("gate_late", QUAD + HELPED, F32, gate_at)
        nc.sync.dma_start(gate_late[:], gate[0:P, Q4 : Q5 + HELPED])
        gather_on_scalar(0, Q5, Q6, area_e)
        gather_on_scalar(2, Q5, Q6, area_e + GATHERED * QUAD)

        open_banks(EARLY_BANKS)
        for index, run in enumerate(((0, Q0, Q2), (0, Q2, Q4), (1, Q0, Q2))):
            quantise(area_f + index * CODES + GROUP, area_f + index * CODES, run)
        for index, run in enumerate(((1, Q2, Q4), (2, Q0, Q2), (2, Q2, Q4))):
            quantise(rounded_0 + index * CODES + GROUP, rounded_0 + index * CODES, run)
        quantise(area_c, rounded_1, (0, Q4, Q5), (2, Q4, Q5))
        y = placed("y", S, F32, 0)

        def finish(first, end, on_vector):
            for e in range(first, end):
                if on_vector:
                    nc.vector.tensor_scalar(y[:, e * C : (e + 1) * C], banks[e][0], bias[:, e : e + 1], 0.0, ADD, MAX)
                else:
                    nc.scalar.activation(y[:, e * C : (e + 1) * C], banks[e][0], RELU, bias=bias[:, e : e + 1])

        finish(0, Q4 // C, False)

        place_rounded(rounded_2, GROUP, (1, Q4))
        place_rounded(rounded_2 + ROUNDED * GROUP, QUAD, (0, Q5))
        product(nc.gpsimd, GPSIMD_RUN, 1, Q4, Q4, Q5, gate_late[:, 0:QUAD])
        multiply(1, Q4, Q5, Q6)
        multiply(0, Q5, Q5, Q6)

        open_banks(LATE_BANKS)
        quantise(area_d + GROUP, area_d, (1, Q4, Q6))
        quantise(area_d + CODES + QUAD, area_d + CODES, (0, Q5, Q6))
        finish(Q4 // C, Q5 // C, False)

        middle = Q5 + HALF
        place_rounded(rounded_2, HALF, (2, Q5))
        place_rounded(rounded_2 + ROUNDED * HALF, HALF, (2, middle))
        product(nc.gpsimd, GPSIMD_RUN, 2, Q5, Q5, Q5 + HELPED, gate_late[:, QUAD:])
        multiply(2, Q5, middle, Q6)
        multiply(2, Q5, Q5 + HELPED, middle)
        for index, (first, end, bank_index) in enumerate(LATE_BANKS):
            at = area_c + CODES + index * 5 * HALF
            quantise(at + HALF, at, (2, first * C, end * C))
        for first, end, bank_index in LATE_BANKS:
            finish(first, end, end == E)

        sums = placed("sums", 4 * T, F32, pass_at[1])

        def looked_up(choice, lo, hi):
            return y[:].indirect(entries(pos_t[choice], lo, hi))

        def part(row, lo, hi):
            return sums[:, row * T + lo : row * T + hi]

        def fetch_on_scalar(choice, lo, hi):
            nc.scalar.activation(part(choice, lo, hi), looked_up(choice, lo, hi), COPY)

        def fetch_and_add(target, choice, source, lo, hi):
            nc.vector.tensor_tensor(part(target, lo, hi), looked_up(choice, lo, hi), part(source, lo, hi), ADD)

        def add_last(other, lo, hi):
            nc.vector.tensor_tensor(part(3, lo, hi), part(2, lo, hi), part(other, lo, hi), ADD)

        fetch_on_scalar(0, 0, TWICE)
        fetch_on_scalar(0, TWICE, STORE_CUT)
        fetch_on_scalar(1, ALONE, STORE_CUT)
        fetch_on_scalar(0, STORE_CUT, T)
        fetch_on_scalar(1, STORE_CUT, T)
        nc.vector.tensor_copy(part(1, TWICE, ALONE), looked_up(2, TWICE, ALONE))
        fetch_and_add(1, 1, 0, 0, TWICE)
        fetch_and_add(2, 1, 1, TWICE, ALONE)
        fetch_and_add(3, 2, 1, 0, TWICE)
        add_last(0, TWICE, ALONE)
        nc.sync.dma_start(out[:, 0:ALONE], part(3, 0, ALONE))
        fetch_and_add(2, 2, 0, ALONE, STORE_CUT)
        fetch_and_add(2, 2, 0, STORE_CUT, T)
        for queue, lo, hi in ((nc.sync, ALONE, STORE_CUT), (nc.scalar, STORE_CUT, T)):
            add_last(1, lo, hi)
            queue.dma_start(out[:, lo:hi], part(3, lo, hi))
